import numpy as np
import ml_dtypes


def mxq(x, axis, fmt="e4m3"):
    dtype, down = {"e4m3": (ml_dtypes.float8_e4m3fn, 7), "e5m2": (ml_dtypes.float8_e5m2, 14)}[fmt]
    v = np.moveaxis(np.asarray(x, np.float32).astype(ml_dtypes.bfloat16).astype(np.float64), axis, -1)
    blocks = v.reshape(v.shape[:-1] + (-1, 32))
    amax = np.abs(blocks).max(-1, keepdims=True)
    byte = np.maximum(np.where(amax > 0, np.frexp(amax)[1] - 1 + 127, 0) - down, 1)
    scale = np.exp2(byte - 127.0)
    codes = (blocks / scale).astype(np.float32).astype(dtype).astype(np.float64)
    return np.moveaxis((codes * scale).reshape(v.shape), -1, axis)


WIDE = False


def mx_kscale(k):
    if not WIDE:
        return np.ones(k)
    levels = np.array([10, -10, 5, -5, 0])
    if k % 512:
        return np.exp2(np.random.permutation(np.resize(levels, k // 32))).repeat(32)
    a = np.empty((k // 512, 16))
    for p in range(k // 512):
        a[p, :8] = np.random.permutation(np.resize(levels, 8))
        for g in range(8):
            far = levels[np.abs(levels - a[p, g]) >= 10]
            a[p, g + 8] = far[np.random.randint(len(far))]
    return np.exp2(a.ravel()).repeat(32)


def f64(x):
    return np.asarray(x).astype(np.float64)


def striped(idx):
    return np.tile(idx.reshape(-1, 16).T, (8, 1)).astype(np.uint16)


def unstriped(offs):
    return offs[:16].T.reshape(-1).astype(np.int64)


E2M1 = np.array([0.0, 0.5, 1.0, 1.5, 2.0, 3.0, 4.0, 6.0, -0.0, -0.5, -1.0, -1.5, -2.0, -3.0, -4.0, -6.0])


def pack_weight(w, fmt):
    k, n = w.shape
    w = f64(np.asarray(w, np.float32).astype(ml_dtypes.bfloat16)).reshape(k // 32, 32, n)
    amax = np.abs(w).max(1)
    if fmt == "e4m3":
        byte = np.frexp(amax)[1] - 1 + 127 - 7
    else:
        mant, ex = np.frexp(amax / 6.0)
        byte = np.where(mant > 0.5, ex, ex - 1) + 127
    byte = np.clip(np.where(amax > 0, byte, 1), 1, 254)
    scaled = (w * np.exp2(127.0 - byte)[:, None, :]).reshape(k, n).astype(np.float32)
    by_word = np.ascontiguousarray(scaled.reshape(k // 512, 128, 4, n).transpose(0, 1, 3, 2))
    if fmt == "e4m3":
        words = by_word.astype(ml_dtypes.float8_e4m3fn).view(np.uint8)
    else:
        c = by_word.astype(ml_dtypes.float4_e2m1fn).view(np.uint8) & 0xF
        words = (c[..., 0::2] | (c[..., 1::2] << 4)).reshape(k // 512, 128, 2 * n)
    return np.ascontiguousarray(words), np.ascontiguousarray(byte.astype(np.uint8).reshape(k // 512, 16, n))


def unpack_weight(words, scales, fmt):
    g, _, n = scales.shape
    words = np.ascontiguousarray(words).reshape(g, 128, n, -1)
    if fmt == "e4m3":
        vals = words.view(ml_dtypes.float8_e4m3fn).astype(np.float64)
    else:
        nib = np.empty((g, 128, n, 4), np.uint8)
        nib[..., 0::2] = words & 0xF
        nib[..., 1::2] = words >> 4
        vals = E2M1[nib]
    vals = vals * np.repeat(np.exp2(scales.astype(np.float64) - 127.0), 8, axis=1)[..., None]
    return vals.transpose(0, 1, 3, 2).reshape(g * 512, n)


def silu(v):
    return v / (1.0 + np.exp(-np.maximum(v, -700.0)))


K, M, T, S = 1024, 1024, 2048, 1024


def setup_inputs():
    n = np.random.standard_normal
    s = mx_kscale(K)[:, None]
    u = mx_kscale(512)[:, None]
    v = pack_weight(n((K, T)) * s, "e4m3")
    p_w4 = pack_weight(n((K, M)) / np.sqrt(K) / s, "e2m1")
    return {
        "tab_words": v[0],
        "tab_scales": v[1],
        "w4_words": p_w4[0],
        "w4_scales": p_w4[1],
        "down": (n((K, 512)) / np.sqrt(K) / s * u.T).astype(np.float32),
        "up": (0.5 * n((512, M)) / np.sqrt(512) / u).astype(np.float32),
        "ts": np.tile(np.exp(0.5 * n(T)), (128, 1)).astype(np.float32),
        "b": (0.3 * n(1024)).astype(np.float32),
        "offs": striped(np.random.permutation(T)[:S]),
    }


def reference(tab_words, tab_scales, w4_words, w4_scales, down, up, ts, b, offs):
    tab_ = unpack_weight(tab_words, tab_scales, "e4m3")[:, unstriped(offs)]
    w4_ = unpack_weight(w4_words, w4_scales, "e2m1")
    down_ = mxq(f64(down), 0, "e4m3")
    up_ = mxq(f64(up), 0, "e4m3")
    h_ = mxq(down_.T @ tab_, 0, "e4m3")
    y = w4_.T @ tab_ + up_.T @ h_
    y = y * f64(ts)[0][unstriped(offs)]
    return silu(y + f64(b)[:, None])

@@ -1,0 +1,257 @@
+from contextlib import ExitStack
+
+import concourse.mybir as mybir
+from concourse.masks import make_identity
+
+K, M, T, S, R = 1024, 1024, 2048, 1024, 512
+FLOPS = 2 * K * R * S + 2 * K * M * S + 2 * R * M * S
+
+F32 = mybir.dt.float32
+BF16 = mybir.dt.bfloat16
+I32 = mybir.dt.int32
+U32 = mybir.dt.uint32
+U16 = mybir.dt.uint16
+U8 = mybir.dt.uint8
+FP8X4 = mybir.dt.float8_e4m3fn_x4
+FP4X4 = mybir.dt.float4_e2m1fn_x4
+MULT = mybir.AluOpType.mult
+ADD = mybir.AluOpType.add
+SILU = mybir.ActivationFunctionType.Silu
+
+P = 128
+HALF = 512
+Y_BANKS = 6
+
+
+def tile_list_tabts_silu_kernel(tc, tab_words, tab_scales, w4_words, w4_scales, down, up, ts, b, offs, out):
+    nc = tc.nc
+    with ExitStack() as ctx:
+        keep = ctx.enter_context(tc.tile_pool(name="keep", bufs=1))
+        ring = ctx.enter_context(tc.tile_pool(name="ring", bufs=4))
+        psum = ctx.enter_context(tc.psum_pool(name="psum", bufs=1))
+
+        offsets = keep.tile([P, S // 16], U16, name="offsets")
+        nc.sync.dma_start(offsets[:], offs)
+
+        tab_planes = keep.tile([P, 2, T // 4], I32, name="tab_planes", align_bytes=64)
+        w4_planes = keep.tile([P, 2, M // 4], I32, name="w4_planes", align_bytes=64)
+        warm = keep.tile([P, 16], F32, name="warm")
+        nc.gpsimd.memset(tab_planes[:, 0, :], 0)
+        nc.vector.memset(tab_planes[:, 1, :], 0)
+        nc.vector.memset(w4_planes[:], 0)
+        nc.vector.memset(warm[:, 0:8], 0.0)
+        nc.scalar.activation(warm[:, 8:9], warm[:, 0:1], SILU)
+
+        identity = keep.tile([P, P], F32, name="identity")
+        make_identity(nc, identity[:])
+        b_rows = keep.tile([P, P], F32, name="b_rows")
+        nc.gpsimd.memset(b_rows[:], 0.0)
+
+        ts_cols = keep.tile([P, T // P], F32, name="ts_cols")
+        nc.sync.dma_start(ts_cols[:], ts[0].rearrange("(n m) -> n m", n=P))
+        for q in range(4):
+            nc.sync.dma_start(tab_planes[32 * q : 32 * q + 4, :, :], tab_scales[:, 4 * q : 4 * q + 4, :].rearrange("a r n -> r a n").bitcast(I32))
+        words = [keep.tile([P, T], I32, name=f"words{a}", align_bytes=64) for a in range(2)]
+        nc.sync.dma_start(words[0][:], tab_words[0].rearrange("p t i -> p (t i)").bitcast(I32))
+        w4_codes = keep.tile([P, 2, 2 * M], U8, name="w4_codes", align_bytes=64)
+        nc.sync.dma_start(w4_codes[:].bitcast(I32), w4_words.rearrange("a p n -> p a n").bitcast(I32))
+        for q in range(4):
+            nc.sync.dma_start(w4_planes[32 * q : 32 * q + 4, :, :], w4_scales[:, 4 * q : 4 * q + 4, :].rearrange("a r n -> r a n").bitcast(I32))
+        nc.gpsimd.dma_start(b_rows[0 : M // P, :], b.rearrange("(c p) -> c p", p=P))
+        nc.sync.dma_start(words[1][:], tab_words[1].rearrange("p t i -> p (t i)").bitcast(I32))
+
+        down0 = keep.tile([P, 4, R], F32, name="down0")
+        nc.sync.dma_start(down0[:], down[0:512, :].rearrange("(p j) c -> p j c", j=4))
+        down1 = [keep.tile([P, 4, R // 2], F32, name=f"down1_{u}") for u in range(2)]
+        for u in range(2):
+            nc.sync.dma_start(down1[u][:], down[512:1024, 256 * u : 256 * u + 256].rearrange("(p j) c -> p j c", j=4))
+        up_raw = [keep.tile([P, 4, HALF], F32, name=f"up_raw{u}") for u in range(2)]
+        for u in range(2):
+            nc.sync.dma_start(up_raw[u][:], up[:, HALF * u : HALF * u + HALF].rearrange("(p j) c -> p j c", j=4))
+
+        def bank(kind, shape):
+            return psum.tile(shape, F32, name=kind, tag=kind, bufs=Y_BANKS if kind == "y" else 8 - Y_BANKS)
+
+        ts_all = keep.tile([P, T], F32, name="ts_all")
+        ts_view = ts_all[:].rearrange("p (n m) -> p n m", m=T // P)
+        for u in range(4):
+            spread = bank("y", [P, 4, P])
+            for m in range(4):
+                nc.tensor.transpose(spread[:, m, :], ts_cols[:, 4 * u + m : 4 * u + m + 1].to_broadcast([P, P]), identity[:])
+            nc.scalar.copy(ts_view[:, :, 4 * u : 4 * u + 4], spread[:].rearrange("p m n -> p n m"))
+        b_turned = bank("h", [P, 4, P])
+        nc.tensor.transpose(b_turned[:, 0, :], b_rows[:], identity[:])
+        b_cols = keep.tile([P, M // P], F32, name="b_cols")
+        nc.scalar.copy(b_cols[:], b_turned[:, 0, 0 : M // P])
+
+        def picks(jh):
+            return offsets[:, 32 * jh : 32 * jh + 32]
+
+        got_planes = keep.tile([P, 2, S], U8, name="got_planes", align_bytes=64)
+        got_words = [[keep.tile([P, HALF], U32, name=f"got_words{a}_{jh}", align_bytes=64) for jh in range(2)] for a in range(2)]
+        got_ts = [keep.tile([P, HALF], F32, name=f"got_ts{jh}") for jh in range(2)]
+
+        def gather_plane(a, jh):
+            nc.vector.tensor_copy(got_planes[:, a, HALF * jh : HALF * jh + HALF], tab_planes[:, a, :].bitcast(U8).indirect(picks(jh)))
+
+        def gather_words(a, jh):
+            nc.vector.tensor_copy(got_words[a][jh][:], words[a][:].bitcast(U32).indirect(picks(jh)))
+
+        def gather_ts(jh):
+            nc.vector.tensor_copy(got_ts[jh][:], ts_all[:].indirect(picks(jh)))
+
+        for a in range(2):
+            gather_plane(a, 0)
+            gather_words(a, 0)
+
+        def tab_operand(a, j0, j1):
+            codes = got_words[a][j0 // HALF][:, j0 % HALF : j0 % HALF + (j1 - j0)].bitcast(FP8X4)
+            return codes, got_planes[:, a, j0:j1]
+
+        y_banks = {}
+
+        def w4_pass(jh, n, a):
+            if a == 0:
+                y_banks[jh, n] = bank("y", [P, HALF])
+            codes, plane = tab_operand(a, HALF * jh, HALF * jh + HALF)
+            nc.tensor.matmul_mx(
+                out=y_banks[jh, n][:],
+                lhsT=w4_codes[:, a, 256 * n : 256 * n + 256].bitcast(FP4X4),
+                lhsT_scale=w4_planes[:, a, 32 * n : 32 * n + 32].bitcast(U8),
+                rhs=codes,
+                rhs_scale=plane,
+                start=(a == 0),
+                stop=False,
+            )
+
+        for a in range(2):
+            for n in range(Y_BANKS):
+                w4_pass(0, n, a)
+
+        down0_bf = keep.tile([P, 4, P, 4], BF16, name="down0_bf", align_bytes=64)
+        down1_bf = [keep.tile([P, 4, 64, 4], BF16, name=f"down1_bf{u}", align_bytes=64) for u in range(2)]
+        down_codes = keep.tile([P, 2, R], U32, name="down_codes", align_bytes=64)
+        down_planes = keep.tile([P, 2, R], U8, name="down_planes", align_bytes=64)
+
+        def pool_copy(dst, src):
+            nc.gpsimd.tensor_scalar(dst, src, 1.0, 0.0, MULT, ADD)
+
+        def quantize_down(a, c0, c1, src):
+            nc.vector.quantize_mx(out=down_codes[:, a, c0:c1].bitcast(FP8X4), scales=down_planes[:, a, c0:c1], in_=src)
+
+        down0_view = down0[:].rearrange("p j (m t) -> p m t j", t=4)
+        nc.scalar.copy(down0_bf[:, 0:2, :, :].rearrange("p t m j -> p m t j"), down0_view[:, :, 0:2, :])
+        for m0 in (0, 64):
+            pool_copy(down0_bf[:, 2:4, m0 : m0 + 64, :].rearrange("p t m j -> p m t j"), down0_view[:, m0 : m0 + 64, 2:4, :])
+        nc.scalar.copy(down1_bf[0][:].rearrange("p t m j -> p m t j"), down1[0][:].rearrange("p j (m t) -> p m t j", t=4))
+        for u in range(2):
+            quantize_down(0, 256 * u, 256 * u + 256, down0_bf[:, 2 * u : 2 * u + 2, :, :].rearrange("p t m j -> p (t m j)"))
+        nc.vector.tensor_copy(down1_bf[1][:].rearrange("p t m j -> p m t j"), down1[1][:].rearrange("p j (m t) -> p m t j", t=4))
+        for u in range(2):
+            for t in range(4):
+                quantize_down(1, P * t + 64 * u, P * t + 64 * u + 64, down1_bf[u][:, t, :, :].rearrange("p m j -> p (m j)"))
+
+        for a in range(2):
+            gather_plane(a, 1)
+            gather_words(a, 1)
+        gather_ts(0)
+
+        h_bf = keep.tile([P, S, 4], BF16, name="h_bf", align_bytes=64)
+        h_codes = keep.tile([P, S], U32, name="h_codes", align_bytes=64)
+        h_plane = keep.tile([P, S], U8, name="h_plane", align_bytes=64)
+
+        def h_block(jb):
+            acc = bank("h", [P, 4, P])
+            for t in range(4):
+                for a in range(2):
+                    codes, plane = tab_operand(a, P * jb, P * jb + P)
+                    nc.tensor.matmul_mx(
+                        out=acc[:, t, :],
+                        lhsT=down_codes[:, a, P * t : P * t + P].bitcast(FP8X4),
+                        lhsT_scale=down_planes[:, a, P * t : P * t + P],
+                        rhs=codes,
+                        rhs_scale=plane,
+                        start=(a == 0),
+                        stop=(a == 1),
+                    )
+            nc.scalar.copy(h_bf[:, P * jb : P * jb + P, :], acc[:].rearrange("p t n -> p n t"))
+
+        def quantize_h(j0, j1):
+            nc.vector.quantize_mx(
+                out=h_codes[:, j0:j1].bitcast(FP8X4),
+                scales=h_plane[:, j0:j1],
+                in_=h_bf[:, j0:j1, :].rearrange("p n t -> p (n t)"),
+            )
+
+        up_bf = keep.tile([P, M, 4], BF16, name="up_bf", align_bytes=64)
+        up_codes = keep.tile([P, M], U32, name="up_codes", align_bytes=64)
+        up_plane = keep.tile([P, M], U8, name="up_plane", align_bytes=64)
+
+        def cast_up(u):
+            for c0 in range(256 * u, 256 * u + 256, P):
+                raw = up_raw[c0 // HALF][:, :, c0 % HALF : c0 % HALF + P]
+                pool_copy(up_bf[:, c0 : c0 + P, :], raw.rearrange("p j c -> p c j"))
+
+        def quantize_up(u):
+            cols = slice(256 * u, 256 * u + 256)
+            nc.vector.quantize_mx(
+                out=up_codes[:, cols].bitcast(FP8X4),
+                scales=up_plane[:, cols],
+                in_=up_bf[:, cols, :].rearrange("p n j -> p (n j)"),
+            )
+
+        def finish(jh, n):
+            acc = y_banks[jh, n]
+            js = slice(HALF * jh, HALF * jh + HALF)
+            ns = slice(P * n, P * n + P)
+            nc.tensor.matmul_mx(
+                out=acc[:],
+                lhsT=up_codes[:, ns].bitcast(FP8X4),
+                lhsT_scale=up_plane[:, ns],
+                rhs=h_codes[:, js].bitcast(FP8X4),
+                rhs_scale=h_plane[:, js],
+                start=False,
+                stop=True,
+            )
+            scaled = ring.tile([P, HALF], F32, name="scaled")
+            result = ring.tile([P, HALF], F32, name="result", bufs=6)
+            step = HALF // 2 if (jh, n) == (1, M // P - 1) else HALF
+            for c0 in range(0, HALF, step):
+                cs = slice(c0, c0 + step)
+                nc.vector.tensor_tensor(scaled[:, cs], acc[:, cs], got_ts[jh][:, cs], MULT)
+                nc.scalar.activation(result[:, cs], scaled[:, cs], SILU, bias=b_cols[:, n : n + 1])
+                nc.sync.dma_start(out[ns, HALF * jh + c0 : HALF * jh + c0 + step], result[:, cs])
+
+        h_block(0)
+        h_block(1)
+        cast_up(0)
+        h_block(2)
+        quantize_h(0, 256)
+        cast_up(1)
+        quantize_up(0)
+        h_block(3)
+        h_block(4)
+        quantize_h(256, 512)
+        quantize_up(1)
+        h_block(5)
+        finish(0, 0)
+        cast_up(2)
+        finish(0, 1)
+        h_block(6)
+        quantize_up(2)
+        finish(0, 2)
+        cast_up(3)
+        finish(0, 3)
+        h_block(7)
+        quantize_up(3)
+        finish(0, 4)
+        quantize_h(512, 1024)
+        gather_ts(1)
+        finish(0, 5)
+        for jh in range(2):
+            for n in range(M // P):
+                if jh == 0 and n < Y_BANKS:
+                    continue
+                w4_pass(jh, n, 0)
+                w4_pass(jh, n, 1)
+                finish(jh, n)

@@ -15,7 +15,6 @@ U8 = mybir.dt.uint8
 FP8X4 = mybir.dt.float8_e4m3fn_x4
 FP4X4 = mybir.dt.float4_e2m1fn_x4
 MULT = mybir.AluOpType.mult
-ADD = mybir.AluOpType.add
 SILU = mybir.ActivationFunctionType.Silu
 
 P = 128
@@ -33,13 +32,14 @@ def tile_list_tabts_silu_kernel(tc, tab_words, tab_scales, w4_words, w4_scales, 
         offsets = keep.tile([P, S // 16], U16, name="offsets")
         nc.sync.dma_start(offsets[:], offs)
 
-        tab_planes = keep.tile([P, 2, T // 4], I32, name="tab_planes", align_bytes=64)
+        tab_planes = keep.tile([P, T // 4], I32, name="tab_planes", align_bytes=64)
         w4_planes = keep.tile([P, 2, M // 4], I32, name="w4_planes", align_bytes=64)
+        got_plane1 = keep.tile([P, S // 4], I32, name="got_plane1", align_bytes=64)
         warm = keep.tile([P, 16], F32, name="warm")
-        nc.gpsimd.memset(tab_planes[:, 0, :], 0)
-        nc.vector.memset(tab_planes[:, 1, :], 0)
+        nc.gpsimd.memset(tab_planes[:], 0)
         nc.vector.memset(w4_planes[:], 0)
         nc.vector.memset(warm[:, 0:8], 0.0)
+        nc.vector.memset(got_plane1[96:128, :], 0)
         nc.scalar.activation(warm[:, 8:9], warm[:, 0:1], SILU)
 
         identity = keep.tile([P, P], F32, name="identity")
@@ -49,19 +49,19 @@ def tile_list_tabts_silu_kernel(tc, tab_words, tab_scales, w4_words, w4_scales, 
 
         ts_cols = keep.tile([P, T // P], F32, name="ts_cols")
         nc.sync.dma_start(ts_cols[:], ts[0].rearrange("(n m) -> n m", n=P))
-        for q in range(4):
-            nc.sync.dma_start(tab_planes[32 * q : 32 * q + 4, :, :], tab_scales[:, 4 * q : 4 * q + 4, :].rearrange("a r n -> r a n").bitcast(I32))
+        for r in range(4):
+            nc.sync.dma_start(tab_planes[r:P:16, :], tab_scales[:, r:16:4, :].rearrange("a q t -> q a t").bitcast(I32))
         words = [keep.tile([P, T], I32, name=f"words{a}", align_bytes=64) for a in range(2)]
         nc.sync.dma_start(words[0][:], tab_words[0].rearrange("p t i -> p (t i)").bitcast(I32))
-        w4_codes = keep.tile([P, 2, 2 * M], U8, name="w4_codes", align_bytes=64)
-        nc.sync.dma_start(w4_codes[:].bitcast(I32), w4_words.rearrange("a p n -> p a n").bitcast(I32))
-        for q in range(4):
-            nc.sync.dma_start(w4_planes[32 * q : 32 * q + 4, :, :], w4_scales[:, 4 * q : 4 * q + 4, :].rearrange("a r n -> r a n").bitcast(I32))
-        nc.gpsimd.dma_start(b_rows[0 : M // P, :], b.rearrange("(c p) -> c p", p=P))
-        nc.sync.dma_start(words[1][:], tab_words[1].rearrange("p t i -> p (t i)").bitcast(I32))
-
         down0 = keep.tile([P, 4, R], F32, name="down0")
         nc.sync.dma_start(down0[:], down[0:512, :].rearrange("(p j) c -> p j c", j=4))
+        nc.sync.dma_start(b_rows[0 : M // P, :], b.rearrange("(c p) -> c p", p=P))
+        w4_codes = keep.tile([P, 2, 2 * M], U8, name="w4_codes", align_bytes=64)
+        for q in range(4):
+            nc.sync.dma_start(w4_planes[32 * q : 32 * q + 4, :, :], w4_scales[:, 4 * q : 4 * q + 4, :].rearrange("a r n -> r a n").bitcast(I32))
+        nc.sync.dma_start(w4_codes[:].bitcast(I32), w4_words.rearrange("a p n -> p a n").bitcast(I32))
+        nc.sync.dma_start(words[1][:], tab_words[1].rearrange("p t i -> p (t i)").bitcast(I32))
+
         down1 = [keep.tile([P, 4, R // 2], F32, name=f"down1_{u}") for u in range(2)]
         for u in range(2):
             nc.sync.dma_start(down1[u][:], down[512:1024, 256 * u : 256 * u + 256].rearrange("(p j) c -> p j c", j=4))
@@ -87,12 +87,11 @@ def tile_list_tabts_silu_kernel(tc, tab_words, tab_scales, w4_words, w4_scales, 
         def picks(jh):
             return offsets[:, 32 * jh : 32 * jh + 32]
 
-        got_planes = keep.tile([P, 2, S], U8, name="got_planes", align_bytes=64)
+        got_planes = keep.tile([P, S], U8, name="got_planes", align_bytes=64)
         got_words = [[keep.tile([P, HALF], U32, name=f"got_words{a}_{jh}", align_bytes=64) for jh in range(2)] for a in range(2)]
         got_ts = [keep.tile([P, HALF], F32, name=f"got_ts{jh}") for jh in range(2)]
-
-        def gather_plane(a, jh):
-            nc.vector.tensor_copy(got_planes[:, a, HALF * jh : HALF * jh + HALF], tab_planes[:, a, :].bitcast(U8).indirect(picks(jh)))
+        nc.vector.tensor_copy(got_planes[:], tab_planes[:].bitcast(U8).indirect(offsets[:]))
+        nc.scalar.dma_start(got_plane1[0:112, :], got_planes[16:128, :].bitcast(I32))
 
         def gather_words(a, jh):
             nc.vector.tensor_copy(got_words[a][jh][:], words[a][:].bitcast(U32).indirect(picks(jh)))
@@ -100,13 +99,13 @@ def tile_list_tabts_silu_kernel(tc, tab_words, tab_scales, w4_words, w4_scales, 
         def gather_ts(jh):
             nc.vector.tensor_copy(got_ts[jh][:], ts_all[:].indirect(picks(jh)))
 
-        for a in range(2):
-            gather_plane(a, 0)
-            gather_words(a, 0)
+        gather_words(0, 0)
+        gather_words(1, 0)
 
         def tab_operand(a, j0, j1):
             codes = got_words[a][j0 // HALF][:, j0 % HALF : j0 % HALF + (j1 - j0)].bitcast(FP8X4)
-            return codes, got_planes[:, a, j0:j1]
+            plane = got_planes[:, j0:j1] if a == 0 else got_plane1[:, j0 // 4 : j1 // 4].bitcast(U8)
+            return codes, plane
 
         y_banks = {}
 
@@ -133,28 +132,22 @@ def tile_list_tabts_silu_kernel(tc, tab_words, tab_scales, w4_words, w4_scales, 
         down_codes = keep.tile([P, 2, R], U32, name="down_codes", align_bytes=64)
         down_planes = keep.tile([P, 2, R], U8, name="down_planes", align_bytes=64)
 
-        def pool_copy(dst, src):
-            nc.gpsimd.tensor_scalar(dst, src, 1.0, 0.0, MULT, ADD)
-
         def quantize_down(a, c0, c1, src):
             nc.vector.quantize_mx(out=down_codes[:, a, c0:c1].bitcast(FP8X4), scales=down_planes[:, a, c0:c1], in_=src)
 
         down0_view = down0[:].rearrange("p j (m t) -> p m t j", t=4)
-        nc.scalar.copy(down0_bf[:, 0:2, :, :].rearrange("p t m j -> p m t j"), down0_view[:, :, 0:2, :])
-        for m0 in (0, 64):
-            pool_copy(down0_bf[:, 2:4, m0 : m0 + 64, :].rearrange("p t m j -> p m t j"), down0_view[:, m0 : m0 + 64, 2:4, :])
+        nc.scalar.copy(down0_bf[:].rearrange("p t m j -> p m t j"), down0_view)
         nc.scalar.copy(down1_bf[0][:].rearrange("p t m j -> p m t j"), down1[0][:].rearrange("p j (m t) -> p m t j", t=4))
-        for u in range(2):
-            quantize_down(0, 256 * u, 256 * u + 256, down0_bf[:, 2 * u : 2 * u + 2, :, :].rearrange("p t m j -> p (t m j)"))
+        quantize_down(0, 0, R, down0_bf[:].rearrange("p t m j -> p (t m j)"))
         nc.vector.tensor_copy(down1_bf[1][:].rearrange("p t m j -> p m t j"), down1[1][:].rearrange("p j (m t) -> p m t j", t=4))
         for u in range(2):
             for t in range(4):
                 quantize_down(1, P * t + 64 * u, P * t + 64 * u + 64, down1_bf[u][:, t, :, :].rearrange("p m j -> p (m j)"))
 
-        for a in range(2):
-            gather_plane(a, 1)
-            gather_words(a, 1)
+        gather_words(0, 1)
+        gather_words(1, 1)
         gather_ts(0)
+        gather_ts(1)
 
         h_bf = keep.tile([P, S, 4], BF16, name="h_bf", align_bytes=64)
         h_codes = keep.tile([P, S], U32, name="h_codes", align_bytes=64)
@@ -188,9 +181,12 @@ def tile_list_tabts_silu_kernel(tc, tab_words, tab_scales, w4_words, w4_scales, 
         up_plane = keep.tile([P, M], U8, name="up_plane", align_bytes=64)
 
         def cast_up(u):
-            for c0 in range(256 * u, 256 * u + 256, P):
-                raw = up_raw[c0 // HALF][:, :, c0 % HALF : c0 % HALF + P]
-                pool_copy(up_bf[:, c0 : c0 + P, :], raw.rearrange("p j c -> p c j"))
+            raw = up_raw[u // 2][:, :, 256 * (u % 2) : 256 * (u % 2) + 256]
+            copy = nc.scalar.copy if u == 3 else nc.vector.tensor_copy
+            copy(
+                up_bf[:, 256 * u : 256 * u + 256, :].rearrange("p (c i) j -> p c j i", i=4),
+                raw.rearrange("p j (c i) -> p c j i", i=4),
+            )
 
         def quantize_up(u):
             cols = slice(256 * u, 256 * u + 256)
@@ -246,7 +242,6 @@ def tile_list_tabts_silu_kernel(tc, tab_words, tab_scales, w4_words, w4_scales, 
         quantize_up(3)
         finish(0, 4)
         quantize_h(512, 1024)
-        gather_ts(1)
         finish(0, 5)
         for jh in range(2):
             for n in range(M // P):

@@ -15,6 +15,7 @@ U8 = mybir.dt.uint8
 FP8X4 = mybir.dt.float8_e4m3fn_x4
 FP4X4 = mybir.dt.float4_e2m1fn_x4
 MULT = mybir.AluOpType.mult
+ADD = mybir.AluOpType.add
 SILU = mybir.ActivationFunctionType.Silu
 
 P = 128
@@ -26,13 +27,13 @@ def tile_list_tabts_silu_kernel(tc, tab_words, tab_scales, w4_words, w4_scales, 
     nc = tc.nc
     with ExitStack() as ctx:
         keep = ctx.enter_context(tc.tile_pool(name="keep", bufs=1))
-        ring = ctx.enter_context(tc.tile_pool(name="ring", bufs=4))
+        ring = ctx.enter_context(tc.tile_pool(name="ring", bufs=16))
         psum = ctx.enter_context(tc.psum_pool(name="psum", bufs=1))
 
         offsets = keep.tile([P, S // 16], U16, name="offsets")
         nc.sync.dma_start(offsets[:], offs)
 
-        tab_planes = keep.tile([P, T // 4], I32, name="tab_planes", align_bytes=64)
+        tab_planes = keep.tile([P, T // 4], I32, name="tab_planes", tag="slot_b", align_bytes=64)
         w4_planes = keep.tile([P, 2, M // 4], I32, name="w4_planes", align_bytes=64)
         got_plane1 = keep.tile([P, S // 4], I32, name="got_plane1", align_bytes=64)
         warm = keep.tile([P, 16], F32, name="warm")
@@ -51,62 +52,56 @@ def tile_list_tabts_silu_kernel(tc, tab_words, tab_scales, w4_words, w4_scales, 
         nc.sync.dma_start(ts_cols[:], ts[0].rearrange("(n m) -> n m", n=P))
         for r in range(4):
             nc.sync.dma_start(tab_planes[r:P:16, :], tab_scales[:, r:16:4, :].rearrange("a q t -> q a t").bitcast(I32))
-        words = [keep.tile([P, T], I32, name=f"words{a}", align_bytes=64) for a in range(2)]
+        words = [keep.tile([P, T], I32, name=f"words{a}", tag=f"slot_words{a}", align_bytes=64) for a in range(2)]
         nc.sync.dma_start(words[0][:], tab_words[0].rearrange("p t i -> p (t i)").bitcast(I32))
-        down0 = keep.tile([P, 4, R], F32, name="down0")
+        down0 = keep.tile([P, 4, R], F32, name="down0", tag="slot_d")
         nc.sync.dma_start(down0[:], down[0:512, :].rearrange("(p j) c -> p j c", j=4))
         nc.sync.dma_start(b_rows[0 : M // P, :], b.rearrange("(c p) -> c p", p=P))
         w4_codes = keep.tile([P, 2, 2 * M], U8, name="w4_codes", align_bytes=64)
         for q in range(4):
             nc.sync.dma_start(w4_planes[32 * q : 32 * q + 4, :, :], w4_scales[:, 4 * q : 4 * q + 4, :].rearrange("a r n -> r a n").bitcast(I32))
-        nc.sync.dma_start(w4_codes[:].bitcast(I32), w4_words.rearrange("a p n -> p a n").bitcast(I32))
+        nc.sync.dma_start(w4_codes[:, 0, :].bitcast(I32), w4_words[0].bitcast(I32))
         nc.sync.dma_start(words[1][:], tab_words[1].rearrange("p t i -> p (t i)").bitcast(I32))
+        nc.sync.dma_start(w4_codes[:, 1, :].bitcast(I32), w4_words[1].bitcast(I32))
 
-        down1 = [keep.tile([P, 4, R // 2], F32, name=f"down1_{u}") for u in range(2)]
-        for u in range(2):
-            nc.sync.dma_start(down1[u][:], down[512:1024, 256 * u : 256 * u + 256].rearrange("(p j) c -> p j c", j=4))
-        up_raw = [keep.tile([P, 4, HALF], F32, name=f"up_raw{u}") for u in range(2)]
-        for u in range(2):
-            nc.sync.dma_start(up_raw[u][:], up[:, HALF * u : HALF * u + HALF].rearrange("(p j) c -> p j c", j=4))
 
         def bank(kind, shape):
             return psum.tile(shape, F32, name=kind, tag=kind, bufs=Y_BANKS if kind == "y" else 8 - Y_BANKS)
 
-        ts_all = keep.tile([P, T], F32, name="ts_all")
+        ts_all = keep.tile([P, T], F32, name="ts_all", tag="slot_e", align_bytes=64)
         ts_view = ts_all[:].rearrange("p (n m) -> p n m", m=T // P)
+        ts_wide = keep.tile([P, T // P, P], F32, name="ts_wide", tag="slot_a", align_bytes=64)
+        for u in range(2):
+            nc.vector.tensor_copy(ts_wide[:, 8 * u : 8 * u + 8, :], ts_cols[:, 8 * u : 8 * u + 8].unsqueeze(2).to_broadcast([P, 8, P]))
         for u in range(4):
             spread = bank("y", [P, 4, P])
             for m in range(4):
-                nc.tensor.transpose(spread[:, m, :], ts_cols[:, 4 * u + m : 4 * u + m + 1].to_broadcast([P, P]), identity[:])
+                nc.tensor.transpose(spread[:, m, :], ts_wide[:, 4 * u + m, :], identity[:])
             nc.scalar.copy(ts_view[:, :, 4 * u : 4 * u + 4], spread[:].rearrange("p m n -> p n m"))
-        b_turned = bank("h", [P, 4, P])
-        nc.tensor.transpose(b_turned[:, 0, :], b_rows[:], identity[:])
-        b_cols = keep.tile([P, M // P], F32, name="b_cols")
-        nc.scalar.copy(b_cols[:], b_turned[:, 0, 0 : M // P])
-
-        def picks(jh):
-            return offsets[:, 32 * jh : 32 * jh + 32]
 
         got_planes = keep.tile([P, S], U8, name="got_planes", align_bytes=64)
-        got_words = [[keep.tile([P, HALF], U32, name=f"got_words{a}_{jh}", align_bytes=64) for jh in range(2)] for a in range(2)]
-        got_ts = [keep.tile([P, HALF], F32, name=f"got_ts{jh}") for jh in range(2)]
         nc.vector.tensor_copy(got_planes[:], tab_planes[:].bitcast(U8).indirect(offsets[:]))
-        nc.scalar.dma_start(got_plane1[0:112, :], got_planes[16:128, :].bitcast(I32))
+        nc.sync.dma_start(got_plane1[0:112, :], got_planes[16:128, :].bitcast(I32))
+        down1_lo = keep.tile([P, 4, R // 2], F32, name="down1_lo", tag="slot_b", align_bytes=64)
+        nc.sync.dma_start(down1_lo[:], down[512:1024, 0:256].rearrange("(p j) c -> p j c", j=4))
+        got_words = [keep.tile([P, S], U32, name="got_words0", align_bytes=64)]
+        got_ts = keep.tile([P, S], F32, name="got_ts")
 
-        def gather_words(a, jh):
-            nc.vector.tensor_copy(got_words[a][jh][:], words[a][:].bitcast(U32).indirect(picks(jh)))
+        def gather_words(a, j0, j1):
+            nc.vector.tensor_copy(got_words[a][:, j0:j1], words[a][:].bitcast(U32).indirect(offsets[:, j0 // 16 : j1 // 16]))
 
-        def gather_ts(jh):
-            nc.vector.tensor_copy(got_ts[jh][:], ts_all[:].indirect(picks(jh)))
-
-        gather_words(0, 0)
-        gather_words(1, 0)
+        gather_words(0, 0, S)
+        down1_hi = keep.tile([P, 4, R // 2], F32, name="down1_hi", tag="slot_words0", align_bytes=64)
+        nc.sync.dma_start(down1_hi[:], down[512:1024, 256:512].rearrange("(p j) c -> p j c", j=4))
+        down1 = [down1_lo, down1_hi]
+        nc.vector.tensor_copy(got_ts[:], ts_all[:].indirect(offsets[:]))
+        got_words.append(keep.tile([P, S], U32, name="got_words1", tag="slot_e", align_bytes=64))
 
         def tab_operand(a, j0, j1):
-            codes = got_words[a][j0 // HALF][:, j0 % HALF : j0 % HALF + (j1 - j0)].bitcast(FP8X4)
             plane = got_planes[:, j0:j1] if a == 0 else got_plane1[:, j0 // 4 : j1 // 4].bitcast(U8)
-            return codes, plane
+            return got_words[a][:, j0:j1].bitcast(FP8X4), plane
 
+        order = [(jh, n0 + n) for n0 in (0, 4) for jh in range(2) for n in range(4)]
         y_banks = {}
 
         def w4_pass(jh, n, a):
@@ -123,33 +118,41 @@ def tile_list_tabts_silu_kernel(tc, tab_words, tab_scales, w4_words, w4_scales, 
                 stop=False,
             )
 
-        for a in range(2):
-            for n in range(Y_BANKS):
-                w4_pass(0, n, a)
+        for jh, n in order[:Y_BANKS]:
+            w4_pass(jh, n, 0)
 
-        down0_bf = keep.tile([P, 4, P, 4], BF16, name="down0_bf", align_bytes=64)
-        down1_bf = [keep.tile([P, 4, 64, 4], BF16, name=f"down1_bf{u}", align_bytes=64) for u in range(2)]
+        down_bf = [keep.tile([P, 4, P, 4], BF16, name=f"down_bf{a}", tag=("slot_a", "down_bf1")[a], align_bytes=64) for a in range(2)]
         down_codes = keep.tile([P, 2, R], U32, name="down_codes", align_bytes=64)
         down_planes = keep.tile([P, 2, R], U8, name="down_planes", align_bytes=64)
 
-        def quantize_down(a, c0, c1, src):
-            nc.vector.quantize_mx(out=down_codes[:, a, c0:c1].bitcast(FP8X4), scales=down_planes[:, a, c0:c1], in_=src)
+        def cast_down(copy, a, raw, m0):
+            m1 = m0 + raw.shape[2] // 4
+            copy(down_bf[a][:, :, m0:m1, :].rearrange("p t m j -> p m t j"), raw.rearrange("p j (m t) -> p m t j", t=4))
 
-        down0_view = down0[:].rearrange("p j (m t) -> p m t j", t=4)
-        nc.scalar.copy(down0_bf[:].rearrange("p t m j -> p m t j"), down0_view)
-        nc.scalar.copy(down1_bf[0][:].rearrange("p t m j -> p m t j"), down1[0][:].rearrange("p j (m t) -> p m t j", t=4))
-        quantize_down(0, 0, R, down0_bf[:].rearrange("p t m j -> p (t m j)"))
-        nc.vector.tensor_copy(down1_bf[1][:].rearrange("p t m j -> p m t j"), down1[1][:].rearrange("p j (m t) -> p m t j", t=4))
-        for u in range(2):
-            for t in range(4):
-                quantize_down(1, P * t + 64 * u, P * t + 64 * u + 64, down1_bf[u][:, t, :, :].rearrange("p m j -> p (m j)"))
+        def quantize_down(a):
+            nc.vector.quantize_mx(out=down_codes[:, a, :].bitcast(FP8X4), scales=down_planes[:, a, :], in_=down_bf[a][:].rearrange("p t m j -> p (t m j)"))
 
-        gather_words(0, 1)
-        gather_words(1, 1)
-        gather_ts(0)
-        gather_ts(1)
+        cast_down(nc.scalar.copy, 0, down0[:], 0)
+        up_lo = keep.tile([P, 4, HALF], F32, name="up_lo", tag="slot_d")
+        nc.sync.dma_start(up_lo[:], up[:, 0:HALF].rearrange("(p j) c -> p j c", j=4))
+        b_turned = bank("h", [P, 4, P])
+        nc.tensor.transpose(b_turned[:, 0, :], b_rows[:], identity[:])
+        b_cols = keep.tile([P, M // P], F32, name="b_cols")
+        nc.scalar.copy(b_cols[:], b_turned[:, 0, 0 : M // P])
+        gather_words(1, 0, HALF)
+        quantize_down(0)
+        up_hi = keep.tile([P, 4, HALF], F32, name="up_hi", tag="slot_a", align_bytes=64)
+        nc.sync.dma_start(up_hi[:], up[:, HALF:M].rearrange("(p j) c -> p j c", j=4))
+        up_raw = [up_lo, up_hi]
+        gather_words(1, HALF, S)
+        for jh, n in order[:Y_BANKS]:
+            w4_pass(jh, n, 1)
+        cast_down(nc.scalar.copy, 1, down1[0][:], 0)
+        cast_down(nc.scalar.copy, 1, down1[1][:, :, 0:128], 64)
+        cast_down(nc.vector.tensor_copy, 1, down1[1][:, :, 128:256], 96)
+        quantize_down(1)
 
-        h_bf = keep.tile([P, S, 4], BF16, name="h_bf", align_bytes=64)
+        h_bf = keep.tile([P, S, 4], BF16, name="h_bf", tag="slot_h", align_bytes=64)
         h_codes = keep.tile([P, S], U32, name="h_codes", align_bytes=64)
         h_plane = keep.tile([P, S], U8, name="h_plane", align_bytes=64)
 
@@ -177,21 +180,14 @@ def tile_list_tabts_silu_kernel(tc, tab_words, tab_scales, w4_words, w4_scales, 
             )
 
         up_bf = keep.tile([P, M, 4], BF16, name="up_bf", align_bytes=64)
-        up_codes = keep.tile([P, M], U32, name="up_codes", align_bytes=64)
+        up_codes = {}
         up_plane = keep.tile([P, M], U8, name="up_plane", align_bytes=64)
 
-        def cast_up(u):
-            raw = up_raw[u // 2][:, :, 256 * (u % 2) : 256 * (u % 2) + 256]
-            copy = nc.scalar.copy if u == 3 else nc.vector.tensor_copy
-            copy(
-                up_bf[:, 256 * u : 256 * u + 256, :].rearrange("p (c i) j -> p c j i", i=4),
-                raw.rearrange("p j (c i) -> p c j i", i=4),
-            )
-
         def quantize_up(u):
-            cols = slice(256 * u, 256 * u + 256)
+            cols = slice(HALF * u, HALF * u + HALF)
+            up_codes[u] = keep.tile([P, HALF], U32, name=f"up_codes{u}", tag=("up_codes0", "slot_h")[u], align_bytes=64)
             nc.vector.quantize_mx(
-                out=up_codes[:, cols].bitcast(FP8X4),
+                out=up_codes[u][:].bitcast(FP8X4),
                 scales=up_plane[:, cols],
                 in_=up_bf[:, cols, :].rearrange("p n j -> p (n j)"),
             )
@@ -202,7 +198,7 @@ def tile_list_tabts_silu_kernel(tc, tab_words, tab_scales, w4_words, w4_scales, 
             ns = slice(P * n, P * n + P)
             nc.tensor.matmul_mx(
                 out=acc[:],
-                lhsT=up_codes[:, ns].bitcast(FP8X4),
+                lhsT=up_codes[n // 4][:, P * (n % 4) : P * (n % 4) + P].bitcast(FP8X4),
                 lhsT_scale=up_plane[:, ns],
                 rhs=h_codes[:, js].bitcast(FP8X4),
                 rhs_scale=h_plane[:, js],
@@ -210,43 +206,40 @@ def tile_list_tabts_silu_kernel(tc, tab_words, tab_scales, w4_words, w4_scales, 
                 stop=True,
             )
             scaled = ring.tile([P, HALF], F32, name="scaled")
-            result = ring.tile([P, HALF], F32, name="result", bufs=6)
+            result = ring.tile([P, HALF], F32, name="result")
             step = HALF // 2 if (jh, n) == (1, M // P - 1) else HALF
             for c0 in range(0, HALF, step):
                 cs = slice(c0, c0 + step)
-                nc.vector.tensor_tensor(scaled[:, cs], acc[:, cs], got_ts[jh][:, cs], MULT)
+                nc.vector.tensor_tensor(scaled[:, cs], acc[:, cs], got_ts[:, HALF * jh + c0 : HALF * jh + c0 + step], MULT)
                 nc.scalar.activation(result[:, cs], scaled[:, cs], SILU, bias=b_cols[:, n : n + 1])
                 nc.sync.dma_start(out[ns, HALF * jh + c0 : HALF * jh + c0 + step], result[:, cs])
 
         h_block(0)
         h_block(1)
-        cast_up(0)
+        nc.vector.tensor_copy(
+            up_bf[:, 0:HALF, :].rearrange("p (c i) j -> p c j i", i=4),
+            up_raw[0][:].rearrange("p j (c i) -> p c j i", i=4),
+        )
         h_block(2)
         quantize_h(0, 256)
-        cast_up(1)
         quantize_up(0)
         h_block(3)
-        h_block(4)
         quantize_h(256, 512)
-        quantize_up(1)
+        for c0 in range(0, HALF, P):
+            nc.gpsimd.tensor_scalar(up_bf[:, HALF + c0 : HALF + c0 + P, :], up_raw[1][:, :, c0 : c0 + P].rearrange("p j c -> p c j"), 1.0, 0.0, MULT, ADD)
+        h_block(4)
+        finish(*order[0])
         h_block(5)
-        finish(0, 0)
-        cast_up(2)
-        finish(0, 1)
+        finish(*order[1])
         h_block(6)
-        quantize_up(2)
-        finish(0, 2)
-        cast_up(3)
-        finish(0, 3)
+        finish(*order[2])
         h_block(7)
-        quantize_up(3)
-        finish(0, 4)
+        finish(*order[3])
         quantize_h(512, 1024)
-        finish(0, 5)
-        for jh in range(2):
-            for n in range(M // P):
-                if jh == 0 and n < Y_BANKS:
-                    continue
-                w4_pass(jh, n, 0)
-                w4_pass(jh, n, 1)
-                finish(jh, n)
+        for i in range(4, len(order)):
+            if i + 2 < len(order):
+                w4_pass(*order[i + 2], 0)
+                w4_pass(*order[i + 2], 1)
+            if i == 6:
+                quantize_up(1)
+            finish(*order[i])

@@ -19,28 +19,38 @@ ADD = mybir.AluOpType.add
 SILU = mybir.ActivationFunctionType.Silu
 
 P = 128
-HALF = 512
+PACK = 4
+K_PASS = P * PACK
+BANK = 512
+UP_HALF = M // 2
+DOWN_HALF = R // 2
+PLANE_SHIFT = 16
 Y_BANKS = 6
+H_BANKS = 8 - Y_BANKS
+TILES = (M // P) * (S // BANK)
 
 
 def tile_list_tabts_silu_kernel(tc, tab_words, tab_scales, w4_words, w4_scales, down, up, ts, b, offs, out):
     nc = tc.nc
     with ExitStack() as ctx:
         keep = ctx.enter_context(tc.tile_pool(name="keep", bufs=1))
-        ring = ctx.enter_context(tc.tile_pool(name="ring", bufs=16))
+        epilogue = ctx.enter_context(tc.tile_pool(name="epilogue", bufs=TILES))
         psum = ctx.enter_context(tc.psum_pool(name="psum", bufs=1))
+
+        def bank(kind, shape):
+            return psum.tile(shape, F32, name=kind, tag=kind, bufs=Y_BANKS if kind == "y" else H_BANKS)
 
         offsets = keep.tile([P, S // 16], U16, name="offsets")
         nc.sync.dma_start(offsets[:], offs)
 
-        tab_planes = keep.tile([P, T // 4], I32, name="tab_planes", tag="slot_b", align_bytes=64)
+        tab_planes = keep.tile([P, T // 4], I32, name="tab_planes", tag="planes_then_down", align_bytes=64)
         w4_planes = keep.tile([P, 2, M // 4], I32, name="w4_planes", align_bytes=64)
         got_plane1 = keep.tile([P, S // 4], I32, name="got_plane1", align_bytes=64)
         warm = keep.tile([P, 16], F32, name="warm")
         nc.gpsimd.memset(tab_planes[:], 0)
         nc.vector.memset(w4_planes[:], 0)
         nc.vector.memset(warm[:, 0:8], 0.0)
-        nc.vector.memset(got_plane1[96:128, :], 0)
+        nc.vector.memset(got_plane1[96:P, :], 0)
         nc.scalar.activation(warm[:, 8:9], warm[:, 0:1], SILU)
 
         identity = keep.tile([P, P], F32, name="identity")
@@ -48,14 +58,14 @@ def tile_list_tabts_silu_kernel(tc, tab_words, tab_scales, w4_words, w4_scales, 
         b_rows = keep.tile([P, P], F32, name="b_rows")
         nc.gpsimd.memset(b_rows[:], 0.0)
 
-        ts_cols = keep.tile([P, T // P], F32, name="ts_cols")
-        nc.sync.dma_start(ts_cols[:], ts[0].rearrange("(n m) -> n m", n=P))
+        ts_cols = keep.tile([P, T // P], F32, name="ts_cols", tag="ts_then_down_then_up", align_bytes=64)
+        nc.sync.dma_start(ts_cols[:], ts[0].rearrange("(c m) -> c m", c=P))
         for r in range(4):
-            nc.sync.dma_start(tab_planes[r:P:16, :], tab_scales[:, r:16:4, :].rearrange("a q t -> q a t").bitcast(I32))
-        words = [keep.tile([P, T], I32, name=f"words{a}", tag=f"slot_words{a}", align_bytes=64) for a in range(2)]
+            nc.sync.dma_start(tab_planes[r:P:PLANE_SHIFT, :], tab_scales[:, r:16:4, :].rearrange("a q t -> q a t").bitcast(I32))
+        words = [keep.tile([P, T], I32, name=f"words{a}", tag=("words_then_down", "words1")[a], align_bytes=64) for a in range(2)]
         nc.sync.dma_start(words[0][:], tab_words[0].rearrange("p t i -> p (t i)").bitcast(I32))
-        down0 = keep.tile([P, 4, R], F32, name="down0", tag="slot_d")
-        nc.sync.dma_start(down0[:], down[0:512, :].rearrange("(p j) c -> p j c", j=4))
+        down0 = keep.tile([P, PACK, R], F32, name="down0", tag="down_then_up")
+        nc.sync.dma_start(down0[:], down[0:K_PASS, :].rearrange("(p i) r -> p i r", i=PACK))
         nc.sync.dma_start(b_rows[0 : M // P, :], b.rearrange("(c p) -> c p", p=P))
         w4_codes = keep.tile([P, 2, 2 * M], U8, name="w4_codes", align_bytes=64)
         for q in range(4):
@@ -64,54 +74,47 @@ def tile_list_tabts_silu_kernel(tc, tab_words, tab_scales, w4_words, w4_scales, 
         nc.sync.dma_start(words[1][:], tab_words[1].rearrange("p t i -> p (t i)").bitcast(I32))
         nc.sync.dma_start(w4_codes[:, 1, :].bitcast(I32), w4_words[1].bitcast(I32))
 
-
-        def bank(kind, shape):
-            return psum.tile(shape, F32, name=kind, tag=kind, bufs=Y_BANKS if kind == "y" else 8 - Y_BANKS)
-
-        ts_all = keep.tile([P, T], F32, name="ts_all", tag="slot_e", align_bytes=64)
-        ts_view = ts_all[:].rearrange("p (n m) -> p n m", m=T // P)
-        ts_wide = keep.tile([P, T // P, P], F32, name="ts_wide", tag="slot_a", align_bytes=64)
-        for u in range(2):
-            nc.vector.tensor_copy(ts_wide[:, 8 * u : 8 * u + 8, :], ts_cols[:, 8 * u : 8 * u + 8].unsqueeze(2).to_broadcast([P, 8, P]))
-        for u in range(4):
+        ts_all = keep.tile([P, T], F32, name="ts_all", tag="ts_then_words", align_bytes=64)
+        ts_view = ts_all[:].rearrange("p (c m) -> p c m", m=T // P)
+        for m0 in range(0, T // P, 4):
             spread = bank("y", [P, 4, P])
             for m in range(4):
-                nc.tensor.transpose(spread[:, m, :], ts_wide[:, 4 * u + m, :], identity[:])
-            nc.scalar.copy(ts_view[:, :, 4 * u : 4 * u + 4], spread[:].rearrange("p m n -> p n m"))
+                nc.tensor.transpose(spread[:, m, :], ts_cols[:, m0 + m : m0 + m + 1].to_broadcast([P, P]), identity[:])
+            nc.scalar.copy(ts_view[:, :, m0 : m0 + 4], spread[:].rearrange("p m c -> p c m"))
 
         got_planes = keep.tile([P, S], U8, name="got_planes", align_bytes=64)
         nc.vector.tensor_copy(got_planes[:], tab_planes[:].bitcast(U8).indirect(offsets[:]))
-        nc.sync.dma_start(got_plane1[0:112, :], got_planes[16:128, :].bitcast(I32))
-        down1_lo = keep.tile([P, 4, R // 2], F32, name="down1_lo", tag="slot_b", align_bytes=64)
-        nc.sync.dma_start(down1_lo[:], down[512:1024, 0:256].rearrange("(p j) c -> p j c", j=4))
-        got_words = [keep.tile([P, S], U32, name="got_words0", align_bytes=64)]
+        nc.sync.dma_start(got_plane1[0 : P - PLANE_SHIFT, :], got_planes[PLANE_SHIFT:P, :].bitcast(I32))
+        down1_lo = keep.tile([P, PACK, DOWN_HALF], F32, name="down1_lo", tag="planes_then_down", align_bytes=64)
+        nc.sync.dma_start(down1_lo[:], down[K_PASS:K, 0:DOWN_HALF].rearrange("(p i) r -> p i r", i=PACK))
+        got_words0 = keep.tile([P, S], U32, name="got_words0", align_bytes=64)
         got_ts = keep.tile([P, S], F32, name="got_ts")
 
-        def gather_words(a, j0, j1):
-            nc.vector.tensor_copy(got_words[a][:, j0:j1], words[a][:].bitcast(U32).indirect(offsets[:, j0 // 16 : j1 // 16]))
+        def gather_words(dst, a, j0, j1):
+            nc.vector.tensor_copy(dst[:, j0:j1], words[a][:].bitcast(U32).indirect(offsets[:, j0 // 16 : j1 // 16]))
 
-        gather_words(0, 0, S)
-        down1_hi = keep.tile([P, 4, R // 2], F32, name="down1_hi", tag="slot_words0", align_bytes=64)
-        nc.sync.dma_start(down1_hi[:], down[512:1024, 256:512].rearrange("(p j) c -> p j c", j=4))
-        down1 = [down1_lo, down1_hi]
+        gather_words(got_words0, 0, 0, S)
+        down1_hi = keep.tile([P, PACK, DOWN_HALF], F32, name="down1_hi", tag="words_then_down", align_bytes=64)
+        nc.sync.dma_start(down1_hi[:], down[K_PASS:K, DOWN_HALF:R].rearrange("(p i) r -> p i r", i=PACK))
         nc.vector.tensor_copy(got_ts[:], ts_all[:].indirect(offsets[:]))
-        got_words.append(keep.tile([P, S], U32, name="got_words1", tag="slot_e", align_bytes=64))
+        got_words1 = keep.tile([P, S], U32, name="got_words1", tag="ts_then_words", align_bytes=64)
 
         def tab_operand(a, j0, j1):
-            plane = got_planes[:, j0:j1] if a == 0 else got_plane1[:, j0 // 4 : j1 // 4].bitcast(U8)
-            return got_words[a][:, j0:j1].bitcast(FP8X4), plane
+            if a == 0:
+                return got_words0[:, j0:j1].bitcast(FP8X4), got_planes[:, j0:j1]
+            return got_words1[:, j0:j1].bitcast(FP8X4), got_plane1[:, j0 // 4 : j1 // 4].bitcast(U8)
 
-        order = [(jh, n0 + n) for n0 in (0, 4) for jh in range(2) for n in range(4)]
+        order = [(jh, n0 + n) for n0 in (0, UP_HALF // P) for jh in range(S // BANK) for n in range(UP_HALF // P)]
         y_banks = {}
 
         def w4_pass(jh, n, a):
             if a == 0:
-                y_banks[jh, n] = bank("y", [P, HALF])
-            codes, plane = tab_operand(a, HALF * jh, HALF * jh + HALF)
+                y_banks[jh, n] = bank("y", [P, BANK])
+            codes, plane = tab_operand(a, BANK * jh, BANK * jh + BANK)
             nc.tensor.matmul_mx(
                 out=y_banks[jh, n][:],
-                lhsT=w4_codes[:, a, 256 * n : 256 * n + 256].bitcast(FP4X4),
-                lhsT_scale=w4_planes[:, a, 32 * n : 32 * n + 32].bitcast(U8),
+                lhsT=w4_codes[:, a, 2 * P * n : 2 * P * (n + 1)].bitcast(FP4X4),
+                lhsT_scale=w4_planes[:, a, P // 4 * n : P // 4 * (n + 1)].bitcast(U8),
                 rhs=codes,
                 rhs_scale=plane,
                 start=(a == 0),
@@ -121,44 +124,51 @@ def tile_list_tabts_silu_kernel(tc, tab_words, tab_scales, w4_words, w4_scales, 
         for jh, n in order[:Y_BANKS]:
             w4_pass(jh, n, 0)
 
-        down_bf = [keep.tile([P, 4, P, 4], BF16, name=f"down_bf{a}", tag=("slot_a", "down_bf1")[a], align_bytes=64) for a in range(2)]
+        down_bf = [
+            keep.tile([P, PACK, P, PACK], BF16, name=f"down_bf{a}", tag=("ts_then_down_then_up", "down_bf1")[a], align_bytes=64)
+            for a in range(2)
+        ]
         down_codes = keep.tile([P, 2, R], U32, name="down_codes", align_bytes=64)
         down_planes = keep.tile([P, 2, R], U8, name="down_planes", align_bytes=64)
 
-        def cast_down(copy, a, raw, m0):
-            m1 = m0 + raw.shape[2] // 4
-            copy(down_bf[a][:, :, m0:m1, :].rearrange("p t m j -> p m t j"), raw.rearrange("p j (m t) -> p m t j", t=4))
+        def cast_down(copy, a, raw, r0):
+            m0, m1 = r0 // PACK, (r0 + raw.shape[2]) // PACK
+            copy(down_bf[a][:, :, m0:m1, :].rearrange("p t m i -> p m t i"), raw.rearrange("p i (m t) -> p m t i", t=PACK))
 
-        def quantize_down(a):
-            nc.vector.quantize_mx(out=down_codes[:, a, :].bitcast(FP8X4), scales=down_planes[:, a, :], in_=down_bf[a][:].rearrange("p t m j -> p (t m j)"))
+        def quantize_down(a, t0, t1):
+            cols = slice(P * t0, P * t1)
+            nc.vector.quantize_mx(
+                out=down_codes[:, a, cols].bitcast(FP8X4),
+                scales=down_planes[:, a, cols],
+                in_=down_bf[a][:, t0:t1, :, :].rearrange("p t m i -> p (t m i)"),
+            )
 
         cast_down(nc.scalar.copy, 0, down0[:], 0)
-        up_lo = keep.tile([P, 4, HALF], F32, name="up_lo", tag="slot_d")
-        nc.sync.dma_start(up_lo[:], up[:, 0:HALF].rearrange("(p j) c -> p j c", j=4))
-        b_turned = bank("h", [P, 4, P])
+        up_lo = keep.tile([P, PACK, UP_HALF], F32, name="up_lo", tag="down_then_up")
+        nc.sync.dma_start(up_lo[:], up[:, 0:UP_HALF].rearrange("(p i) n -> p i n", i=PACK))
+        b_turned = bank("h", [P, PACK, P])
         nc.tensor.transpose(b_turned[:, 0, :], b_rows[:], identity[:])
         b_cols = keep.tile([P, M // P], F32, name="b_cols")
         nc.scalar.copy(b_cols[:], b_turned[:, 0, 0 : M // P])
-        gather_words(1, 0, HALF)
-        quantize_down(0)
-        up_hi = keep.tile([P, 4, HALF], F32, name="up_hi", tag="slot_a", align_bytes=64)
-        nc.sync.dma_start(up_hi[:], up[:, HALF:M].rearrange("(p j) c -> p j c", j=4))
-        up_raw = [up_lo, up_hi]
-        gather_words(1, HALF, S)
+        gather_words(got_words1, 1, 0, BANK)
+        quantize_down(0, 0, PACK)
+        up_hi = keep.tile([P, PACK, UP_HALF], F32, name="up_hi", tag="ts_then_down_then_up", align_bytes=64)
+        nc.sync.dma_start(up_hi[:], up[:, UP_HALF:M].rearrange("(p i) n -> p i n", i=PACK))
+        gather_words(got_words1, 1, BANK, S)
         for jh, n in order[:Y_BANKS]:
             w4_pass(jh, n, 1)
-        cast_down(nc.scalar.copy, 1, down1[0][:], 0)
-        cast_down(nc.scalar.copy, 1, down1[1][:, :, 0:128], 64)
-        cast_down(nc.vector.tensor_copy, 1, down1[1][:, :, 128:256], 96)
-        quantize_down(1)
+        cast_down(nc.scalar.copy, 1, down1_lo[:], 0)
+        cast_down(nc.vector.tensor_copy, 1, down1_hi[:], DOWN_HALF)
+        quantize_down(1, 0, PACK // 2)
+        quantize_down(1, PACK // 2, PACK)
 
-        h_bf = keep.tile([P, S, 4], BF16, name="h_bf", tag="slot_h", align_bytes=64)
+        h_bf = keep.tile([P, S, PACK], BF16, name="h_bf", tag="h_then_up", align_bytes=64)
         h_codes = keep.tile([P, S], U32, name="h_codes", align_bytes=64)
         h_plane = keep.tile([P, S], U8, name="h_plane", align_bytes=64)
 
         def h_block(jb):
-            acc = bank("h", [P, 4, P])
-            for t in range(4):
+            acc = bank("h", [P, PACK, P])
+            for t in range(PACK):
                 for a in range(2):
                     codes, plane = tab_operand(a, P * jb, P * jb + P)
                     nc.tensor.matmul_mx(
@@ -170,76 +180,77 @@ def tile_list_tabts_silu_kernel(tc, tab_words, tab_scales, w4_words, w4_scales, 
                         start=(a == 0),
                         stop=(a == 1),
                     )
-            nc.scalar.copy(h_bf[:, P * jb : P * jb + P, :], acc[:].rearrange("p t n -> p n t"))
+            nc.scalar.copy(h_bf[:, P * jb : P * jb + P, :], acc[:].rearrange("p t j -> p j t"))
 
         def quantize_h(j0, j1):
             nc.vector.quantize_mx(
                 out=h_codes[:, j0:j1].bitcast(FP8X4),
                 scales=h_plane[:, j0:j1],
-                in_=h_bf[:, j0:j1, :].rearrange("p n t -> p (n t)"),
+                in_=h_bf[:, j0:j1, :].rearrange("p j t -> p (j t)"),
             )
 
-        up_bf = keep.tile([P, M, 4], BF16, name="up_bf", align_bytes=64)
-        up_codes = {}
+        up_bf = keep.tile([P, M, PACK], BF16, name="up_bf", align_bytes=64)
+        up_codes = []
         up_plane = keep.tile([P, M], U8, name="up_plane", align_bytes=64)
 
         def quantize_up(u):
-            cols = slice(HALF * u, HALF * u + HALF)
-            up_codes[u] = keep.tile([P, HALF], U32, name=f"up_codes{u}", tag=("up_codes0", "slot_h")[u], align_bytes=64)
+            cols = slice(UP_HALF * u, UP_HALF * u + UP_HALF)
+            up_codes.append(keep.tile([P, UP_HALF], U32, name=f"up_codes{u}", tag=("up_codes0", "h_then_up")[u], align_bytes=64))
             nc.vector.quantize_mx(
                 out=up_codes[u][:].bitcast(FP8X4),
                 scales=up_plane[:, cols],
-                in_=up_bf[:, cols, :].rearrange("p n j -> p (n j)"),
+                in_=up_bf[:, cols, :].rearrange("p n i -> p (n i)"),
             )
 
         def finish(jh, n):
             acc = y_banks[jh, n]
-            js = slice(HALF * jh, HALF * jh + HALF)
+            js = slice(BANK * jh, BANK * jh + BANK)
             ns = slice(P * n, P * n + P)
+            u, c = divmod(P * n, UP_HALF)
             nc.tensor.matmul_mx(
                 out=acc[:],
-                lhsT=up_codes[n // 4][:, P * (n % 4) : P * (n % 4) + P].bitcast(FP8X4),
+                lhsT=up_codes[u][:, c : c + P].bitcast(FP8X4),
                 lhsT_scale=up_plane[:, ns],
                 rhs=h_codes[:, js].bitcast(FP8X4),
                 rhs_scale=h_plane[:, js],
                 start=False,
                 stop=True,
             )
-            scaled = ring.tile([P, HALF], F32, name="scaled")
-            result = ring.tile([P, HALF], F32, name="result")
-            step = HALF // 2 if (jh, n) == (1, M // P - 1) else HALF
-            for c0 in range(0, HALF, step):
+            scaled = epilogue.tile([P, BANK], F32, name="scaled")
+            result = epilogue.tile([P, BANK], F32, name="result")
+            step = BANK // 2 if (jh, n) == order[-1] else BANK
+            for c0 in range(0, BANK, step):
                 cs = slice(c0, c0 + step)
-                nc.vector.tensor_tensor(scaled[:, cs], acc[:, cs], got_ts[:, HALF * jh + c0 : HALF * jh + c0 + step], MULT)
+                out_cols = slice(BANK * jh + c0, BANK * jh + c0 + step)
+                nc.vector.tensor_tensor(scaled[:, cs], acc[:, cs], got_ts[:, out_cols], MULT)
                 nc.scalar.activation(result[:, cs], scaled[:, cs], SILU, bias=b_cols[:, n : n + 1])
-                nc.sync.dma_start(out[ns, HALF * jh + c0 : HALF * jh + c0 + step], result[:, cs])
+                nc.sync.dma_start(out[ns, out_cols], result[:, cs])
 
         h_block(0)
         h_block(1)
         nc.vector.tensor_copy(
-            up_bf[:, 0:HALF, :].rearrange("p (c i) j -> p c j i", i=4),
-            up_raw[0][:].rearrange("p j (c i) -> p c j i", i=4),
+            up_bf[:, 0:UP_HALF, :].rearrange("p (c e) i -> p c i e", e=4),
+            up_lo[:].rearrange("p i (c e) -> p c i e", e=4),
         )
         h_block(2)
-        quantize_h(0, 256)
+        quantize_h(0, BANK // 2)
         quantize_up(0)
         h_block(3)
-        quantize_h(256, 512)
-        for c0 in range(0, HALF, P):
-            nc.gpsimd.tensor_scalar(up_bf[:, HALF + c0 : HALF + c0 + P, :], up_raw[1][:, :, c0 : c0 + P].rearrange("p j c -> p c j"), 1.0, 0.0, MULT, ADD)
-        h_block(4)
-        finish(*order[0])
-        h_block(5)
-        finish(*order[1])
-        h_block(6)
-        finish(*order[2])
-        h_block(7)
-        finish(*order[3])
-        quantize_h(512, 1024)
-        for i in range(4, len(order)):
-            if i + 2 < len(order):
-                w4_pass(*order[i + 2], 0)
-                w4_pass(*order[i + 2], 1)
-            if i == 6:
+        quantize_h(BANK // 2, BANK)
+        for c0 in range(0, UP_HALF, P):
+            nc.gpsimd.tensor_scalar(
+                up_bf[:, UP_HALF + c0 : UP_HALF + c0 + P, :], up_hi[:, :, c0 : c0 + P].rearrange("p i n -> p n i"), 1.0, 0.0, MULT, ADD
+            )
+        first_tiles = UP_HALF // P
+        for i in range(first_tiles):
+            h_block(BANK // P + i)
+            finish(*order[i])
+        quantize_h(BANK, S)
+        ahead = Y_BANKS - first_tiles
+        for i in range(first_tiles, TILES):
+            if i + ahead < TILES:
+                w4_pass(*order[i + ahead], 0)
+                w4_pass(*order[i + ahead], 1)
+            if i + ahead == TILES // 2:
                 quantize_up(1)
             finish(*order[i])

@@ -23,10 +23,10 @@ PACK = 4
 K_PASS = P * PACK
 BANK = 512
 UP_HALF = M // 2
-DOWN_HALF = R // 2
 PLANE_SHIFT = 16
-Y_BANKS = 6
-H_BANKS = 8 - Y_BANKS
+AHEAD = 3
+WARM_PASSES = 3
+UP1_AFTER = 3
 TILES = (M // P) * (S // BANK)
 
 
@@ -34,175 +34,189 @@ def tile_list_tabts_silu_kernel(tc, tab_words, tab_scales, w4_words, w4_scales, 
     nc = tc.nc
     with ExitStack() as ctx:
         keep = ctx.enter_context(tc.tile_pool(name="keep", bufs=1))
-        epilogue = ctx.enter_context(tc.tile_pool(name="epilogue", bufs=TILES))
-        psum = ctx.enter_context(tc.psum_pool(name="psum", bufs=1))
+        psum = ctx.enter_context(tc.psum_pool(name="psum", bufs=8))
 
-        def bank(kind, shape):
-            return psum.tile(shape, F32, name=kind, tag=kind, bufs=Y_BANKS if kind == "y" else H_BANKS)
+        def bank(shape):
+            return psum.tile(shape, F32, name="bank", tag="bank")
 
         offsets = keep.tile([P, S // 16], U16, name="offsets")
+        ts_cols = keep.tile([P, T // P], F32, name="ts_cols", tag="chain", align_bytes=64)
+        nc.sync.dma_start(ts_cols[:], ts[0].rearrange("(c m) -> c m", c=P))
         nc.sync.dma_start(offsets[:], offs)
 
-        tab_planes = keep.tile([P, T // 4], I32, name="tab_planes", tag="planes_then_down", align_bytes=64)
+        tab_planes = keep.tile([P, T // 4], I32, name="tab_planes", tag="planes_then_ts", align_bytes=64)
         w4_planes = keep.tile([P, 2, M // 4], I32, name="w4_planes", align_bytes=64)
         got_plane1 = keep.tile([P, S // 4], I32, name="got_plane1", align_bytes=64)
         warm = keep.tile([P, 16], F32, name="warm")
+        b_rows = keep.tile([P, P], F32, name="b_rows", tag="b_then_down_then_words", align_bytes=64)
         nc.gpsimd.memset(tab_planes[:], 0)
-        nc.vector.memset(w4_planes[:], 0)
+        nc.vector.memset(b_rows[:], 0.0)
         nc.vector.memset(warm[:, 0:8], 0.0)
+        nc.vector.memset(w4_planes[:], 0)
         nc.vector.memset(got_plane1[96:P, :], 0)
         nc.scalar.activation(warm[:, 8:9], warm[:, 0:1], SILU)
 
         identity = keep.tile([P, P], F32, name="identity")
         make_identity(nc, identity[:])
-        b_rows = keep.tile([P, P], F32, name="b_rows")
-        nc.gpsimd.memset(b_rows[:], 0.0)
 
-        ts_cols = keep.tile([P, T // P], F32, name="ts_cols", tag="ts_then_down_then_up", align_bytes=64)
-        nc.sync.dma_start(ts_cols[:], ts[0].rearrange("(c m) -> c m", c=P))
         for r in range(4):
             nc.sync.dma_start(tab_planes[r:P:PLANE_SHIFT, :], tab_scales[:, r:16:4, :].rearrange("a q t -> q a t").bitcast(I32))
-        words = [keep.tile([P, T], I32, name=f"words{a}", tag=("words_then_down", "words1")[a], align_bytes=64) for a in range(2)]
-        nc.sync.dma_start(words[0][:], tab_words[0].rearrange("p t i -> p (t i)").bitcast(I32))
-        down0 = keep.tile([P, PACK, R], F32, name="down0", tag="down_then_up")
-        nc.sync.dma_start(down0[:], down[0:K_PASS, :].rearrange("(p i) r -> p i r", i=PACK))
         nc.sync.dma_start(b_rows[0 : M // P, :], b.rearrange("(c p) -> c p", p=P))
+        words = [keep.tile([P, T], I32, name=f"words{a}", tag=f"words{a}", align_bytes=64) for a in range(2)]
+        down_raw = [keep.tile([P, PACK, R], F32, name=f"down_raw{a}") for a in range(2)]
+        nc.sync.dma_start(words[0][:], tab_words[0].rearrange("p t i -> p (t i)").bitcast(I32))
+        for a in range(2):
+            nc.sync.dma_start(down_raw[a][:], down[K_PASS * a : K_PASS * (a + 1), :].rearrange("(p i) r -> p i r", i=PACK))
+        nc.sync.dma_start(words[1][:], tab_words[1].rearrange("p t i -> p (t i)").bitcast(I32))
+        up_raw = [keep.tile([P, PACK, UP_HALF], F32, name=f"up_raw{u}", tag=f"up_raw{u}", align_bytes=64) for u in range(2)]
+
+        def load_up(u):
+            nc.sync.dma_start(up_raw[u][:], up[:, UP_HALF * u : UP_HALF * (u + 1)].rearrange("(p i) n -> p i n", i=PACK))
+
+        load_up(0)
         w4_codes = keep.tile([P, 2, 2 * M], U8, name="w4_codes", align_bytes=64)
         for q in range(4):
             nc.sync.dma_start(w4_planes[32 * q : 32 * q + 4, :, :], w4_scales[:, 4 * q : 4 * q + 4, :].rearrange("a r n -> r a n").bitcast(I32))
-        nc.sync.dma_start(w4_codes[:, 0, :].bitcast(I32), w4_words[0].bitcast(I32))
-        nc.sync.dma_start(words[1][:], tab_words[1].rearrange("p t i -> p (t i)").bitcast(I32))
-        nc.sync.dma_start(w4_codes[:, 1, :].bitcast(I32), w4_words[1].bitcast(I32))
+        nc.sync.dma_start(w4_codes[:].bitcast(I32), w4_words.rearrange("a p n -> p a n").bitcast(I32))
+        load_up(1)
 
-        ts_all = keep.tile([P, T], F32, name="ts_all", tag="ts_then_words", align_bytes=64)
+        ts_all = keep.tile([P, T], F32, name="ts_all", tag="ts_all", align_bytes=64)
         ts_view = ts_all[:].rearrange("p (c m) -> p c m", m=T // P)
         for m0 in range(0, T // P, 4):
-            spread = bank("y", [P, 4, P])
+            spread = bank([P, 4, P])
             for m in range(4):
                 nc.tensor.transpose(spread[:, m, :], ts_cols[:, m0 + m : m0 + m + 1].to_broadcast([P, P]), identity[:])
             nc.scalar.copy(ts_view[:, :, m0 : m0 + 4], spread[:].rearrange("p m c -> p c m"))
+        b_turned = bank([P, PACK, P])
+        nc.tensor.transpose(b_turned[:, 0, :], b_rows[:], identity[:])
+        b_cols = keep.tile([P, M // P], F32, name="b_cols")
+        nc.scalar.copy(b_cols[:], b_turned[:, 0, 0 : M // P])
 
         got_planes = keep.tile([P, S], U8, name="got_planes", align_bytes=64)
         nc.vector.tensor_copy(got_planes[:], tab_planes[:].bitcast(U8).indirect(offsets[:]))
-        nc.sync.dma_start(got_plane1[0 : P - PLANE_SHIFT, :], got_planes[PLANE_SHIFT:P, :].bitcast(I32))
-        down1_lo = keep.tile([P, PACK, DOWN_HALF], F32, name="down1_lo", tag="planes_then_down", align_bytes=64)
-        nc.sync.dma_start(down1_lo[:], down[K_PASS:K, 0:DOWN_HALF].rearrange("(p i) r -> p i r", i=PACK))
-        got_words0 = keep.tile([P, S], U32, name="got_words0", align_bytes=64)
-        got_ts = keep.tile([P, S], F32, name="got_ts")
+        nc.gpsimd.dma_start(got_plane1[0 : P - PLANE_SHIFT, :], got_planes[PLANE_SHIFT:P, :].bitcast(I32))
+        got_ts = []
 
-        def gather_words(dst, a, j0, j1):
-            nc.vector.tensor_copy(dst[:, j0:j1], words[a][:].bitcast(U32).indirect(offsets[:, j0 // 16 : j1 // 16]))
+        def gather_ts(jh, tag):
+            got_ts.append(keep.tile([P, BANK], F32, name=f"got_ts{jh}", tag=tag, align_bytes=64))
+            nc.vector.tensor_copy(got_ts[jh][:], ts_all[:].indirect(offsets[:, BANK // 16 * jh : BANK // 16 * (jh + 1)]))
 
-        gather_words(got_words0, 0, 0, S)
-        down1_hi = keep.tile([P, PACK, DOWN_HALF], F32, name="down1_hi", tag="words_then_down", align_bytes=64)
-        nc.sync.dma_start(down1_hi[:], down[K_PASS:K, DOWN_HALF:R].rearrange("(p i) r -> p i r", i=PACK))
-        nc.vector.tensor_copy(got_ts[:], ts_all[:].indirect(offsets[:]))
-        got_words1 = keep.tile([P, S], U32, name="got_words1", tag="ts_then_words", align_bytes=64)
+        got_words = []
+
+        def gather_words(a, j0, j1):
+            nc.vector.tensor_copy(got_words[a][:, j0:j1], words[a][:].bitcast(U32).indirect(offsets[:, j0 // 16 : j1 // 16]))
 
         def tab_operand(a, j0, j1):
             if a == 0:
-                return got_words0[:, j0:j1].bitcast(FP8X4), got_planes[:, j0:j1]
-            return got_words1[:, j0:j1].bitcast(FP8X4), got_plane1[:, j0 // 4 : j1 // 4].bitcast(U8)
+                return got_words[0][:, j0:j1].bitcast(FP8X4), got_planes[:, j0:j1]
+            return got_words[1][:, j0:j1].bitcast(FP8X4), got_plane1[:, j0 // 4 : j1 // 4].bitcast(U8)
+
+        down_bf = {}
+        down_codes = keep.tile([P, 2, R], U32, name="down_codes", align_bytes=64)
+        down_planes = keep.tile([P, 2, R], U8, name="down_planes", align_bytes=64)
+
+        def cast_down(a, half, tag):
+            down_bf[a, half] = keep.tile([P, PACK // 2, P, PACK], BF16, name=f"down_bf{a}{half}", tag=tag, align_bytes=64)
+            raw = down_raw[a][:].rearrange("p i (m t) -> p m t i", t=PACK)
+            copy = (nc.scalar.copy, nc.vector.tensor_copy)[half]
+            copy(down_bf[a, half][:].rearrange("p t m i -> p m t i"), raw[:, :, 2 * half : 2 * half + 2, :])
+
+        def quantize_down(a, half):
+            cols = slice(R // 2 * half, R // 2 * (half + 1))
+            nc.vector.quantize_mx(
+                out=down_codes[:, a, cols].bitcast(FP8X4),
+                scales=down_planes[:, a, cols],
+                in_=down_bf[a, half][:].rearrange("p t m i -> p (t m i)"),
+            )
+
+        h_banks = []
+
+        def h_pass(jb, a):
+            if a == 0:
+                h_banks.append(bank([P, PACK, P]))
+            codes, plane = tab_operand(a, P * jb, P * jb + P)
+            for t in range(PACK):
+                nc.tensor.matmul_mx(
+                    out=h_banks[jb][:, t, :],
+                    lhsT=down_codes[:, a, P * t : P * t + P].bitcast(FP8X4),
+                    lhsT_scale=down_planes[:, a, P * t : P * t + P],
+                    rhs=codes,
+                    rhs_scale=plane,
+                    start=(a == 0 and t == 0),
+                    stop=(a == 1 and t == PACK - 1),
+                )
+
+        got_words.append(keep.tile([P, S], U32, name="got_words0", tag="planes_then_ts", align_bytes=64))
+        gather_words(0, 0, S)
+        for w in range(WARM_PASSES):
+            warm_bank = bank([P, BANK])
+            codes, plane = tab_operand(0, 0, BANK)
+            few_codes, few_plane = tab_operand(0, 0, P)
+            nc.tensor.matmul_mx(out=warm_bank[:], lhsT=few_codes, lhsT_scale=few_plane, rhs=codes, rhs_scale=plane, start=True, stop=True)
+        cast_down(0, 0, "chain")
+        cast_down(0, 1, "b_then_down_then_words")
+        gather_ts(0, "words0")
+        quantize_down(0, 1)
+        quantize_down(0, 0)
+        gather_ts(1, "chain")
+        for jb in range(S // P):
+            h_pass(jb, 0)
+        cast_down(1, 0, "b_then_down_then_words")
+        cast_down(1, 1, "ts_all")
+        quantize_down(1, 1)
+        quantize_down(1, 0)
+        got_words.append(keep.tile([P, S], U32, name="got_words1", tag="b_then_down_then_words", align_bytes=64))
+
+        h_bf = [keep.tile([P, BANK, PACK], BF16, name=f"h_bf{jh}", tag=f"h_then_up{jh}", align_bytes=64) for jh in range(2)]
+        h_codes = []
+        h_plane = keep.tile([P, S], U8, name="h_plane", align_bytes=64)
+
+        def quantize_h(j0, j1):
+            jh, c0 = divmod(j0, BANK)
+            nc.vector.quantize_mx(
+                out=h_codes[jh][:, c0 : c0 + j1 - j0].bitcast(FP8X4),
+                scales=h_plane[:, j0:j1],
+                in_=h_bf[jh][:, c0 : c0 + j1 - j0, :].rearrange("p j t -> p (j t)"),
+            )
+
+        for j0 in range(0, S, 2 * P):
+            gather_words(1, j0, j0 + 2 * P)
+        for jb in range(S // P):
+            h_pass(jb, 1)
+            jh, c0 = divmod(P * jb, BANK)
+            nc.scalar.copy(h_bf[jh][:, c0 : c0 + P, :], h_banks[jb][:].rearrange("p t j -> p j t"))
 
         order = [(jh, n0 + n) for n0 in (0, UP_HALF // P) for jh in range(S // BANK) for n in range(UP_HALF // P)]
         y_banks = {}
 
-        def w4_pass(jh, n, a):
-            if a == 0:
-                y_banks[jh, n] = bank("y", [P, BANK])
-            codes, plane = tab_operand(a, BANK * jh, BANK * jh + BANK)
-            nc.tensor.matmul_mx(
-                out=y_banks[jh, n][:],
-                lhsT=w4_codes[:, a, 2 * P * n : 2 * P * (n + 1)].bitcast(FP4X4),
-                lhsT_scale=w4_planes[:, a, P // 4 * n : P // 4 * (n + 1)].bitcast(U8),
-                rhs=codes,
-                rhs_scale=plane,
-                start=(a == 0),
-                stop=False,
-            )
+        def w4_passes(jh, n):
+            y_banks[jh, n] = bank([P, BANK])
+            for a in range(2):
+                codes, plane = tab_operand(a, BANK * jh, BANK * jh + BANK)
+                nc.tensor.matmul_mx(
+                    out=y_banks[jh, n][:],
+                    lhsT=w4_codes[:, a, 2 * P * n : 2 * P * (n + 1)].bitcast(FP4X4),
+                    lhsT_scale=w4_planes[:, a, P // 4 * n : P // 4 * (n + 1)].bitcast(U8),
+                    rhs=codes,
+                    rhs_scale=plane,
+                    start=(a == 0),
+                    stop=False,
+                )
 
-        for jh, n in order[:Y_BANKS]:
-            w4_pass(jh, n, 0)
-
-        down_bf = [
-            keep.tile([P, PACK, P, PACK], BF16, name=f"down_bf{a}", tag=("ts_then_down_then_up", "down_bf1")[a], align_bytes=64)
-            for a in range(2)
-        ]
-        down_codes = keep.tile([P, 2, R], U32, name="down_codes", align_bytes=64)
-        down_planes = keep.tile([P, 2, R], U8, name="down_planes", align_bytes=64)
-
-        def cast_down(copy, a, raw, r0):
-            m0, m1 = r0 // PACK, (r0 + raw.shape[2]) // PACK
-            copy(down_bf[a][:, :, m0:m1, :].rearrange("p t m i -> p m t i"), raw.rearrange("p i (m t) -> p m t i", t=PACK))
-
-        def quantize_down(a, t0, t1):
-            cols = slice(P * t0, P * t1)
-            nc.vector.quantize_mx(
-                out=down_codes[:, a, cols].bitcast(FP8X4),
-                scales=down_planes[:, a, cols],
-                in_=down_bf[a][:, t0:t1, :, :].rearrange("p t m i -> p (t m i)"),
-            )
-
-        cast_down(nc.scalar.copy, 0, down0[:], 0)
-        up_lo = keep.tile([P, PACK, UP_HALF], F32, name="up_lo", tag="down_then_up")
-        nc.sync.dma_start(up_lo[:], up[:, 0:UP_HALF].rearrange("(p i) n -> p i n", i=PACK))
-        b_turned = bank("h", [P, PACK, P])
-        nc.tensor.transpose(b_turned[:, 0, :], b_rows[:], identity[:])
-        b_cols = keep.tile([P, M // P], F32, name="b_cols")
-        nc.scalar.copy(b_cols[:], b_turned[:, 0, 0 : M // P])
-        gather_words(got_words1, 1, 0, BANK)
-        quantize_down(0, 0, PACK)
-        up_hi = keep.tile([P, PACK, UP_HALF], F32, name="up_hi", tag="ts_then_down_then_up", align_bytes=64)
-        nc.sync.dma_start(up_hi[:], up[:, UP_HALF:M].rearrange("(p i) n -> p i n", i=PACK))
-        gather_words(got_words1, 1, BANK, S)
-        for jh, n in order[:Y_BANKS]:
-            w4_pass(jh, n, 1)
-        cast_down(nc.scalar.copy, 1, down1_lo[:], 0)
-        cast_down(nc.vector.tensor_copy, 1, down1_hi[:], DOWN_HALF)
-        quantize_down(1, 0, PACK // 2)
-        quantize_down(1, PACK // 2, PACK)
-
-        h_bf = keep.tile([P, S, PACK], BF16, name="h_bf", tag="h_then_up", align_bytes=64)
-        h_codes = keep.tile([P, S], U32, name="h_codes", align_bytes=64)
-        h_plane = keep.tile([P, S], U8, name="h_plane", align_bytes=64)
-
-        def h_block(jb):
-            acc = bank("h", [P, PACK, P])
-            for t in range(PACK):
-                for a in range(2):
-                    codes, plane = tab_operand(a, P * jb, P * jb + P)
-                    nc.tensor.matmul_mx(
-                        out=acc[:, t, :],
-                        lhsT=down_codes[:, a, P * t : P * t + P].bitcast(FP8X4),
-                        lhsT_scale=down_planes[:, a, P * t : P * t + P],
-                        rhs=codes,
-                        rhs_scale=plane,
-                        start=(a == 0),
-                        stop=(a == 1),
-                    )
-            nc.scalar.copy(h_bf[:, P * jb : P * jb + P, :], acc[:].rearrange("p t j -> p j t"))
-
-        def quantize_h(j0, j1):
-            nc.vector.quantize_mx(
-                out=h_codes[:, j0:j1].bitcast(FP8X4),
-                scales=h_plane[:, j0:j1],
-                in_=h_bf[:, j0:j1, :].rearrange("p j t -> p (j t)"),
-            )
-
-        up_bf = keep.tile([P, M, PACK], BF16, name="up_bf", align_bytes=64)
+        up_bf = []
         up_codes = []
         up_plane = keep.tile([P, M], U8, name="up_plane", align_bytes=64)
 
-        def quantize_up(u):
-            cols = slice(UP_HALF * u, UP_HALF * u + UP_HALF)
-            up_codes.append(keep.tile([P, UP_HALF], U32, name=f"up_codes{u}", tag=("up_codes0", "h_then_up")[u], align_bytes=64))
+        def quantize_up(u, tag):
+            up_codes.append(keep.tile([P, UP_HALF], U32, name=f"up_codes{u}", tag=tag, align_bytes=64))
             nc.vector.quantize_mx(
                 out=up_codes[u][:].bitcast(FP8X4),
-                scales=up_plane[:, cols],
-                in_=up_bf[:, cols, :].rearrange("p n i -> p (n i)"),
+                scales=up_plane[:, UP_HALF * u : UP_HALF * u + UP_HALF],
+                in_=up_bf[u][:].rearrange("p n i -> p (n i)"),
             )
 
-        def finish(jh, n):
+        def finish(i):
+            jh, n = order[i]
             acc = y_banks[jh, n]
             js = slice(BANK * jh, BANK * jh + BANK)
             ns = slice(P * n, P * n + P)
@@ -211,46 +225,43 @@ def tile_list_tabts_silu_kernel(tc, tab_words, tab_scales, w4_words, w4_scales, 
                 out=acc[:],
                 lhsT=up_codes[u][:, c : c + P].bitcast(FP8X4),
                 lhsT_scale=up_plane[:, ns],
-                rhs=h_codes[:, js].bitcast(FP8X4),
+                rhs=h_codes[jh][:].bitcast(FP8X4),
                 rhs_scale=h_plane[:, js],
                 start=False,
                 stop=True,
             )
-            scaled = epilogue.tile([P, BANK], F32, name="scaled")
-            result = epilogue.tile([P, BANK], F32, name="result")
-            step = BANK // 2 if (jh, n) == order[-1] else BANK
+            scaled = keep.tile([P, BANK], F32, name=f"scaled{i}", tag=f"scaled{i}", align_bytes=64)
+            result = keep.tile([P, BANK], F32, name=f"result{i}")
+            step = BANK // 2 if i == TILES - 1 else BANK
             for c0 in range(0, BANK, step):
                 cs = slice(c0, c0 + step)
                 out_cols = slice(BANK * jh + c0, BANK * jh + c0 + step)
-                nc.vector.tensor_tensor(scaled[:, cs], acc[:, cs], got_ts[:, out_cols], MULT)
+                nc.vector.tensor_tensor(scaled[:, cs], acc[:, cs], got_ts[jh][:, cs], MULT)
                 nc.scalar.activation(result[:, cs], scaled[:, cs], SILU, bias=b_cols[:, n : n + 1])
                 nc.sync.dma_start(out[ns, out_cols], result[:, cs])
 
-        h_block(0)
-        h_block(1)
+        up_bf.append(keep.tile([P, UP_HALF, PACK], BF16, name="up_bf0", tag="words1", align_bytes=64))
         nc.vector.tensor_copy(
-            up_bf[:, 0:UP_HALF, :].rearrange("p (c e) i -> p c i e", e=4),
-            up_lo[:].rearrange("p i (c e) -> p c i e", e=4),
+            up_bf[0][:].rearrange("p (c e) i -> p c i e", e=4),
+            up_raw[0][:].rearrange("p i (c e) -> p c i e", e=4),
         )
-        h_block(2)
+        h_codes.append(keep.tile([P, BANK], U32, name="h_codes0", tag="up_raw0", align_bytes=64))
         quantize_h(0, BANK // 2)
-        quantize_up(0)
-        h_block(3)
+        quantize_up(0, "up_codes0")
         quantize_h(BANK // 2, BANK)
+        for i in range(AHEAD):
+            w4_passes(*order[i])
+        finish(0)
+        h_codes.append(keep.tile([P, BANK], U32, name="h_codes1", tag="scaled0", align_bytes=64))
+        quantize_h(BANK, S)
+        up_bf.append(keep.tile([P, UP_HALF, PACK], BF16, name="up_bf1", tag="h_then_up1", align_bytes=64))
         for c0 in range(0, UP_HALF, P):
             nc.gpsimd.tensor_scalar(
-                up_bf[:, UP_HALF + c0 : UP_HALF + c0 + P, :], up_hi[:, :, c0 : c0 + P].rearrange("p i n -> p n i"), 1.0, 0.0, MULT, ADD
+                up_bf[1][:, c0 : c0 + P, :], up_raw[1][:, :, c0 : c0 + P].rearrange("p i n -> p n i"), 1.0, 0.0, MULT, ADD
             )
-        first_tiles = UP_HALF // P
-        for i in range(first_tiles):
-            h_block(BANK // P + i)
-            finish(*order[i])
-        quantize_h(BANK, S)
-        ahead = Y_BANKS - first_tiles
-        for i in range(first_tiles, TILES):
-            if i + ahead < TILES:
-                w4_pass(*order[i + ahead], 0)
-                w4_pass(*order[i + ahead], 1)
-            if i + ahead == TILES // 2:
-                quantize_up(1)
-            finish(*order[i])
+        for i in range(1, TILES):
+            if i + AHEAD - 1 < TILES:
+                w4_passes(*order[i + AHEAD - 1])
+            finish(i)
+            if i == UP1_AFTER:
+                quantize_up(1, f"scaled{i}")

@@ -24,8 +24,8 @@ K_PASS = P * PACK
 BANK = 512
 UP_HALF = M // 2
 PLANE_SHIFT = 16
-AHEAD = 3
-WARM_PASSES = 3
+AHEAD = 5
+WARM_PASSES = 2
 UP1_AFTER = 3
 TILES = (M // P) * (S // BANK)
 
@@ -34,36 +34,39 @@ def tile_list_tabts_silu_kernel(tc, tab_words, tab_scales, w4_words, w4_scales, 
     nc = tc.nc
     with ExitStack() as ctx:
         keep = ctx.enter_context(tc.tile_pool(name="keep", bufs=1))
-        psum = ctx.enter_context(tc.psum_pool(name="psum", bufs=8))
+        reuse = [ctx.enter_context(tc.tile_pool(name=f"reuse{a}", bufs=1)) for a in range(2)]
+        psum = ctx.enter_context(tc.psum_pool(name="psum", bufs=1))
 
-        def bank(shape):
-            return psum.tile(shape, F32, name="bank", tag="bank")
+        def bank(k, shape):
+            return psum.tile(shape, F32, name=f"bank{k}", tag=f"bank{k}")
 
         offsets = keep.tile([P, S // 16], U16, name="offsets")
-        ts_cols = keep.tile([P, T // P], F32, name="ts_cols", tag="chain", align_bytes=64)
-        nc.sync.dma_start(ts_cols[:], ts[0].rearrange("(c m) -> c m", c=P))
         nc.sync.dma_start(offsets[:], offs)
+        ts_cols = keep.tile([P, T // P], F32, name="ts_cols", tag="ts_then_down", align_bytes=64)
+        nc.sync.dma_start(ts_cols[:], ts[0].rearrange("(c m) -> c m", c=P))
 
-        tab_planes = keep.tile([P, T // 4], I32, name="tab_planes", tag="planes_then_ts", align_bytes=64)
+        tab_planes = keep.tile([P, T // 4], I32, name="tab_planes", align_bytes=64)
         w4_planes = keep.tile([P, 2, M // 4], I32, name="w4_planes", align_bytes=64)
         got_plane1 = keep.tile([P, S // 4], I32, name="got_plane1", align_bytes=64)
         warm = keep.tile([P, 16], F32, name="warm")
-        b_rows = keep.tile([P, P], F32, name="b_rows", tag="b_then_down_then_words", align_bytes=64)
+        b_rows = keep.tile([P, P], F32, name="b_rows")
         nc.gpsimd.memset(tab_planes[:], 0)
-        nc.vector.memset(b_rows[:], 0.0)
-        nc.vector.memset(warm[:, 0:8], 0.0)
+        nc.gpsimd.memset(b_rows[:], 0.0)
+        nc.gpsimd.memset(warm[:, 0:8], 0.0)
         nc.vector.memset(w4_planes[:], 0)
         nc.vector.memset(got_plane1[96:P, :], 0)
+
+        for r in range(4):
+            queue = (nc.sync, nc.scalar)[r // 2]
+            queue.dma_start(tab_planes[r:P:PLANE_SHIFT, :], tab_scales[:, r:16:4, :].rearrange("a q t -> q a t").bitcast(I32))
+        nc.scalar.dma_start(b_rows[0 : M // P, :], b.rearrange("(c p) -> c p", p=P))
         nc.scalar.activation(warm[:, 8:9], warm[:, 0:1], SILU)
 
         identity = keep.tile([P, P], F32, name="identity")
         make_identity(nc, identity[:])
 
-        for r in range(4):
-            nc.sync.dma_start(tab_planes[r:P:PLANE_SHIFT, :], tab_scales[:, r:16:4, :].rearrange("a q t -> q a t").bitcast(I32))
-        nc.sync.dma_start(b_rows[0 : M // P, :], b.rearrange("(c p) -> c p", p=P))
         words = [keep.tile([P, T], I32, name=f"words{a}", tag=f"words{a}", align_bytes=64) for a in range(2)]
-        down_raw = [keep.tile([P, PACK, R], F32, name=f"down_raw{a}") for a in range(2)]
+        down_raw = [reuse[a].tile([P, PACK, R], F32, name=f"down_raw{a}", offset=1024 * a, align_bytes=64) for a in range(2)]
         nc.sync.dma_start(words[0][:], tab_words[0].rearrange("p t i -> p (t i)").bitcast(I32))
         for a in range(2):
             nc.sync.dma_start(down_raw[a][:], down[K_PASS * a : K_PASS * (a + 1), :].rearrange("(p i) r -> p i r", i=PACK))
@@ -73,21 +76,22 @@ def tile_list_tabts_silu_kernel(tc, tab_words, tab_scales, w4_words, w4_scales, 
         def load_up(u):
             nc.sync.dma_start(up_raw[u][:], up[:, UP_HALF * u : UP_HALF * (u + 1)].rearrange("(p i) n -> p i n", i=PACK))
 
-        load_up(0)
-        w4_codes = keep.tile([P, 2, 2 * M], U8, name="w4_codes", align_bytes=64)
+        w4_codes = [keep.tile([P, 2, 2 * UP_HALF], U8, name=f"w4_codes{u}", align_bytes=64) for u in range(2)]
         for q in range(4):
             nc.sync.dma_start(w4_planes[32 * q : 32 * q + 4, :, :], w4_scales[:, 4 * q : 4 * q + 4, :].rearrange("a r n -> r a n").bitcast(I32))
-        nc.sync.dma_start(w4_codes[:].bitcast(I32), w4_words.rearrange("a p n -> p a n").bitcast(I32))
-        load_up(1)
+        for u in range(2):
+            w4_half = w4_words[:, :, 2 * UP_HALF * u : 2 * UP_HALF * (u + 1)]
+            nc.sync.dma_start(w4_codes[u][:].bitcast(I32), w4_half.rearrange("a p n -> p a n").bitcast(I32))
+            load_up(u)
 
         ts_all = keep.tile([P, T], F32, name="ts_all", tag="ts_all", align_bytes=64)
         ts_view = ts_all[:].rearrange("p (c m) -> p c m", m=T // P)
         for m0 in range(0, T // P, 4):
-            spread = bank([P, 4, P])
+            spread = bank(m0 // 4, [P, 4, P])
             for m in range(4):
                 nc.tensor.transpose(spread[:, m, :], ts_cols[:, m0 + m : m0 + m + 1].to_broadcast([P, P]), identity[:])
             nc.scalar.copy(ts_view[:, :, m0 : m0 + 4], spread[:].rearrange("p m c -> p c m"))
-        b_turned = bank([P, PACK, P])
+        b_turned = bank(4, [P, PACK, P])
         nc.tensor.transpose(b_turned[:, 0, :], b_rows[:], identity[:])
         b_cols = keep.tile([P, M // P], F32, name="b_cols")
         nc.scalar.copy(b_cols[:], b_turned[:, 0, 0 : M // P])
@@ -97,8 +101,8 @@ def tile_list_tabts_silu_kernel(tc, tab_words, tab_scales, w4_words, w4_scales, 
         nc.gpsimd.dma_start(got_plane1[0 : P - PLANE_SHIFT, :], got_planes[PLANE_SHIFT:P, :].bitcast(I32))
         got_ts = []
 
-        def gather_ts(jh, tag):
-            got_ts.append(keep.tile([P, BANK], F32, name=f"got_ts{jh}", tag=tag, align_bytes=64))
+        def gather_ts(jh):
+            got_ts.append(reuse[jh].tile([P, BANK], F32, name=f"got_ts{jh}", offset=4096, align_bytes=64))
             nc.vector.tensor_copy(got_ts[jh][:], ts_all[:].indirect(offsets[:, BANK // 16 * jh : BANK // 16 * (jh + 1)]))
 
         got_words = []
@@ -115,8 +119,12 @@ def tile_list_tabts_silu_kernel(tc, tab_words, tab_scales, w4_words, w4_scales, 
         down_codes = keep.tile([P, 2, R], U32, name="down_codes", align_bytes=64)
         down_planes = keep.tile([P, 2, R], U8, name="down_planes", align_bytes=64)
 
-        def cast_down(a, half, tag):
-            down_bf[a, half] = keep.tile([P, PACK // 2, P, PACK], BF16, name=f"down_bf{a}{half}", tag=tag, align_bytes=64)
+        def cast_down(a, half):
+            shape = [P, PACK // 2, P, PACK]
+            if a == 0:
+                down_bf[a, half] = keep.tile(shape, BF16, name=f"down_bf0{half}", tag=("ts_then_down", "down_bf01")[half], align_bytes=64)
+            else:
+                down_bf[a, half] = reuse[0].tile(shape, BF16, name=f"down_bf1{half}", offset=2048 * half, align_bytes=64)
             raw = down_raw[a][:].rearrange("p i (m t) -> p m t i", t=PACK)
             copy = (nc.scalar.copy, nc.vector.tensor_copy)[half]
             copy(down_bf[a, half][:].rearrange("p t m i -> p m t i"), raw[:, :, 2 * half : 2 * half + 2, :])
@@ -133,7 +141,7 @@ def tile_list_tabts_silu_kernel(tc, tab_words, tab_scales, w4_words, w4_scales, 
 
         def h_pass(jb, a):
             if a == 0:
-                h_banks.append(bank([P, PACK, P]))
+                h_banks.append(bank(jb, [P, PACK, P]))
             codes, plane = tab_operand(a, P * jb, P * jb + P)
             for t in range(PACK):
                 nc.tensor.matmul_mx(
@@ -146,26 +154,25 @@ def tile_list_tabts_silu_kernel(tc, tab_words, tab_scales, w4_words, w4_scales, 
                     stop=(a == 1 and t == PACK - 1),
                 )
 
-        got_words.append(keep.tile([P, S], U32, name="got_words0", tag="planes_then_ts", align_bytes=64))
+        got_words.append(keep.tile([P, S], U32, name="got_words0", align_bytes=64))
         gather_words(0, 0, S)
         for w in range(WARM_PASSES):
-            warm_bank = bank([P, BANK])
+            warm_bank = bank(3 + w % 2, [P, BANK])
             codes, plane = tab_operand(0, 0, BANK)
             few_codes, few_plane = tab_operand(0, 0, P)
             nc.tensor.matmul_mx(out=warm_bank[:], lhsT=few_codes, lhsT_scale=few_plane, rhs=codes, rhs_scale=plane, start=True, stop=True)
-        cast_down(0, 0, "chain")
-        cast_down(0, 1, "b_then_down_then_words")
-        gather_ts(0, "words0")
+        cast_down(0, 0)
+        cast_down(0, 1)
         quantize_down(0, 1)
         quantize_down(0, 0)
-        gather_ts(1, "chain")
+        gather_ts(0)
         for jb in range(S // P):
             h_pass(jb, 0)
-        cast_down(1, 0, "b_then_down_then_words")
-        cast_down(1, 1, "ts_all")
+        cast_down(1, 0)
+        cast_down(1, 1)
         quantize_down(1, 1)
         quantize_down(1, 0)
-        got_words.append(keep.tile([P, S], U32, name="got_words1", tag="b_then_down_then_words", align_bytes=64))
+        got_words.append(reuse[1].tile([P, S], U32, name="got_words1", offset=0, align_bytes=64))
 
         h_bf = [keep.tile([P, BANK, PACK], BF16, name=f"h_bf{jh}", tag=f"h_then_up{jh}", align_bytes=64) for jh in range(2)]
         h_codes = []
@@ -181,6 +188,7 @@ def tile_list_tabts_silu_kernel(tc, tab_words, tab_scales, w4_words, w4_scales, 
 
         for j0 in range(0, S, 2 * P):
             gather_words(1, j0, j0 + 2 * P)
+        gather_ts(1)
         for jb in range(S // P):
             h_pass(jb, 1)
             jh, c0 = divmod(P * jb, BANK)
@@ -189,13 +197,15 @@ def tile_list_tabts_silu_kernel(tc, tab_words, tab_scales, w4_words, w4_scales, 
         order = [(jh, n0 + n) for n0 in (0, UP_HALF // P) for jh in range(S // BANK) for n in range(UP_HALF // P)]
         y_banks = {}
 
-        def w4_passes(jh, n):
-            y_banks[jh, n] = bank([P, BANK])
+        def w4_passes(i):
+            jh, n = order[i]
+            y_banks[jh, n] = bank(i % 8, [P, BANK])
+            u, c = divmod(P * n, UP_HALF)
             for a in range(2):
                 codes, plane = tab_operand(a, BANK * jh, BANK * jh + BANK)
                 nc.tensor.matmul_mx(
                     out=y_banks[jh, n][:],
-                    lhsT=w4_codes[:, a, 2 * P * n : 2 * P * (n + 1)].bitcast(FP4X4),
+                    lhsT=w4_codes[u][:, a, 2 * c : 2 * (c + P)].bitcast(FP4X4),
                     lhsT_scale=w4_planes[:, a, P // 4 * n : P // 4 * (n + 1)].bitcast(U8),
                     rhs=codes,
                     rhs_scale=plane,
@@ -240,28 +250,27 @@ def tile_list_tabts_silu_kernel(tc, tab_words, tab_scales, w4_words, w4_scales, 
                 nc.scalar.activation(result[:, cs], scaled[:, cs], SILU, bias=b_cols[:, n : n + 1])
                 nc.sync.dma_start(out[ns, out_cols], result[:, cs])
 
-        up_bf.append(keep.tile([P, UP_HALF, PACK], BF16, name="up_bf0", tag="words1", align_bytes=64))
+        up_bf.append(reuse[1].tile([P, UP_HALF, PACK], BF16, name="up_bf0", offset=6144, align_bytes=64))
         nc.vector.tensor_copy(
             up_bf[0][:].rearrange("p (c e) i -> p c i e", e=4),
             up_raw[0][:].rearrange("p i (c e) -> p c i e", e=4),
         )
-        h_codes.append(keep.tile([P, BANK], U32, name="h_codes0", tag="up_raw0", align_bytes=64))
+        h_codes.append(keep.tile([P, BANK], U32, name="h_codes0", align_bytes=64))
         quantize_h(0, BANK // 2)
         quantize_up(0, "up_codes0")
         quantize_h(BANK // 2, BANK)
-        for i in range(AHEAD):
-            w4_passes(*order[i])
-        finish(0)
-        h_codes.append(keep.tile([P, BANK], U32, name="h_codes1", tag="scaled0", align_bytes=64))
+        h_codes.append(keep.tile([P, BANK], U32, name="h_codes1", align_bytes=64))
         quantize_h(BANK, S)
         up_bf.append(keep.tile([P, UP_HALF, PACK], BF16, name="up_bf1", tag="h_then_up1", align_bytes=64))
         for c0 in range(0, UP_HALF, P):
             nc.gpsimd.tensor_scalar(
                 up_bf[1][:, c0 : c0 + P, :], up_raw[1][:, :, c0 : c0 + P].rearrange("p i n -> p n i"), 1.0, 0.0, MULT, ADD
             )
-        for i in range(1, TILES):
-            if i + AHEAD - 1 < TILES:
-                w4_passes(*order[i + AHEAD - 1])
+        for i in range(AHEAD):
+            w4_passes(i)
+        for i in range(TILES):
+            if i >= AHEAD:
+                w4_passes(i)
             finish(i)
             if i == UP1_AFTER:
                 quantize_up(1, f"scaled{i}")

@@ -35,6 +35,7 @@ def tile_list_tabts_silu_kernel(tc, tab_words, tab_scales, w4_words, w4_scales, 
     with ExitStack() as ctx:
         keep = ctx.enter_context(tc.tile_pool(name="keep", bufs=1))
         reuse = [ctx.enter_context(tc.tile_pool(name=f"reuse{a}", bufs=1)) for a in range(2)]
+        after_ts = ctx.enter_context(tc.tile_pool(name="after_ts", bufs=1))
         psum = ctx.enter_context(tc.psum_pool(name="psum", bufs=1))
 
         def bank(k, shape):
@@ -42,19 +43,17 @@ def tile_list_tabts_silu_kernel(tc, tab_words, tab_scales, w4_words, w4_scales, 
 
         offsets = keep.tile([P, S // 16], U16, name="offsets")
         nc.sync.dma_start(offsets[:], offs)
-        ts_cols = keep.tile([P, T // P], F32, name="ts_cols", tag="ts_then_down", align_bytes=64)
+        ts_cols = after_ts.tile([P, T // P], F32, name="ts_cols", offset=2048 - 32)
         nc.sync.dma_start(ts_cols[:], ts[0].rearrange("(c m) -> c m", c=P))
 
         tab_planes = keep.tile([P, T // 4], I32, name="tab_planes", align_bytes=64)
         w4_planes = keep.tile([P, 2, M // 4], I32, name="w4_planes", align_bytes=64)
-        got_plane1 = keep.tile([P, S // 4], I32, name="got_plane1", align_bytes=64)
         warm = keep.tile([P, 16], F32, name="warm")
         b_rows = keep.tile([P, P], F32, name="b_rows")
         nc.gpsimd.memset(tab_planes[:], 0)
         nc.gpsimd.memset(b_rows[:], 0.0)
         nc.gpsimd.memset(warm[:, 0:8], 0.0)
         nc.vector.memset(w4_planes[:], 0)
-        nc.vector.memset(got_plane1[96:P, :], 0)
 
         for r in range(4):
             queue = (nc.sync, nc.scalar)[r // 2]
@@ -98,7 +97,9 @@ def tile_list_tabts_silu_kernel(tc, tab_words, tab_scales, w4_words, w4_scales, 
 
         got_planes = keep.tile([P, S], U8, name="got_planes", align_bytes=64)
         nc.vector.tensor_copy(got_planes[:], tab_planes[:].bitcast(U8).indirect(offsets[:]))
-        nc.gpsimd.dma_start(got_plane1[0 : P - PLANE_SHIFT, :], got_planes[PLANE_SHIFT:P, :].bitcast(I32))
+        got_plane1 = after_ts.tile([P, S // 4], I32, name="got_plane1", offset=2048, align_bytes=64)
+        nc.gpsimd.memset(got_plane1[96:P, :], 0)
+        nc.scalar.dma_start(got_plane1[0 : P - PLANE_SHIFT, :], got_planes[PLANE_SHIFT:P, :].bitcast(I32))
         got_ts = []
 
         def gather_ts(jh):
@@ -121,8 +122,10 @@ def tile_list_tabts_silu_kernel(tc, tab_words, tab_scales, w4_words, w4_scales, 
 
         def cast_down(a, half):
             shape = [P, PACK // 2, P, PACK]
-            if a == 0:
-                down_bf[a, half] = keep.tile(shape, BF16, name=f"down_bf0{half}", tag=("ts_then_down", "down_bf01")[half], align_bytes=64)
+            if (a, half) == (0, 0):
+                down_bf[a, half] = after_ts.tile(shape, BF16, name="down_bf00", offset=0, align_bytes=64)
+            elif a == 0:
+                down_bf[a, half] = keep.tile(shape, BF16, name="down_bf01", align_bytes=64)
             else:
                 down_bf[a, half] = reuse[0].tile(shape, BF16, name=f"down_bf1{half}", offset=2048 * half, align_bytes=64)
             raw = down_raw[a][:].rearrange("p i (m t) -> p m t i", t=PACK)

@@ -25,7 +25,6 @@ BANK = 512
 UP_HALF = M // 2
 PLANE_SHIFT = 16
 AHEAD = 5
-WARM_PASSES = 2
 UP1_AFTER = 3
 TILES = (M // P) * (S // BANK)
 
@@ -48,21 +47,18 @@ def tile_list_tabts_silu_kernel(tc, tab_words, tab_scales, w4_words, w4_scales, 
 
         tab_planes = keep.tile([P, T // 4], I32, name="tab_planes", align_bytes=64)
         w4_planes = keep.tile([P, 2, M // 4], I32, name="w4_planes", align_bytes=64)
-        warm = keep.tile([P, 16], F32, name="warm")
         b_rows = keep.tile([P, P], F32, name="b_rows")
         nc.gpsimd.memset(tab_planes[:], 0)
-        nc.gpsimd.memset(b_rows[:], 0.0)
-        nc.gpsimd.memset(warm[:, 0:8], 0.0)
         nc.vector.memset(w4_planes[:], 0)
 
         for r in range(4):
             queue = (nc.sync, nc.scalar)[r // 2]
             queue.dma_start(tab_planes[r:P:PLANE_SHIFT, :], tab_scales[:, r:16:4, :].rearrange("a q t -> q a t").bitcast(I32))
-        nc.scalar.dma_start(b_rows[0 : M // P, :], b.rearrange("(c p) -> c p", p=P))
-        nc.scalar.activation(warm[:, 8:9], warm[:, 0:1], SILU)
 
         identity = keep.tile([P, P], F32, name="identity")
         make_identity(nc, identity[:])
+        nc.scalar.activation(b_rows[:], identity[:], SILU, scale=0.0)
+        nc.scalar.dma_start(b_rows[0 : M // P, :], b.rearrange("(c p) -> c p", p=P))
 
         words = [keep.tile([P, T], I32, name=f"words{a}", tag=f"words{a}", align_bytes=64) for a in range(2)]
         down_raw = [reuse[a].tile([P, PACK, R], F32, name=f"down_raw{a}", offset=1024 * a, align_bytes=64) for a in range(2)]
@@ -159,11 +155,6 @@ def tile_list_tabts_silu_kernel(tc, tab_words, tab_scales, w4_words, w4_scales, 
 
         got_words.append(keep.tile([P, S], U32, name="got_words0", align_bytes=64))
         gather_words(0, 0, S)
-        for w in range(WARM_PASSES):
-            warm_bank = bank(3 + w % 2, [P, BANK])
-            codes, plane = tab_operand(0, 0, BANK)
-            few_codes, few_plane = tab_operand(0, 0, P)
-            nc.tensor.matmul_mx(out=warm_bank[:], lhsT=few_codes, lhsT_scale=few_plane, rhs=codes, rhs_scale=plane, start=True, stop=True)
         cast_down(0, 0)
         cast_down(0, 1)
         quantize_down(0, 1)

@@ -52,8 +52,7 @@ def tile_list_tabts_silu_kernel(tc, tab_words, tab_scales, w4_words, w4_scales, 
         nc.vector.memset(w4_planes[:], 0)
 
         for r in range(4):
-            queue = (nc.sync, nc.scalar)[r // 2]
-            queue.dma_start(tab_planes[r:P:PLANE_SHIFT, :], tab_scales[:, r:16:4, :].rearrange("a q t -> q a t").bitcast(I32))
+            nc.sync.dma_start(tab_planes[r:P:PLANE_SHIFT, :], tab_scales[:, r:16:4, :].rearrange("a q t -> q a t").bitcast(I32))
 
         identity = keep.tile([P, P], F32, name="identity")
         make_identity(nc, identity[:])

@@ -45,8 +45,8 @@ def tile_list_tabts_silu_kernel(tc, tab_words, tab_scales, w4_words, w4_scales, 
         ts_cols = after_ts.tile([P, T // P], F32, name="ts_cols", offset=2048 - 32)
         nc.sync.dma_start(ts_cols[:], ts[0].rearrange("(c m) -> c m", c=P))
 
-        tab_planes = keep.tile([P, T // 4], I32, name="tab_planes", align_bytes=64)
-        w4_planes = keep.tile([P, 2, M // 4], I32, name="w4_planes", align_bytes=64)
+        tab_planes = keep.tile([P, T // 4], I32, name="tab_planes", align_bytes=256)
+        w4_planes = keep.tile([P, 2, M // 4], I32, name="w4_planes", align_bytes=256)
         b_rows = keep.tile([P, P], F32, name="b_rows")
         nc.gpsimd.memset(tab_planes[:], 0)
         nc.vector.memset(w4_planes[:], 0)
@@ -59,18 +59,18 @@ def tile_list_tabts_silu_kernel(tc, tab_words, tab_scales, w4_words, w4_scales, 
         nc.scalar.activation(b_rows[:], identity[:], SILU, scale=0.0)
         nc.scalar.dma_start(b_rows[0 : M // P, :], b.rearrange("(c p) -> c p", p=P))
 
-        words = [keep.tile([P, T], I32, name=f"words{a}", tag=f"words{a}", align_bytes=64) for a in range(2)]
-        down_raw = [reuse[a].tile([P, PACK, R], F32, name=f"down_raw{a}", offset=1024 * a, align_bytes=64) for a in range(2)]
+        words = [keep.tile([P, T], I32, name=f"words{a}", tag=f"words{a}", align_bytes=256) for a in range(2)]
+        down_raw = [reuse[a].tile([P, PACK, R], F32, name=f"down_raw{a}", offset=1024 * a, align_bytes=256) for a in range(2)]
         nc.sync.dma_start(words[0][:], tab_words[0].rearrange("p t i -> p (t i)").bitcast(I32))
         for a in range(2):
             nc.sync.dma_start(down_raw[a][:], down[K_PASS * a : K_PASS * (a + 1), :].rearrange("(p i) r -> p i r", i=PACK))
         nc.sync.dma_start(words[1][:], tab_words[1].rearrange("p t i -> p (t i)").bitcast(I32))
-        up_raw = [keep.tile([P, PACK, UP_HALF], F32, name=f"up_raw{u}", tag=f"up_raw{u}", align_bytes=64) for u in range(2)]
+        up_raw = [keep.tile([P, PACK, UP_HALF], F32, name=f"up_raw{u}", tag=f"up_raw{u}", align_bytes=256) for u in range(2)]
 
         def load_up(u):
             nc.sync.dma_start(up_raw[u][:], up[:, UP_HALF * u : UP_HALF * (u + 1)].rearrange("(p i) n -> p i n", i=PACK))
 
-        w4_codes = [keep.tile([P, 2, 2 * UP_HALF], U8, name=f"w4_codes{u}", align_bytes=64) for u in range(2)]
+        w4_codes = [keep.tile([P, 2, 2 * UP_HALF], U8, name=f"w4_codes{u}", align_bytes=256) for u in range(2)]
         for q in range(4):
             nc.sync.dma_start(w4_planes[32 * q : 32 * q + 4, :, :], w4_scales[:, 4 * q : 4 * q + 4, :].rearrange("a r n -> r a n").bitcast(I32))
         for u in range(2):
@@ -78,7 +78,7 @@ def tile_list_tabts_silu_kernel(tc, tab_words, tab_scales, w4_words, w4_scales, 
             nc.sync.dma_start(w4_codes[u][:].bitcast(I32), w4_half.rearrange("a p n -> p a n").bitcast(I32))
             load_up(u)
 
-        ts_all = keep.tile([P, T], F32, name="ts_all", tag="ts_all", align_bytes=64)
+        ts_all = keep.tile([P, T], F32, name="ts_all", tag="ts_all", align_bytes=256)
         ts_view = ts_all[:].rearrange("p (c m) -> p c m", m=T // P)
         for m0 in range(0, T // P, 4):
             spread = bank(m0 // 4, [P, 4, P])
@@ -90,15 +90,15 @@ def tile_list_tabts_silu_kernel(tc, tab_words, tab_scales, w4_words, w4_scales, 
         b_cols = keep.tile([P, M // P], F32, name="b_cols")
         nc.scalar.copy(b_cols[:], b_turned[:, 0, 0 : M // P])
 
-        got_planes = keep.tile([P, S], U8, name="got_planes", align_bytes=64)
+        got_planes = keep.tile([P, S], U8, name="got_planes", align_bytes=256)
         nc.vector.tensor_copy(got_planes[:], tab_planes[:].bitcast(U8).indirect(offsets[:]))
-        got_plane1 = after_ts.tile([P, S // 4], I32, name="got_plane1", offset=2048, align_bytes=64)
+        got_plane1 = after_ts.tile([P, S // 4], I32, name="got_plane1", offset=2048, align_bytes=256)
         nc.gpsimd.memset(got_plane1[96:P, :], 0)
         nc.scalar.dma_start(got_plane1[0 : P - PLANE_SHIFT, :], got_planes[PLANE_SHIFT:P, :].bitcast(I32))
         got_ts = []
 
         def gather_ts(jh):
-            got_ts.append(reuse[jh].tile([P, BANK], F32, name=f"got_ts{jh}", offset=4096, align_bytes=64))
+            got_ts.append(reuse[jh].tile([P, BANK], F32, name=f"got_ts{jh}", offset=4096, align_bytes=256))
             nc.vector.tensor_copy(got_ts[jh][:], ts_all[:].indirect(offsets[:, BANK // 16 * jh : BANK // 16 * (jh + 1)]))
 
         got_words = []
@@ -112,17 +112,17 @@ def tile_list_tabts_silu_kernel(tc, tab_words, tab_scales, w4_words, w4_scales, 
             return got_words[1][:, j0:j1].bitcast(FP8X4), got_plane1[:, j0 // 4 : j1 // 4].bitcast(U8)
 
         down_bf = {}
-        down_codes = keep.tile([P, 2, R], U32, name="down_codes", align_bytes=64)
-        down_planes = keep.tile([P, 2, R], U8, name="down_planes", align_bytes=64)
+        down_codes = keep.tile([P, 2, R], U32, name="down_codes", align_bytes=256)
+        down_planes = keep.tile([P, 2, R], U8, name="down_planes", align_bytes=256)
 
         def cast_down(a, half):
             shape = [P, PACK // 2, P, PACK]
             if (a, half) == (0, 0):
-                down_bf[a, half] = after_ts.tile(shape, BF16, name="down_bf00", offset=0, align_bytes=64)
+                down_bf[a, half] = after_ts.tile(shape, BF16, name="down_bf00", offset=0, align_bytes=256)
             elif a == 0:
-                down_bf[a, half] = keep.tile(shape, BF16, name="down_bf01", align_bytes=64)
+                down_bf[a, half] = keep.tile(shape, BF16, name="down_bf01", align_bytes=256)
             else:
-                down_bf[a, half] = reuse[0].tile(shape, BF16, name=f"down_bf1{half}", offset=2048 * half, align_bytes=64)
+                down_bf[a, half] = reuse[0].tile(shape, BF16, name=f"down_bf1{half}", offset=2048 * half, align_bytes=256)
             raw = down_raw[a][:].rearrange("p i (m t) -> p m t i", t=PACK)
             copy = (nc.scalar.copy, nc.vector.tensor_copy)[half]
             copy(down_bf[a, half][:].rearrange("p t m i -> p m t i"), raw[:, :, 2 * half : 2 * half + 2, :])
@@ -152,7 +152,7 @@ def tile_list_tabts_silu_kernel(tc, tab_words, tab_scales, w4_words, w4_scales, 
                     stop=(a == 1 and t == PACK - 1),
                 )
 
-        got_words.append(keep.tile([P, S], U32, name="got_words0", align_bytes=64))
+        got_words.append(keep.tile([P, S], U32, name="got_words0", align_bytes=256))
         gather_words(0, 0, S)
         cast_down(0, 0)
         cast_down(0, 1)
@@ -165,11 +165,11 @@ def tile_list_tabts_silu_kernel(tc, tab_words, tab_scales, w4_words, w4_scales, 
         cast_down(1, 1)
         quantize_down(1, 1)
         quantize_down(1, 0)
-        got_words.append(reuse[1].tile([P, S], U32, name="got_words1", offset=0, align_bytes=64))
+        got_words.append(reuse[1].tile([P, S], U32, name="got_words1", offset=0, align_bytes=256))
 
-        h_bf = [keep.tile([P, BANK, PACK], BF16, name=f"h_bf{jh}", tag=f"h_then_up{jh}", align_bytes=64) for jh in range(2)]
+        h_bf = [keep.tile([P, BANK, PACK], BF16, name=f"h_bf{jh}", tag=f"h_then_up{jh}", align_bytes=256) for jh in range(2)]
         h_codes = []
-        h_plane = keep.tile([P, S], U8, name="h_plane", align_bytes=64)
+        h_plane = keep.tile([P, S], U8, name="h_plane", align_bytes=256)
 
         def quantize_h(j0, j1):
             jh, c0 = divmod(j0, BANK)
@@ -208,10 +208,10 @@ def tile_list_tabts_silu_kernel(tc, tab_words, tab_scales, w4_words, w4_scales, 
 
         up_bf = []
         up_codes = []
-        up_plane = keep.tile([P, M], U8, name="up_plane", align_bytes=64)
+        up_plane = keep.tile([P, M], U8, name="up_plane", align_bytes=256)
 
         def quantize_up(u, tag):
-            up_codes.append(keep.tile([P, UP_HALF], U32, name=f"up_codes{u}", tag=tag, align_bytes=64))
+            up_codes.append(keep.tile([P, UP_HALF], U32, name=f"up_codes{u}", tag=tag, align_bytes=256))
             nc.vector.quantize_mx(
                 out=up_codes[u][:].bitcast(FP8X4),
                 scales=up_plane[:, UP_HALF * u : UP_HALF * u + UP_HALF],
@@ -233,7 +233,7 @@ def tile_list_tabts_silu_kernel(tc, tab_words, tab_scales, w4_words, w4_scales, 
                 start=False,
                 stop=True,
             )
-            scaled = keep.tile([P, BANK], F32, name=f"scaled{i}", tag=f"scaled{i}", align_bytes=64)
+            scaled = keep.tile([P, BANK], F32, name=f"scaled{i}", tag=f"scaled{i}", align_bytes=256)
             result = keep.tile([P, BANK], F32, name=f"result{i}")
             step = BANK // 2 if i == TILES - 1 else BANK
             for c0 in range(0, BANK, step):
@@ -243,18 +243,18 @@ def tile_list_tabts_silu_kernel(tc, tab_words, tab_scales, w4_words, w4_scales, 
                 nc.scalar.activation(result[:, cs], scaled[:, cs], SILU, bias=b_cols[:, n : n + 1])
                 nc.sync.dma_start(out[ns, out_cols], result[:, cs])
 
-        up_bf.append(reuse[1].tile([P, UP_HALF, PACK], BF16, name="up_bf0", offset=6144, align_bytes=64))
+        up_bf.append(reuse[1].tile([P, UP_HALF, PACK], BF16, name="up_bf0", offset=6144, align_bytes=256))
         nc.vector.tensor_copy(
             up_bf[0][:].rearrange("p (c e) i -> p c i e", e=4),
             up_raw[0][:].rearrange("p i (c e) -> p c i e", e=4),
         )
-        h_codes.append(keep.tile([P, BANK], U32, name="h_codes0", align_bytes=64))
+        h_codes.append(keep.tile([P, BANK], U32, name="h_codes0", align_bytes=256))
         quantize_h(0, BANK // 2)
         quantize_up(0, "up_codes0")
         quantize_h(BANK // 2, BANK)
-        h_codes.append(keep.tile([P, BANK], U32, name="h_codes1", align_bytes=64))
+        h_codes.append(keep.tile([P, BANK], U32, name="h_codes1", align_bytes=256))
         quantize_h(BANK, S)
-        up_bf.append(keep.tile([P, UP_HALF, PACK], BF16, name="up_bf1", tag="h_then_up1", align_bytes=64))
+        up_bf.append(keep.tile([P, UP_HALF, PACK], BF16, name="up_bf1", tag="h_then_up1", align_bytes=256))
         for c0 in range(0, UP_HALF, P):
             nc.gpsimd.tensor_scalar(
                 up_bf[1][:, c0 : c0 + P, :], up_raw[1][:, :, c0 : c0 + P].rearrange("p i n -> p n i"), 1.0, 0.0, MULT, ADD

@@ -24,8 +24,8 @@ K_PASS = P * PACK
 BANK = 512
 UP_HALF = M // 2
 PLANE_SHIFT = 16
-AHEAD = 5
-UP1_AFTER = 3
+AHEAD = 6
+UP1_AFTER = 4
 TILES = (M // P) * (S // BANK)
 
 
@@ -49,6 +49,7 @@ def tile_list_tabts_silu_kernel(tc, tab_words, tab_scales, w4_words, w4_scales, 
         w4_planes = keep.tile([P, 2, M // 4], I32, name="w4_planes", align_bytes=256)
         b_rows = keep.tile([P, P], F32, name="b_rows")
         nc.gpsimd.memset(tab_planes[:], 0)
+        nc.vector.memset(b_rows[0:64, :], 0.0)
         nc.vector.memset(w4_planes[:], 0)
 
         for r in range(4):
@@ -56,8 +57,8 @@ def tile_list_tabts_silu_kernel(tc, tab_words, tab_scales, w4_words, w4_scales, 
 
         identity = keep.tile([P, P], F32, name="identity")
         make_identity(nc, identity[:])
-        nc.scalar.activation(b_rows[:], identity[:], SILU, scale=0.0)
         nc.scalar.dma_start(b_rows[0 : M // P, :], b.rearrange("(c p) -> c p", p=P))
+        nc.scalar.activation(b_rows[64:P, :], identity[64:P, :], SILU, scale=0.0)
 
         words = [keep.tile([P, T], I32, name=f"words{a}", tag=f"words{a}", align_bytes=256) for a in range(2)]
         down_raw = [reuse[a].tile([P, PACK, R], F32, name=f"down_raw{a}", offset=1024 * a, align_bytes=256) for a in range(2)]
@@ -98,7 +99,10 @@ def tile_list_tabts_silu_kernel(tc, tab_words, tab_scales, w4_words, w4_scales, 
         got_ts = []
 
         def gather_ts(jh):
-            got_ts.append(reuse[jh].tile([P, BANK], F32, name=f"got_ts{jh}", offset=4096, align_bytes=256))
+            if jh == 0:
+                got_ts.append(reuse[0].tile([P, BANK], F32, name="got_ts0", offset=4096, align_bytes=256))
+            else:
+                got_ts.append(keep.tile([P, BANK], F32, name="got_ts1", tag="words1", align_bytes=256))
             nc.vector.tensor_copy(got_ts[jh][:], ts_all[:].indirect(offsets[:, BANK // 16 * jh : BANK // 16 * (jh + 1)]))
 
         got_words = []

@@ -127,9 +127,9 @@ def tile_list_tabts_silu_kernel(tc, tab_words, tab_scales, w4_words, w4_scales, 
                 down_bf[a, half] = keep.tile(shape, BF16, name="down_bf01", align_bytes=256)
             else:
                 down_bf[a, half] = reuse[0].tile(shape, BF16, name=f"down_bf1{half}", offset=2048 * half, align_bytes=256)
-            raw = down_raw[a][:].rearrange("p i (m t) -> p m t i", t=PACK)
+            raw = down_raw[a][:].rearrange("p i (m t) -> p m i t", t=PACK)
             copy = (nc.scalar.copy, nc.vector.tensor_copy)[half]
-            copy(down_bf[a, half][:].rearrange("p t m i -> p m t i"), raw[:, :, 2 * half : 2 * half + 2, :])
+            copy(down_bf[a, half][:].rearrange("p t m i -> p m i t"), raw[:, :, :, 2 * half : 2 * half + 2])
 
         def quantize_down(a, half):
             cols = slice(R // 2 * half, R // 2 * (half + 1))

@@ -76,8 +76,11 @@ def tile_list_tabts_silu_kernel(tc, tab_words, tab_scales, w4_words, w4_scales, 
             nc.sync.dma_start(w4_planes[32 * q : 32 * q + 4, :, :], w4_scales[:, 4 * q : 4 * q + 4, :].rearrange("a r n -> r a n").bitcast(I32))
         for u in range(2):
             w4_half = w4_words[:, :, 2 * UP_HALF * u : 2 * UP_HALF * (u + 1)]
+            if u == 1:
+                load_up(u)
             nc.sync.dma_start(w4_codes[u][:].bitcast(I32), w4_half.rearrange("a p n -> p a n").bitcast(I32))
-            load_up(u)
+            if u == 0:
+                load_up(u)
 
         ts_all = keep.tile([P, T], F32, name="ts_all", tag="ts_all", align_bytes=256)
         ts_view = ts_all[:].rearrange("p (c m) -> p c m", m=T // P)
@@ -129,10 +132,10 @@ def tile_list_tabts_silu_kernel(tc, tab_words, tab_scales, w4_words, w4_scales, 
                 down_bf[a, half] = reuse[0].tile(shape, BF16, name=f"down_bf1{half}", offset=2048 * half, align_bytes=256)
             raw = down_raw[a][:].rearrange("p i (m t) -> p m i t", t=PACK)
             copy = (nc.scalar.copy, nc.vector.tensor_copy)[half]
-            copy(down_bf[a, half][:].rearrange("p t m i -> p m i t"), raw[:, :, :, 2 * half : 2 * half + 2])
+            copy(down_bf[a, half][:].rearrange("p t m i -> p m i t"), raw[:, :, :, 2 - 2 * half : 4 - 2 * half])
 
         def quantize_down(a, half):
-            cols = slice(R // 2 * half, R // 2 * (half + 1))
+            cols = slice(R // 2 * (1 - half), R // 2 * (2 - half))
             nc.vector.quantize_mx(
                 out=down_codes[:, a, cols].bitcast(FP8X4),
                 scales=down_planes[:, a, cols],
@@ -158,6 +161,10 @@ def tile_list_tabts_silu_kernel(tc, tab_words, tab_scales, w4_words, w4_scales, 
 
         got_words.append(keep.tile([P, S], U32, name="got_words0", align_bytes=256))
         gather_words(0, 0, S)
+        warm = bank(0, [P, BANK])
+        for w in range(3):
+            codes, plane = tab_operand(0, 0, BANK)
+            nc.tensor.matmul_mx(out=warm[:], lhsT=codes[:, 0:P], lhsT_scale=plane[:, 0:P], rhs=codes, rhs_scale=plane, start=True, stop=True)
         cast_down(0, 0)
         cast_down(0, 1)
         quantize_down(0, 1)
@@ -196,7 +203,7 @@ def tile_list_tabts_silu_kernel(tc, tab_words, tab_scales, w4_words, w4_scales, 
 
         def w4_passes(i):
             jh, n = order[i]
-            y_banks[jh, n] = bank(i % 8, [P, BANK])
+            y_banks[jh, n] = bank(i % AHEAD if i < 8 else (i - 2) % 8, [P, BANK])
             u, c = divmod(P * n, UP_HALF)
             for a in range(2):
                 codes, plane = tab_operand(a, BANK * jh, BANK * jh + BANK)
@@ -252,11 +259,11 @@ def tile_list_tabts_silu_kernel(tc, tab_words, tab_scales, w4_words, w4_scales, 
             up_bf[0][:].rearrange("p (c e) i -> p c i e", e=4),
             up_raw[0][:].rearrange("p i (c e) -> p c i e", e=4),
         )
-        h_codes.append(keep.tile([P, BANK], U32, name="h_codes0", align_bytes=256))
+        h_codes.append(keep.tile([P, BANK], U32, name="h_codes0", tag="up_raw0", align_bytes=256))
         quantize_h(0, BANK // 2)
         quantize_up(0, "up_codes0")
         quantize_h(BANK // 2, BANK)
-        h_codes.append(keep.tile([P, BANK], U32, name="h_codes1", align_bytes=256))
+        h_codes.append(reuse[1].tile([P, BANK], U32, name="h_codes1", offset=6144, align_bytes=256))
         quantize_h(BANK, S)
         up_bf.append(keep.tile([P, UP_HALF, PACK], BF16, name="up_bf1", tag="h_then_up1", align_bytes=256))
         for c0 in range(0, UP_HALF, P):

@@ -25,7 +25,7 @@ BANK = 512
 UP_HALF = M // 2
 PLANE_SHIFT = 16
 AHEAD = 6
-UP1_AFTER = 4
+UP1_AFTER = 5
 TILES = (M // P) * (S // BANK)
 
 
@@ -200,10 +200,11 @@ def tile_list_tabts_silu_kernel(tc, tab_words, tab_scales, w4_words, w4_scales, 
 
         order = [(jh, n0 + n) for n0 in (0, UP_HALF // P) for jh in range(S // BANK) for n in range(UP_HALF // P)]
         y_banks = {}
+        y_bank_order = [6, 7, 2, 3, 4, 5, 0, 1]
 
         def w4_passes(i):
             jh, n = order[i]
-            y_banks[jh, n] = bank(i % AHEAD if i < 8 else (i - 2) % 8, [P, BANK])
+            y_banks[jh, n] = bank(y_bank_order[i % 8] if i >= AHEAD else i, [P, BANK])
             u, c = divmod(P * n, UP_HALF)
             for a in range(2):
                 codes, plane = tab_operand(a, BANK * jh, BANK * jh + BANK)
@@ -273,8 +274,9 @@ def tile_list_tabts_silu_kernel(tc, tab_words, tab_scales, w4_words, w4_scales, 
         for i in range(AHEAD):
             w4_passes(i)
         for i in range(TILES):
-            if i >= AHEAD:
-                w4_passes(i)
+            last = i + 2 if i == TILES // 2 else i
+            while len(y_banks) <= last:
+                w4_passes(len(y_banks))
             finish(i)
             if i == UP1_AFTER:
-                quantize_up(1, f"scaled{i}")
+                quantize_up(1, f"scaled{i - 1}")

@@ -161,10 +161,6 @@ def tile_list_tabts_silu_kernel(tc, tab_words, tab_scales, w4_words, w4_scales, 
 
         got_words.append(keep.tile([P, S], U32, name="got_words0", align_bytes=256))
         gather_words(0, 0, S)
-        warm = bank(0, [P, BANK])
-        for w in range(3):
-            codes, plane = tab_operand(0, 0, BANK)
-            nc.tensor.matmul_mx(out=warm[:], lhsT=codes[:, 0:P], lhsT_scale=plane[:, 0:P], rhs=codes, rhs_scale=plane, start=True, stop=True)
         cast_down(0, 0)
         cast_down(0, 1)
         quantize_down(0, 1)

@@ -24,17 +24,18 @@ K_PASS = P * PACK
 BANK = 512
 UP_HALF = M // 2
 PLANE_SHIFT = 16
+TILES = (M // P) * (S // BANK)
 AHEAD = 6
 UP1_AFTER = 5
-TILES = (M // P) * (S // BANK)
 
 
 def tile_list_tabts_silu_kernel(tc, tab_words, tab_scales, w4_words, w4_scales, down, up, ts, b, offs, out):
     nc = tc.nc
     with ExitStack() as ctx:
         keep = ctx.enter_context(tc.tile_pool(name="keep", bufs=1))
-        reuse = [ctx.enter_context(tc.tile_pool(name=f"reuse{a}", bufs=1)) for a in range(2)]
         after_ts = ctx.enter_context(tc.tile_pool(name="after_ts", bufs=1))
+        after_down = [ctx.enter_context(tc.tile_pool(name=f"after_down{a}", bufs=1)) for a in range(2)]
+        after_words1 = ctx.enter_context(tc.tile_pool(name="after_words1", bufs=1))
         psum = ctx.enter_context(tc.psum_pool(name="psum", bufs=1))
 
         def bank(k, shape):
@@ -60,29 +61,45 @@ def tile_list_tabts_silu_kernel(tc, tab_words, tab_scales, w4_words, w4_scales, 
         nc.scalar.dma_start(b_rows[0 : M // P, :], b.rearrange("(c p) -> c p", p=P))
         nc.scalar.activation(b_rows[64:P, :], identity[64:P, :], SILU, scale=0.0)
 
-        words = [keep.tile([P, T], I32, name=f"words{a}", tag=f"words{a}", align_bytes=256) for a in range(2)]
-        down_raw = [reuse[a].tile([P, PACK, R], F32, name=f"down_raw{a}", offset=1024 * a, align_bytes=256) for a in range(2)]
-        nc.sync.dma_start(words[0][:], tab_words[0].rearrange("p t i -> p (t i)").bitcast(I32))
-        for a in range(2):
-            nc.sync.dma_start(down_raw[a][:], down[K_PASS * a : K_PASS * (a + 1), :].rearrange("(p i) r -> p i r", i=PACK))
-        nc.sync.dma_start(words[1][:], tab_words[1].rearrange("p t i -> p (t i)").bitcast(I32))
+        words = [
+            keep.tile([P, T], I32, name="words0", align_bytes=256),
+            after_words1.tile([P, T], I32, name="words1", offset=0, align_bytes=256),
+        ]
+        down_raw = [after_down[a].tile([P, PACK, R], F32, name=f"down_raw{a}", offset=0, align_bytes=256) for a in range(2)]
         up_raw = [keep.tile([P, PACK, UP_HALF], F32, name=f"up_raw{u}", tag=f"up_raw{u}", align_bytes=256) for u in range(2)]
+        w4_codes = [keep.tile([P, 2, 2 * UP_HALF], U8, name=f"w4_codes{u}", align_bytes=256) for u in range(2)]
+
+        def load_words(a):
+            nc.sync.dma_start(words[a][:], tab_words[a].rearrange("p t i -> p (t i)").bitcast(I32))
+
+        def load_down(a):
+            nc.sync.dma_start(down_raw[a][:], down[K_PASS * a : K_PASS * (a + 1), :].rearrange("(p i) r -> p i r", i=PACK))
 
         def load_up(u):
             nc.sync.dma_start(up_raw[u][:], up[:, UP_HALF * u : UP_HALF * (u + 1)].rearrange("(p i) n -> p i n", i=PACK))
 
-        w4_codes = [keep.tile([P, 2, 2 * UP_HALF], U8, name=f"w4_codes{u}", align_bytes=256) for u in range(2)]
-        for q in range(4):
-            nc.sync.dma_start(w4_planes[32 * q : 32 * q + 4, :, :], w4_scales[:, 4 * q : 4 * q + 4, :].rearrange("a r n -> r a n").bitcast(I32))
-        for u in range(2):
+        def load_w4(u):
             w4_half = w4_words[:, :, 2 * UP_HALF * u : 2 * UP_HALF * (u + 1)]
-            if u == 1:
-                load_up(u)
             nc.sync.dma_start(w4_codes[u][:].bitcast(I32), w4_half.rearrange("a p n -> p a n").bitcast(I32))
-            if u == 0:
-                load_up(u)
 
-        ts_all = keep.tile([P, T], F32, name="ts_all", tag="ts_all", align_bytes=256)
+        got_planes = keep.tile([P, S], U8, name="got_planes", align_bytes=256)
+        nc.vector.tensor_copy(got_planes[:], tab_planes[:].bitcast(U8).indirect(offsets[:]))
+        got_plane1 = keep.tile([P, S // 4], I32, name="got_plane1", align_bytes=256)
+        nc.gpsimd.memset(got_plane1[96:P, :], 0)
+
+        load_down(0)
+        load_words(0)
+        load_down(1)
+        load_words(1)
+        nc.sync.dma_start(got_plane1[0 : P - PLANE_SHIFT, :], got_planes[PLANE_SHIFT:P, :].bitcast(I32))
+        for r in range(4):
+            nc.sync.dma_start(w4_planes[r:P:32, :, :], w4_scales[:, r:16:4, :].rearrange("a q n -> q a n").bitcast(I32))
+        load_w4(0)
+        load_up(0)
+        load_up(1)
+        load_w4(1)
+
+        ts_all = keep.tile([P, T], F32, name="ts_all", align_bytes=256)
         ts_view = ts_all[:].rearrange("p (c m) -> p c m", m=T // P)
         for m0 in range(0, T // P, 4):
             spread = bank(m0 // 4, [P, 4, P])
@@ -94,61 +111,55 @@ def tile_list_tabts_silu_kernel(tc, tab_words, tab_scales, w4_words, w4_scales, 
         b_cols = keep.tile([P, M // P], F32, name="b_cols")
         nc.scalar.copy(b_cols[:], b_turned[:, 0, 0 : M // P])
 
-        got_planes = keep.tile([P, S], U8, name="got_planes", align_bytes=256)
-        nc.vector.tensor_copy(got_planes[:], tab_planes[:].bitcast(U8).indirect(offsets[:]))
-        got_plane1 = after_ts.tile([P, S // 4], I32, name="got_plane1", offset=2048, align_bytes=256)
-        nc.gpsimd.memset(got_plane1[96:P, :], 0)
-        nc.scalar.dma_start(got_plane1[0 : P - PLANE_SHIFT, :], got_planes[PLANE_SHIFT:P, :].bitcast(I32))
         got_ts = []
 
-        def gather_ts(jh):
-            if jh == 0:
-                got_ts.append(reuse[0].tile([P, BANK], F32, name="got_ts0", offset=4096, align_bytes=256))
-            else:
-                got_ts.append(keep.tile([P, BANK], F32, name="got_ts1", tag="words1", align_bytes=256))
+        def gather_ts(jh, pool, offset):
+            got_ts.append(pool.tile([P, BANK], F32, name=f"got_ts{jh}", offset=offset, align_bytes=256))
             nc.vector.tensor_copy(got_ts[jh][:], ts_all[:].indirect(offsets[:, BANK // 16 * jh : BANK // 16 * (jh + 1)]))
 
-        got_words = []
+        got_words = {}
 
-        def gather_words(a, j0, j1):
-            nc.vector.tensor_copy(got_words[a][:, j0:j1], words[a][:].bitcast(U32).indirect(offsets[:, j0 // 16 : j1 // 16]))
+        def gather_words(a, cuts, pool, offset):
+            j0 = cuts[0]
+            got = pool.tile([P, cuts[-1] - j0], U32, name=f"got_words{a}_{j0}", offset=offset, align_bytes=256)
+            for jh in range(j0 // BANK, cuts[-1] // BANK):
+                got_words[a, jh] = got[:, BANK * jh - j0 : BANK * (jh + 1) - j0]
+            for c0, c1 in zip(cuts[:-1], cuts[1:]):
+                nc.vector.tensor_copy(got[:, c0 - j0 : c1 - j0], words[a][:].bitcast(U32).indirect(offsets[:, c0 // 16 : c1 // 16]))
 
         def tab_operand(a, j0, j1):
+            jh, c0 = divmod(j0, BANK)
+            codes = got_words[a, jh][:, c0 : c0 + j1 - j0].bitcast(FP8X4)
             if a == 0:
-                return got_words[0][:, j0:j1].bitcast(FP8X4), got_planes[:, j0:j1]
-            return got_words[1][:, j0:j1].bitcast(FP8X4), got_plane1[:, j0 // 4 : j1 // 4].bitcast(U8)
+                return codes, got_planes[:, j0:j1]
+            return codes, got_plane1[:, j0 // 4 : j1 // 4].bitcast(U8)
 
         down_bf = {}
         down_codes = keep.tile([P, 2, R], U32, name="down_codes", align_bytes=256)
         down_planes = keep.tile([P, 2, R], U8, name="down_planes", align_bytes=256)
 
-        def cast_down(a, half):
+        def cast_down(a, half, copy):
             shape = [P, PACK // 2, P, PACK]
-            if (a, half) == (0, 0):
-                down_bf[a, half] = after_ts.tile(shape, BF16, name="down_bf00", offset=0, align_bytes=256)
-            elif a == 0:
-                down_bf[a, half] = keep.tile(shape, BF16, name="down_bf01", align_bytes=256)
-            else:
-                down_bf[a, half] = reuse[0].tile(shape, BF16, name=f"down_bf1{half}", offset=2048 * half, align_bytes=256)
+            pool, offset = (after_ts, 0) if a == 0 else (after_down[0], 4096)
+            down_bf[a, half] = pool.tile(shape, BF16, name=f"down_bf{a}{half}", offset=offset + 2048 * half, align_bytes=256)
             raw = down_raw[a][:].rearrange("p i (m t) -> p m i t", t=PACK)
-            copy = (nc.scalar.copy, nc.vector.tensor_copy)[half]
-            copy(down_bf[a, half][:].rearrange("p t m i -> p m i t"), raw[:, :, :, 2 - 2 * half : 4 - 2 * half])
+            copy(down_bf[a, half][:].rearrange("p t m i -> p m i t"), raw[:, :, :, 2 * half : 2 * half + 2])
 
         def quantize_down(a, half):
-            cols = slice(R // 2 * (1 - half), R // 2 * (2 - half))
+            cols = slice(R // 2 * half, R // 2 * (half + 1))
             nc.vector.quantize_mx(
                 out=down_codes[:, a, cols].bitcast(FP8X4),
                 scales=down_planes[:, a, cols],
                 in_=down_bf[a, half][:].rearrange("p t m i -> p (t m i)"),
             )
 
-        h_banks = []
+        h_banks = {}
 
-        def h_pass(jb, a):
-            if a == 0:
-                h_banks.append(bank(jb, [P, PACK, P]))
+        def h_passes(jb, a, t0, t1):
+            if jb not in h_banks:
+                h_banks[jb] = bank(jb, [P, PACK, P])
             codes, plane = tab_operand(a, P * jb, P * jb + P)
-            for t in range(PACK):
+            for t in range(t0, t1):
                 nc.tensor.matmul_mx(
                     out=h_banks[jb][:, t, :],
                     lhsT=down_codes[:, a, P * t : P * t + P].bitcast(FP8X4),
@@ -159,24 +170,33 @@ def tile_list_tabts_silu_kernel(tc, tab_words, tab_scales, w4_words, w4_scales, 
                     stop=(a == 1 and t == PACK - 1),
                 )
 
-        got_words.append(keep.tile([P, S], U32, name="got_words0", align_bytes=256))
-        gather_words(0, 0, S)
-        cast_down(0, 0)
-        cast_down(0, 1)
-        quantize_down(0, 1)
-        quantize_down(0, 0)
-        gather_ts(0)
-        for jb in range(S // P):
-            h_pass(jb, 0)
-        cast_down(1, 0)
-        cast_down(1, 1)
-        quantize_down(1, 1)
-        quantize_down(1, 0)
-        got_words.append(reuse[1].tile([P, S], U32, name="got_words1", offset=0, align_bytes=256))
+        order = [(jh, n0 + n) for n0 in (0, UP_HALF // P) for jh in range(S // BANK) for n in range(UP_HALF // P)]
+        y_banks = {}
+        y_bank_order = [6, 7, 2, 3, 4, 5, 0, 1]
+
+        def w4_pass(i, a):
+            jh, n = order[i]
+            if a == 0:
+                y_banks[i] = bank(y_bank_order[i % 8] if i >= AHEAD else i, [P, BANK])
+            u, c = divmod(P * n, UP_HALF)
+            codes, plane = tab_operand(a, BANK * jh, BANK * jh + BANK)
+            nc.tensor.matmul_mx(
+                out=y_banks[i][:],
+                lhsT=w4_codes[u][:, a, 2 * c : 2 * (c + P)].bitcast(FP4X4),
+                lhsT_scale=w4_planes[:, a, P // 4 * n : P // 4 * (n + 1)].bitcast(U8),
+                rhs=codes,
+                rhs_scale=plane,
+                start=(a == 0),
+                stop=False,
+            )
 
         h_bf = [keep.tile([P, BANK, PACK], BF16, name=f"h_bf{jh}", tag=f"h_then_up{jh}", align_bytes=256) for jh in range(2)]
         h_codes = []
         h_plane = keep.tile([P, S], U8, name="h_plane", align_bytes=256)
+
+        def empty_h(jb):
+            jh, c0 = divmod(P * jb, BANK)
+            nc.scalar.copy(h_bf[jh][:, c0 : c0 + P, :], h_banks[jb][:].rearrange("p t j -> p j t"))
 
         def quantize_h(j0, j1):
             jh, c0 = divmod(j0, BANK)
@@ -185,34 +205,6 @@ def tile_list_tabts_silu_kernel(tc, tab_words, tab_scales, w4_words, w4_scales, 
                 scales=h_plane[:, j0:j1],
                 in_=h_bf[jh][:, c0 : c0 + j1 - j0, :].rearrange("p j t -> p (j t)"),
             )
-
-        for j0 in range(0, S, 2 * P):
-            gather_words(1, j0, j0 + 2 * P)
-        gather_ts(1)
-        for jb in range(S // P):
-            h_pass(jb, 1)
-            jh, c0 = divmod(P * jb, BANK)
-            nc.scalar.copy(h_bf[jh][:, c0 : c0 + P, :], h_banks[jb][:].rearrange("p t j -> p j t"))
-
-        order = [(jh, n0 + n) for n0 in (0, UP_HALF // P) for jh in range(S // BANK) for n in range(UP_HALF // P)]
-        y_banks = {}
-        y_bank_order = [6, 7, 2, 3, 4, 5, 0, 1]
-
-        def w4_passes(i):
-            jh, n = order[i]
-            y_banks[jh, n] = bank(y_bank_order[i % 8] if i >= AHEAD else i, [P, BANK])
-            u, c = divmod(P * n, UP_HALF)
-            for a in range(2):
-                codes, plane = tab_operand(a, BANK * jh, BANK * jh + BANK)
-                nc.tensor.matmul_mx(
-                    out=y_banks[jh, n][:],
-                    lhsT=w4_codes[u][:, a, 2 * c : 2 * (c + P)].bitcast(FP4X4),
-                    lhsT_scale=w4_planes[:, a, P // 4 * n : P // 4 * (n + 1)].bitcast(U8),
-                    rhs=codes,
-                    rhs_scale=plane,
-                    start=(a == 0),
-                    stop=False,
-                )
 
         up_bf = []
         up_codes = []
@@ -228,7 +220,7 @@ def tile_list_tabts_silu_kernel(tc, tab_words, tab_scales, w4_words, w4_scales, 
 
         def finish(i):
             jh, n = order[i]
-            acc = y_banks[jh, n]
+            acc = y_banks[i]
             js = slice(BANK * jh, BANK * jh + BANK)
             ns = slice(P * n, P * n + P)
             u, c = divmod(P * n, UP_HALF)
@@ -251,7 +243,28 @@ def tile_list_tabts_silu_kernel(tc, tab_words, tab_scales, w4_words, w4_scales, 
                 nc.scalar.activation(result[:, cs], scaled[:, cs], SILU, bias=b_cols[:, n : n + 1])
                 nc.sync.dma_start(out[ns, out_cols], result[:, cs])
 
-        up_bf.append(reuse[1].tile([P, UP_HALF, PACK], BF16, name="up_bf0", offset=6144, align_bytes=256))
+        gather_ts(0, after_ts, 4096)
+        cast_down(0, 0, nc.scalar.copy)
+        cast_down(0, 1, nc.scalar.copy)
+        quantize_down(0, 0)
+        gather_words(0, [0, P, 2 * P, BANK], after_ts, 0)
+        quantize_down(0, 1)
+        gather_words(0, [BANK, S], after_down[0], 2048)
+        for jb in range(BANK // P):
+            h_passes(jb, 0, 0, 2)
+        for jb in range(S // P):
+            h_passes(jb, 0, 2 if jb < BANK // P else 0, PACK)
+        cast_down(1, 0, nc.scalar.copy)
+        cast_down(1, 1, nc.vector.tensor_copy)
+        quantize_down(1, 0)
+        quantize_down(1, 1)
+        gather_words(1, [0, P, 3 * P, 5 * P, 7 * P, S], after_down[0], 4096)
+        for jb in range(S // P):
+            h_passes(jb, 1, 0, PACK)
+            empty_h(jb)
+        gather_ts(1, after_words1, 0)
+
+        up_bf.append(after_words1.tile([P, UP_HALF, PACK], BF16, name="up_bf0", offset=4096, align_bytes=256))
         nc.vector.tensor_copy(
             up_bf[0][:].rearrange("p (c e) i -> p c i e", e=4),
             up_raw[0][:].rearrange("p i (c e) -> p c i e", e=4),
@@ -260,19 +273,19 @@ def tile_list_tabts_silu_kernel(tc, tab_words, tab_scales, w4_words, w4_scales, 
         quantize_h(0, BANK // 2)
         quantize_up(0, "up_codes0")
         quantize_h(BANK // 2, BANK)
-        h_codes.append(reuse[1].tile([P, BANK], U32, name="h_codes1", offset=6144, align_bytes=256))
+        h_codes.append(after_words1.tile([P, BANK], U32, name="h_codes1", offset=4096, align_bytes=256))
         quantize_h(BANK, S)
         up_bf.append(keep.tile([P, UP_HALF, PACK], BF16, name="up_bf1", tag="h_then_up1", align_bytes=256))
         for c0 in range(0, UP_HALF, P):
             nc.gpsimd.tensor_scalar(
                 up_bf[1][:, c0 : c0 + P, :], up_raw[1][:, :, c0 : c0 + P].rearrange("p i n -> p n i"), 1.0, 0.0, MULT, ADD
             )
-        for i in range(AHEAD):
-            w4_passes(i)
         for i in range(TILES):
-            last = i + 2 if i == TILES // 2 else i
+            last = max(AHEAD - 1, i + 2 if i == TILES // 2 else i)
             while len(y_banks) <= last:
-                w4_passes(len(y_banks))
+                started = len(y_banks)
+                w4_pass(started, 0)
+                w4_pass(started, 1)
             finish(i)
             if i == UP1_AFTER:
                 quantize_up(1, f"scaled{i - 1}")

@@ -25,7 +25,9 @@ BANK = 512
 UP_HALF = M // 2
 PLANE_SHIFT = 16
 TILES = (M // P) * (S // BANK)
-AHEAD = 6
+WAIT_LEAD = 4
+UP_FIRST = M // 4
+LEAD = 2
 UP1_AFTER = 5
 
 
@@ -36,6 +38,7 @@ def tile_list_tabts_silu_kernel(tc, tab_words, tab_scales, w4_words, w4_scales, 
         after_ts = ctx.enter_context(tc.tile_pool(name="after_ts", bufs=1))
         after_down = [ctx.enter_context(tc.tile_pool(name=f"after_down{a}", bufs=1)) for a in range(2)]
         after_words1 = ctx.enter_context(tc.tile_pool(name="after_words1", bufs=1))
+        after_h0 = ctx.enter_context(tc.tile_pool(name="after_h0", bufs=1))
         psum = ctx.enter_context(tc.psum_pool(name="psum", bufs=1))
 
         def bank(k, shape):
@@ -66,7 +69,10 @@ def tile_list_tabts_silu_kernel(tc, tab_words, tab_scales, w4_words, w4_scales, 
             after_words1.tile([P, T], I32, name="words1", offset=0, align_bytes=256),
         ]
         down_raw = [after_down[a].tile([P, PACK, R], F32, name=f"down_raw{a}", offset=0, align_bytes=256) for a in range(2)]
-        up_raw = [keep.tile([P, PACK, UP_HALF], F32, name=f"up_raw{u}", tag=f"up_raw{u}", align_bytes=256) for u in range(2)]
+        up_cuts = [0, UP_FIRST, UP_HALF, M]
+        up_raw = [
+            keep.tile([P, PACK, up_cuts[u + 1] - up_cuts[u]], F32, name=f"up_raw{u}", tag=f"up_raw{u}", align_bytes=256) for u in range(3)
+        ]
         w4_codes = [keep.tile([P, 2, 2 * UP_HALF], U8, name=f"w4_codes{u}", align_bytes=256) for u in range(2)]
 
         def load_words(a):
@@ -76,7 +82,7 @@ def tile_list_tabts_silu_kernel(tc, tab_words, tab_scales, w4_words, w4_scales, 
             nc.sync.dma_start(down_raw[a][:], down[K_PASS * a : K_PASS * (a + 1), :].rearrange("(p i) r -> p i r", i=PACK))
 
         def load_up(u):
-            nc.sync.dma_start(up_raw[u][:], up[:, UP_HALF * u : UP_HALF * (u + 1)].rearrange("(p i) n -> p i n", i=PACK))
+            nc.sync.dma_start(up_raw[u][:], up[:, up_cuts[u] : up_cuts[u + 1]].rearrange("(p i) n -> p i n", i=PACK))
 
         def load_w4(u):
             w4_half = w4_words[:, :, 2 * UP_HALF * u : 2 * UP_HALF * (u + 1)]
@@ -92,11 +98,12 @@ def tile_list_tabts_silu_kernel(tc, tab_words, tab_scales, w4_words, w4_scales, 
         load_down(1)
         load_words(1)
         nc.sync.dma_start(got_plane1[0 : P - PLANE_SHIFT, :], got_planes[PLANE_SHIFT:P, :].bitcast(I32))
+        load_up(0)
         for r in range(4):
             nc.sync.dma_start(w4_planes[r:P:32, :, :], w4_scales[:, r:16:4, :].rearrange("a q n -> q a n").bitcast(I32))
         load_w4(0)
-        load_up(0)
         load_up(1)
+        load_up(2)
         load_w4(1)
 
         ts_all = keep.tile([P, T], F32, name="ts_all", align_bytes=256)
@@ -170,14 +177,13 @@ def tile_list_tabts_silu_kernel(tc, tab_words, tab_scales, w4_words, w4_scales, 
                     stop=(a == 1 and t == PACK - 1),
                 )
 
-        order = [(jh, n0 + n) for n0 in (0, UP_HALF // P) for jh in range(S // BANK) for n in range(UP_HALF // P)]
+        order = [(jh, n0 + n) for n0 in range(0, M // P, 2) for jh in range(S // BANK) for n in range(2)]
         y_banks = {}
-        y_bank_order = [6, 7, 2, 3, 4, 5, 0, 1]
 
         def w4_pass(i, a):
             jh, n = order[i]
             if a == 0:
-                y_banks[i] = bank(y_bank_order[i % 8] if i >= AHEAD else i, [P, BANK])
+                y_banks[i] = bank(i % 8, [P, BANK])
             u, c = divmod(P * n, UP_HALF)
             codes, plane = tab_operand(a, BANK * jh, BANK * jh + BANK)
             nc.tensor.matmul_mx(
@@ -190,7 +196,10 @@ def tile_list_tabts_silu_kernel(tc, tab_words, tab_scales, w4_words, w4_scales, 
                 stop=False,
             )
 
-        h_bf = [keep.tile([P, BANK, PACK], BF16, name=f"h_bf{jh}", tag=f"h_then_up{jh}", align_bytes=256) for jh in range(2)]
+        h_bf = [
+            after_h0.tile([P, BANK, PACK], BF16, name="h_bf0", offset=0, align_bytes=256),
+            keep.tile([P, BANK, PACK], BF16, name="h_bf1", tag="h_bf1", align_bytes=256),
+        ]
         h_codes = []
         h_plane = keep.tile([P, S], U8, name="h_plane", align_bytes=256)
 
@@ -206,27 +215,27 @@ def tile_list_tabts_silu_kernel(tc, tab_words, tab_scales, w4_words, w4_scales, 
                 in_=h_bf[jh][:, c0 : c0 + j1 - j0, :].rearrange("p j t -> p (j t)"),
             )
 
-        up_bf = []
-        up_codes = []
+        up_codes = {}
         up_plane = keep.tile([P, M], U8, name="up_plane", align_bytes=256)
 
-        def quantize_up(u, tag):
-            up_codes.append(keep.tile([P, UP_HALF], U32, name=f"up_codes{u}", tag=tag, align_bytes=256))
+        def quantize_up(n0, rounded, codes):
+            width = rounded.shape[1]
             nc.vector.quantize_mx(
-                out=up_codes[u][:].bitcast(FP8X4),
-                scales=up_plane[:, UP_HALF * u : UP_HALF * u + UP_HALF],
-                in_=up_bf[u][:].rearrange("p n i -> p (n i)"),
+                out=codes[:].bitcast(FP8X4),
+                scales=up_plane[:, n0 : n0 + width],
+                in_=rounded.rearrange("p n i -> p (n i)"),
             )
+            for c in range(0, width, P):
+                up_codes[(n0 + c) // P] = codes[:, c : c + P]
 
         def finish(i):
             jh, n = order[i]
             acc = y_banks[i]
             js = slice(BANK * jh, BANK * jh + BANK)
             ns = slice(P * n, P * n + P)
-            u, c = divmod(P * n, UP_HALF)
             nc.tensor.matmul_mx(
                 out=acc[:],
-                lhsT=up_codes[u][:, c : c + P].bitcast(FP8X4),
+                lhsT=up_codes[n].bitcast(FP8X4),
                 lhsT_scale=up_plane[:, ns],
                 rhs=h_codes[jh][:].bitcast(FP8X4),
                 rhs_scale=h_plane[:, js],
@@ -249,7 +258,7 @@ def tile_list_tabts_silu_kernel(tc, tab_words, tab_scales, w4_words, w4_scales, 
         quantize_down(0, 0)
         gather_words(0, [0, P, 2 * P, BANK], after_ts, 0)
         quantize_down(0, 1)
-        gather_words(0, [BANK, S], after_down[0], 2048)
+        gather_words(0, [BANK, S], after_down[0], 0)
         for jb in range(BANK // P):
             h_passes(jb, 0, 0, 2)
         for jb in range(S // P):
@@ -258,34 +267,37 @@ def tile_list_tabts_silu_kernel(tc, tab_words, tab_scales, w4_words, w4_scales, 
         cast_down(1, 1, nc.vector.tensor_copy)
         quantize_down(1, 0)
         quantize_down(1, 1)
-        gather_words(1, [0, P, 3 * P, 5 * P, 7 * P, S], after_down[0], 4096)
+        gather_words(1, [0, P, 3 * P, 5 * P, 7 * P, S], after_down[0], 2048)
         for jb in range(S // P):
             h_passes(jb, 1, 0, PACK)
             empty_h(jb)
-        gather_ts(1, after_words1, 0)
 
-        up_bf.append(after_words1.tile([P, UP_HALF, PACK], BF16, name="up_bf0", offset=4096, align_bytes=256))
-        nc.vector.tensor_copy(
-            up_bf[0][:].rearrange("p (c e) i -> p c i e", e=4),
-            up_raw[0][:].rearrange("p i (c e) -> p c i e", e=4),
-        )
-        h_codes.append(keep.tile([P, BANK], U32, name="h_codes0", tag="up_raw0", align_bytes=256))
+        up_bf0 = after_down[0].tile([P, UP_FIRST, PACK], BF16, name="up_bf0", offset=7168, align_bytes=256)
+        nc.vector.tensor_copy(up_bf0[:].rearrange("p (c e) i -> p c i e", e=4), up_raw[0][:].rearrange("p i (c e) -> p c i e", e=4))
+        h_codes.append(keep.tile([P, BANK], U32, name="h_codes0", align_bytes=256))
         quantize_h(0, BANK // 2)
-        quantize_up(0, "up_codes0")
+        quantize_up(0, up_bf0[:], keep.tile([P, UP_FIRST], U32, name="up_codes0", align_bytes=256))
         quantize_h(BANK // 2, BANK)
-        h_codes.append(after_words1.tile([P, BANK], U32, name="h_codes1", offset=4096, align_bytes=256))
-        quantize_h(BANK, S)
-        up_bf.append(keep.tile([P, UP_HALF, PACK], BF16, name="up_bf1", tag="h_then_up1", align_bytes=256))
-        for c0 in range(0, UP_HALF, P):
-            nc.gpsimd.tensor_scalar(
-                up_bf[1][:, c0 : c0 + P, :], up_raw[1][:, :, c0 : c0 + P].rearrange("p i n -> p n i"), 1.0, 0.0, MULT, ADD
-            )
+        gather_ts(1, after_h0, 0)
+        up_bf1 = after_h0.tile([P, UP_FIRST, PACK], BF16, name="up_bf1", offset=2048, align_bytes=256)
+        nc.scalar.copy(up_bf1[:].rearrange("p (c e) i -> p c i e", e=4), up_raw[1][:].rearrange("p i (c e) -> p c i e", e=4))
         for i in range(TILES):
-            last = max(AHEAD - 1, i + 2 if i == TILES // 2 else i)
+            last = i + (WAIT_LEAD if i == 2 else min(LEAD, (TILES - 1 - i) // 3))
             while len(y_banks) <= last:
                 started = len(y_banks)
                 w4_pass(started, 0)
                 w4_pass(started, 1)
             finish(i)
+            if i == 0:
+                h_codes.append(keep.tile([P, BANK], U32, name="h_codes1", align_bytes=256))
+                quantize_h(BANK, S)
+                up_bf2 = keep.tile([P, UP_HALF, PACK], BF16, name="up_bf2", tag="h_bf1", align_bytes=256)
+                for c0 in range(0, UP_HALF, P):
+                    nc.gpsimd.tensor_scalar(
+                        up_bf2[:, c0 : c0 + P, :], up_raw[2][:, :, c0 : c0 + P].rearrange("p i n -> p n i"), 1.0, 0.0, MULT, ADD
+                    )
+            if i == 1:
+                quantize_up(UP_FIRST, up_bf1[:], keep.tile([P, UP_FIRST], U32, name="up_codes1", align_bytes=256))
             if i == UP1_AFTER:
-                quantize_up(1, f"scaled{i - 1}")
+                codes = keep.tile([P, UP_HALF], U32, name="up_codes2", tag=f"scaled{i - 2}", align_bytes=256)
+                quantize_up(UP_HALF, up_bf2[:], codes)

@@ -145,12 +145,15 @@ def tile_list_tabts_silu_kernel(tc, tab_words, tab_scales, w4_words, w4_scales, 
         down_codes = keep.tile([P, 2, R], U32, name="down_codes", align_bytes=256)
         down_planes = keep.tile([P, 2, R], U8, name="down_planes", align_bytes=256)
 
-        def cast_down(a, half, copy):
+        def cast_down(a, half, copies):
             shape = [P, PACK // 2, P, PACK]
             pool, offset = (after_ts, 0) if a == 0 else (after_down[0], 4096)
             down_bf[a, half] = pool.tile(shape, BF16, name=f"down_bf{a}{half}", offset=offset + 2048 * half, align_bytes=256)
             raw = down_raw[a][:].rearrange("p i (m t) -> p m i t", t=PACK)
-            copy(down_bf[a, half][:].rearrange("p t m i -> p m i t"), raw[:, :, :, 2 * half : 2 * half + 2])
+            share = P // len(copies)
+            for k, copy in enumerate(copies):
+                ms = slice(share * k, share * (k + 1))
+                copy(down_bf[a, half][:, :, ms, :].rearrange("p t m i -> p m i t"), raw[:, ms, :, 2 * half : 2 * half + 2])
 
         def quantize_down(a, half):
             cols = slice(R // 2 * half, R // 2 * (half + 1))
@@ -253,18 +256,16 @@ def tile_list_tabts_silu_kernel(tc, tab_words, tab_scales, w4_words, w4_scales, 
                 nc.sync.dma_start(out[ns, out_cols], result[:, cs])
 
         gather_ts(0, after_ts, 4096)
-        cast_down(0, 0, nc.scalar.copy)
-        cast_down(0, 1, nc.scalar.copy)
+        cast_down(0, 0, [nc.scalar.copy])
+        cast_down(0, 1, [nc.scalar.copy, nc.vector.tensor_copy])
         quantize_down(0, 0)
-        gather_words(0, [0, P, 2 * P, BANK], after_ts, 0)
         quantize_down(0, 1)
+        gather_words(0, [0, P, 2 * P, BANK], after_ts, 0)
         gather_words(0, [BANK, S], after_down[0], 0)
-        for jb in range(BANK // P):
-            h_passes(jb, 0, 0, 2)
         for jb in range(S // P):
-            h_passes(jb, 0, 2 if jb < BANK // P else 0, PACK)
-        cast_down(1, 0, nc.scalar.copy)
-        cast_down(1, 1, nc.vector.tensor_copy)
+            h_passes(jb, 0, 0, PACK)
+        cast_down(1, 0, [nc.scalar.copy])
+        cast_down(1, 1, [nc.vector.tensor_copy])
         quantize_down(1, 0)
         quantize_down(1, 1)
         gather_words(1, [0, P, 3 * P, 5 * P, 7 * P, S], after_down[0], 2048)

@@ -25,7 +25,6 @@ BANK = 512
 UP_HALF = M // 2
 PLANE_SHIFT = 16
 TILES = (M // P) * (S // BANK)
-WAIT_LEAD = 4
 UP_FIRST = M // 4
 LEAD = 2
 UP1_AFTER = 5
@@ -120,8 +119,8 @@ def tile_list_tabts_silu_kernel(tc, tab_words, tab_scales, w4_words, w4_scales, 
 
         got_ts = []
 
-        def gather_ts(jh, pool, offset):
-            got_ts.append(pool.tile([P, BANK], F32, name=f"got_ts{jh}", offset=offset, align_bytes=256))
+        def gather_ts(jh, tag):
+            got_ts.append(keep.tile([P, BANK], F32, name=f"got_ts{jh}", tag=tag, align_bytes=256))
             nc.vector.tensor_copy(got_ts[jh][:], ts_all[:].indirect(offsets[:, BANK // 16 * jh : BANK // 16 * (jh + 1)]))
 
         got_words = {}
@@ -180,7 +179,7 @@ def tile_list_tabts_silu_kernel(tc, tab_words, tab_scales, w4_words, w4_scales, 
                     stop=(a == 1 and t == PACK - 1),
                 )
 
-        order = [(jh, n0 + n) for n0 in range(0, M // P, 2) for jh in range(S // BANK) for n in range(2)]
+        order = [(jh, n0 + n) for n0 in (0, UP_HALF // P) for jh in range(S // BANK) for n in range(UP_HALF // P)]
         y_banks = {}
 
         def w4_pass(i, a):
@@ -255,7 +254,7 @@ def tile_list_tabts_silu_kernel(tc, tab_words, tab_scales, w4_words, w4_scales, 
                 nc.scalar.activation(result[:, cs], scaled[:, cs], SILU, bias=b_cols[:, n : n + 1])
                 nc.sync.dma_start(out[ns, out_cols], result[:, cs])
 
-        gather_ts(0, after_ts, 4096)
+        gather_ts(0, "got_ts0")
         cast_down(0, 0, [nc.scalar.copy])
         cast_down(0, 1, [nc.scalar.copy, nc.vector.tensor_copy])
         quantize_down(0, 0)
@@ -279,17 +278,18 @@ def tile_list_tabts_silu_kernel(tc, tab_words, tab_scales, w4_words, w4_scales, 
         quantize_h(0, BANK // 2)
         quantize_up(0, up_bf0[:], keep.tile([P, UP_FIRST], U32, name="up_codes0", align_bytes=256))
         quantize_h(BANK // 2, BANK)
-        gather_ts(1, after_h0, 0)
         up_bf1 = after_h0.tile([P, UP_FIRST, PACK], BF16, name="up_bf1", offset=2048, align_bytes=256)
-        nc.scalar.copy(up_bf1[:].rearrange("p (c e) i -> p c i e", e=4), up_raw[1][:].rearrange("p i (c e) -> p c i e", e=4))
+        nc.vector.tensor_copy(up_bf1[:].rearrange("p (c e) i -> p c i e", e=4), up_raw[1][:].rearrange("p i (c e) -> p c i e", e=4))
         for i in range(TILES):
-            last = i + (WAIT_LEAD if i == 2 else min(LEAD, (TILES - 1 - i) // 3))
+            last = i + min(LEAD, (TILES - 1 - i) // 3)
             while len(y_banks) <= last:
                 started = len(y_banks)
                 w4_pass(started, 0)
                 w4_pass(started, 1)
             finish(i)
             if i == 0:
+                quantize_up(UP_FIRST, up_bf1[:], keep.tile([P, UP_FIRST], U32, name="up_codes1", align_bytes=256))
+            if i == 1:
                 h_codes.append(keep.tile([P, BANK], U32, name="h_codes1", align_bytes=256))
                 quantize_h(BANK, S)
                 up_bf2 = keep.tile([P, UP_HALF, PACK], BF16, name="up_bf2", tag="h_bf1", align_bytes=256)
@@ -297,8 +297,8 @@ def tile_list_tabts_silu_kernel(tc, tab_words, tab_scales, w4_words, w4_scales, 
                     nc.gpsimd.tensor_scalar(
                         up_bf2[:, c0 : c0 + P, :], up_raw[2][:, :, c0 : c0 + P].rearrange("p i n -> p n i"), 1.0, 0.0, MULT, ADD
                     )
-            if i == 1:
-                quantize_up(UP_FIRST, up_bf1[:], keep.tile([P, UP_FIRST], U32, name="up_codes1", align_bytes=256))
+            if i == 2:
+                gather_ts(1, "scaled0")
             if i == UP1_AFTER:
                 codes = keep.tile([P, UP_HALF], U32, name="up_codes2", tag=f"scaled{i - 2}", align_bytes=256)
                 quantize_up(UP_HALF, up_bf2[:], codes)

@@ -27,7 +27,6 @@ PLANE_SHIFT = 16
 TILES = (M // P) * (S // BANK)
 UP_FIRST = M // 4
 LEAD = 2
-UP1_AFTER = 5
 
 
 def tile_list_tabts_silu_kernel(tc, tab_words, tab_scales, w4_words, w4_scales, down, up, ts, b, offs, out):
@@ -179,7 +178,8 @@ def tile_list_tabts_silu_kernel(tc, tab_words, tab_scales, w4_words, w4_scales, 
                     stop=(a == 1 and t == PACK - 1),
                 )
 
-        order = [(jh, n0 + n) for n0 in (0, UP_HALF // P) for jh in range(S // BANK) for n in range(UP_HALF // P)]
+        order = [(jh, n) for jh in range(S // BANK) for n in range(UP_HALF // P)]
+        order = order + [(jh, n) for n in range(UP_HALF // P, M // P) for jh in range(S // BANK)]
         y_banks = {}
 
         def w4_pass(i, a):
@@ -292,13 +292,19 @@ def tile_list_tabts_silu_kernel(tc, tab_words, tab_scales, w4_words, w4_scales, 
             if i == 1:
                 h_codes.append(keep.tile([P, BANK], U32, name="h_codes1", align_bytes=256))
                 quantize_h(BANK, S)
-                up_bf2 = keep.tile([P, UP_HALF, PACK], BF16, name="up_bf2", tag="h_bf1", align_bytes=256)
-                for c0 in range(0, UP_HALF, P):
-                    nc.gpsimd.tensor_scalar(
-                        up_bf2[:, c0 : c0 + P, :], up_raw[2][:, :, c0 : c0 + P].rearrange("p i n -> p n i"), 1.0, 0.0, MULT, ADD
-                    )
+                up_bf2 = keep.tile([P, UP_FIRST, PACK], BF16, name="up_bf2", tag="scaled1", align_bytes=256)
+                nc.scalar.copy(
+                    up_bf2[:].rearrange("p (c e) i -> p c i e", e=4), up_raw[2][:, :, 0:UP_FIRST].rearrange("p i (c e) -> p c i e", e=4)
+                )
             if i == 2:
                 gather_ts(1, "scaled0")
-            if i == UP1_AFTER:
-                codes = keep.tile([P, UP_HALF], U32, name="up_codes2", tag=f"scaled{i - 2}", align_bytes=256)
+            if i == 3:
+                codes = keep.tile([P, UP_FIRST], U32, name="up_codes2", align_bytes=256)
                 quantize_up(UP_HALF, up_bf2[:], codes)
+                up_bf3 = keep.tile([P, UP_FIRST, PACK], BF16, name="up_bf3", tag="scaled1", align_bytes=256)
+                for c0 in range(0, UP_FIRST, P):
+                    cols = slice(UP_FIRST + c0, UP_FIRST + c0 + P)
+                    nc.gpsimd.tensor_scalar(up_bf3[:, c0 : c0 + P, :], up_raw[2][:, :, cols].rearrange("p i n -> p n i"), 1.0, 0.0, MULT, ADD)
+            if i == 9:
+                codes = keep.tile([P, UP_FIRST], U32, name="up_codes3", tag="scaled7", align_bytes=256)
+                quantize_up(UP_HALF + UP_FIRST, up_bf3[:], codes)

@@ -26,6 +26,7 @@ UP_HALF = M // 2
 PLANE_SHIFT = 16
 TILES = (M // P) * (S // BANK)
 UP_FIRST = M // 4
+SCALAR_M = 48
 LEAD = 2
 
 
@@ -96,10 +97,10 @@ def tile_list_tabts_silu_kernel(tc, tab_words, tab_scales, w4_words, w4_scales, 
         load_down(1)
         load_words(1)
         nc.sync.dma_start(got_plane1[0 : P - PLANE_SHIFT, :], got_planes[PLANE_SHIFT:P, :].bitcast(I32))
-        load_up(0)
         for r in range(4):
             nc.sync.dma_start(w4_planes[r:P:32, :, :], w4_scales[:, r:16:4, :].rearrange("a q n -> q a n").bitcast(I32))
         load_w4(0)
+        load_up(0)
         load_up(1)
         load_up(2)
         load_w4(1)
@@ -143,15 +144,13 @@ def tile_list_tabts_silu_kernel(tc, tab_words, tab_scales, w4_words, w4_scales, 
         down_codes = keep.tile([P, 2, R], U32, name="down_codes", align_bytes=256)
         down_planes = keep.tile([P, 2, R], U8, name="down_planes", align_bytes=256)
 
-        def cast_down(a, half, copies):
-            shape = [P, PACK // 2, P, PACK]
-            pool, offset = (after_ts, 0) if a == 0 else (after_down[0], 4096)
-            down_bf[a, half] = pool.tile(shape, BF16, name=f"down_bf{a}{half}", offset=offset + 2048 * half, align_bytes=256)
+        def cast_down(a, half, m0, m1, copy):
+            if (a, half) not in down_bf:
+                shape = [P, PACK // 2, P, PACK]
+                pool, offset = (after_ts, 0) if a == 0 else (after_down[0], 4096)
+                down_bf[a, half] = pool.tile(shape, BF16, name=f"down_bf{a}{half}", offset=offset + 2048 * half, align_bytes=256)
             raw = down_raw[a][:].rearrange("p i (m t) -> p m i t", t=PACK)
-            share = P // len(copies)
-            for k, copy in enumerate(copies):
-                ms = slice(share * k, share * (k + 1))
-                copy(down_bf[a, half][:, :, ms, :].rearrange("p t m i -> p m i t"), raw[:, ms, :, 2 * half : 2 * half + 2])
+            copy(down_bf[a, half][:, :, m0:m1, :].rearrange("p t m i -> p m i t"), raw[:, m0:m1, :, 2 * half : 2 * half + 2])
 
         def quantize_down(a, half):
             cols = slice(R // 2 * half, R // 2 * (half + 1))
@@ -255,24 +254,30 @@ def tile_list_tabts_silu_kernel(tc, tab_words, tab_scales, w4_words, w4_scales, 
                 nc.sync.dma_start(out[ns, out_cols], result[:, cs])
 
         gather_ts(0, "got_ts0")
-        cast_down(0, 0, [nc.scalar.copy])
-        cast_down(0, 1, [nc.scalar.copy, nc.vector.tensor_copy])
+        cast_down(0, 0, 0, P, nc.scalar.copy)
+        cast_down(0, 1, 0, P // 2, nc.scalar.copy)
+        cast_down(0, 1, P // 2, P, nc.vector.tensor_copy)
         quantize_down(0, 0)
         quantize_down(0, 1)
         gather_words(0, [0, P, 2 * P, BANK], after_ts, 0)
         gather_words(0, [BANK, S], after_down[0], 0)
         for jb in range(S // P):
             h_passes(jb, 0, 0, PACK)
-        cast_down(1, 0, [nc.scalar.copy])
-        cast_down(1, 1, [nc.vector.tensor_copy])
-        quantize_down(1, 0)
+        cast_down(1, 1, 0, SCALAR_M, nc.scalar.copy)
+        cast_down(1, 0, 0, P, nc.scalar.copy)
+        cast_down(1, 1, SCALAR_M, P, nc.vector.tensor_copy)
         quantize_down(1, 1)
-        gather_words(1, [0, P, 3 * P, 5 * P, 7 * P, S], after_down[0], 2048)
+        quantize_down(1, 0)
+        gather_words(1, [0, P, 3 * P, 5 * P, 7 * P, S], after_down[1], 0)
         for jb in range(S // P):
             h_passes(jb, 1, 0, PACK)
             empty_h(jb)
+            if jb in (3, 5):
+                started = len(y_banks)
+                w4_pass(started, 0)
+                w4_pass(started, 1)
 
-        up_bf0 = after_down[0].tile([P, UP_FIRST, PACK], BF16, name="up_bf0", offset=7168, align_bytes=256)
+        up_bf0 = after_down[1].tile([P, UP_FIRST, PACK], BF16, name="up_bf0", offset=4096, align_bytes=256)
         nc.vector.tensor_copy(up_bf0[:].rearrange("p (c e) i -> p c i e", e=4), up_raw[0][:].rearrange("p i (c e) -> p c i e", e=4))
         h_codes.append(keep.tile([P, BANK], U32, name="h_codes0", align_bytes=256))
         quantize_h(0, BANK // 2)

@@ -177,7 +177,7 @@ def tile_list_tabts_silu_kernel(tc, tab_words, tab_scales, w4_words, w4_scales, 
                     stop=(a == 1 and t == PACK - 1),
                 )
 
-        order = [(jh, n) for jh in range(S // BANK) for n in range(UP_HALF // P)]
+        order = [(jh, n0 + n) for n0 in (0, 2) for jh in range(S // BANK) for n in range(2)]
         order = order + [(jh, n) for n in range(UP_HALF // P, M // P) for jh in range(S // BANK)]
         y_banks = {}
 
@@ -283,33 +283,34 @@ def tile_list_tabts_silu_kernel(tc, tab_words, tab_scales, w4_words, w4_scales, 
         quantize_h(0, BANK // 2)
         quantize_up(0, up_bf0[:], keep.tile([P, UP_FIRST], U32, name="up_codes0", align_bytes=256))
         quantize_h(BANK // 2, BANK)
-        up_bf1 = after_h0.tile([P, UP_FIRST, PACK], BF16, name="up_bf1", offset=2048, align_bytes=256)
-        nc.vector.tensor_copy(up_bf1[:].rearrange("p (c e) i -> p c i e", e=4), up_raw[1][:].rearrange("p i (c e) -> p c i e", e=4))
+        got_ts.append(after_h0.tile([P, BANK], F32, name="got_ts1", offset=2048, align_bytes=256))
+        nc.vector.tensor_copy(got_ts[1][:], ts_all[:].indirect(offsets[:, BANK // 16 : S // 16]))
+        h_codes.append(keep.tile([P, BANK], U32, name="h_codes1", align_bytes=256))
+        quantize_h(BANK, BANK + BANK // 2)
+        up_bf1 = after_h0.tile([P, UP_FIRST, PACK], BF16, name="up_bf1", offset=0, align_bytes=256)
+        nc.scalar.copy(up_bf1[:].rearrange("p (c e) i -> p c i e", e=4), up_raw[1][:].rearrange("p i (c e) -> p c i e", e=4))
+
+        def cast_up_late(q):
+            rounded = after_h0.tile([P, UP_FIRST, PACK], BF16, name=f"up_bf{q}", offset=0, align_bytes=256)
+            for c0 in range(0, UP_FIRST, P):
+                cols = slice(UP_FIRST * (q - 2) + c0, UP_FIRST * (q - 2) + c0 + P)
+                nc.gpsimd.tensor_scalar(rounded[:, c0 : c0 + P, :], up_raw[2][:, :, cols].rearrange("p i n -> p n i"), 1.0, 0.0, MULT, ADD)
+            return rounded
+
         for i in range(TILES):
-            last = i + min(LEAD, (TILES - 1 - i) // 3)
+            last = LEAD if i < 2 else max(5, i + min(LEAD, (TILES - i) // 6))
             while len(y_banks) <= last:
                 started = len(y_banks)
                 w4_pass(started, 0)
                 w4_pass(started, 1)
             finish(i)
             if i == 0:
-                quantize_up(UP_FIRST, up_bf1[:], keep.tile([P, UP_FIRST], U32, name="up_codes1", align_bytes=256))
+                quantize_h(BANK + BANK // 2, S)
             if i == 1:
-                h_codes.append(keep.tile([P, BANK], U32, name="h_codes1", align_bytes=256))
-                quantize_h(BANK, S)
-                up_bf2 = keep.tile([P, UP_FIRST, PACK], BF16, name="up_bf2", tag="scaled1", align_bytes=256)
-                nc.scalar.copy(
-                    up_bf2[:].rearrange("p (c e) i -> p c i e", e=4), up_raw[2][:, :, 0:UP_FIRST].rearrange("p i (c e) -> p c i e", e=4)
-                )
-            if i == 2:
-                gather_ts(1, "scaled0")
-            if i == 3:
-                codes = keep.tile([P, UP_FIRST], U32, name="up_codes2", align_bytes=256)
-                quantize_up(UP_HALF, up_bf2[:], codes)
-                up_bf3 = keep.tile([P, UP_FIRST, PACK], BF16, name="up_bf3", tag="scaled1", align_bytes=256)
-                for c0 in range(0, UP_FIRST, P):
-                    cols = slice(UP_FIRST + c0, UP_FIRST + c0 + P)
-                    nc.gpsimd.tensor_scalar(up_bf3[:, c0 : c0 + P, :], up_raw[2][:, :, cols].rearrange("p i n -> p n i"), 1.0, 0.0, MULT, ADD)
+                quantize_up(UP_FIRST, up_bf1[:], keep.tile([P, UP_FIRST], U32, name="up_codes1", align_bytes=256))
+                late = cast_up_late(2)
+            if i == 5:
+                quantize_up(UP_HALF, late[:], keep.tile([P, UP_FIRST], U32, name="up_codes2", tag="scaled3", align_bytes=256))
+                late = cast_up_late(3)
             if i == 9:
-                codes = keep.tile([P, UP_FIRST], U32, name="up_codes3", tag="scaled7", align_bytes=256)
-                quantize_up(UP_HALF + UP_FIRST, up_bf3[:], codes)
+                quantize_up(UP_HALF + UP_FIRST, late[:], keep.tile([P, UP_FIRST], U32, name="up_codes3", tag="scaled7", align_bytes=256))

@@ -26,7 +26,6 @@ UP_HALF = M // 2
 PLANE_SHIFT = 16
 TILES = (M // P) * (S // BANK)
 UP_FIRST = M // 4
-SCALAR_M = 48
 LEAD = 2
 
 
@@ -206,7 +205,9 @@ def tile_list_tabts_silu_kernel(tc, tab_words, tab_scales, w4_words, w4_scales, 
 
         def empty_h(jb):
             jh, c0 = divmod(P * jb, BANK)
-            nc.scalar.copy(h_bf[jh][:, c0 : c0 + P, :], h_banks[jb][:].rearrange("p t j -> p j t"))
+            nc.scalar.copy(
+                h_bf[jh][:, c0 : c0 + P, :].rearrange("p (c e) t -> p c t e", e=2), h_banks[jb][:].rearrange("p t (c e) -> p c t e", e=2)
+            )
 
         def quantize_h(j0, j1):
             jh, c0 = divmod(j0, BANK)
@@ -263,12 +264,11 @@ def tile_list_tabts_silu_kernel(tc, tab_words, tab_scales, w4_words, w4_scales, 
         gather_words(0, [BANK, S], after_down[0], 0)
         for jb in range(S // P):
             h_passes(jb, 0, 0, PACK)
-        cast_down(1, 1, 0, SCALAR_M, nc.scalar.copy)
         cast_down(1, 0, 0, P, nc.scalar.copy)
-        cast_down(1, 1, SCALAR_M, P, nc.vector.tensor_copy)
-        quantize_down(1, 1)
+        cast_down(1, 1, 0, P, nc.vector.tensor_copy)
         quantize_down(1, 0)
-        gather_words(1, [0, P, 3 * P, 5 * P, 7 * P, S], after_down[1], 0)
+        quantize_down(1, 1)
+        gather_words(1, [0, P, 3 * P, 5 * P, 7 * P, S], after_down[0], 2048)
         for jb in range(S // P):
             h_passes(jb, 1, 0, PACK)
             empty_h(jb)
@@ -277,7 +277,7 @@ def tile_list_tabts_silu_kernel(tc, tab_words, tab_scales, w4_words, w4_scales, 
                 w4_pass(started, 0)
                 w4_pass(started, 1)
 
-        up_bf0 = after_down[1].tile([P, UP_FIRST, PACK], BF16, name="up_bf0", offset=4096, align_bytes=256)
+        up_bf0 = after_down[0].tile([P, UP_FIRST, PACK], BF16, name="up_bf0", offset=7168, align_bytes=256)
         nc.vector.tensor_copy(up_bf0[:].rearrange("p (c e) i -> p c i e", e=4), up_raw[0][:].rearrange("p i (c e) -> p c i e", e=4))
         h_codes.append(keep.tile([P, BANK], U32, name="h_codes0", align_bytes=256))
         quantize_h(0, BANK // 2)

@@ -178,14 +178,16 @@ def tile_list_tabts_silu_kernel(tc, tab_words, tab_scales, w4_words, w4_scales, 
 
         order = [(jh, n0 + n) for n0 in (0, 2) for jh in range(S // BANK) for n in range(2)]
         order = order + [(jh, n) for n in range(UP_HALF // P, M // P) for jh in range(S // BANK)]
+        pieces = [(n, BANK * jh, BANK) for jh, n in order[:-1]]
+        pieces = pieces + [(M // P - 1, j0, BANK // 2) for j0 in (BANK, BANK + BANK // 2)]
         y_banks = {}
 
         def w4_pass(i, a):
-            jh, n = order[i]
+            n, j0, width = pieces[i]
             if a == 0:
-                y_banks[i] = bank(i % 8, [P, BANK])
+                y_banks[i] = bank(i % 8, [P, width])
             u, c = divmod(P * n, UP_HALF)
-            codes, plane = tab_operand(a, BANK * jh, BANK * jh + BANK)
+            codes, plane = tab_operand(a, j0, j0 + width)
             nc.tensor.matmul_mx(
                 out=y_banks[i][:],
                 lhsT=w4_codes[u][:, a, 2 * c : 2 * (c + P)].bitcast(FP4X4),
@@ -231,26 +233,27 @@ def tile_list_tabts_silu_kernel(tc, tab_words, tab_scales, w4_words, w4_scales, 
                 up_codes[(n0 + c) // P] = codes[:, c : c + P]
 
         def finish(i):
-            jh, n = order[i]
+            n, j0, width = pieces[i]
+            jh, h0 = divmod(j0, BANK)
             acc = y_banks[i]
-            js = slice(BANK * jh, BANK * jh + BANK)
+            js = slice(j0, j0 + width)
             ns = slice(P * n, P * n + P)
             nc.tensor.matmul_mx(
                 out=acc[:],
                 lhsT=up_codes[n].bitcast(FP8X4),
                 lhsT_scale=up_plane[:, ns],
-                rhs=h_codes[jh][:].bitcast(FP8X4),
+                rhs=h_codes[jh][:, h0 : h0 + width].bitcast(FP8X4),
                 rhs_scale=h_plane[:, js],
                 start=False,
                 stop=True,
             )
             scaled = keep.tile([P, BANK], F32, name=f"scaled{i}", tag=f"scaled{i}", align_bytes=256)
             result = keep.tile([P, BANK], F32, name=f"result{i}")
-            step = BANK // 2 if i == TILES - 1 else BANK
-            for c0 in range(0, BANK, step):
+            step = BANK // 2 if i >= TILES - 2 else BANK
+            for c0 in range(0, width, step):
                 cs = slice(c0, c0 + step)
-                out_cols = slice(BANK * jh + c0, BANK * jh + c0 + step)
-                nc.vector.tensor_tensor(scaled[:, cs], acc[:, cs], got_ts[jh][:, cs], MULT)
+                out_cols = slice(j0 + c0, j0 + c0 + step)
+                nc.vector.tensor_tensor(scaled[:, cs], acc[:, cs], got_ts[jh][:, h0 + c0 : h0 + c0 + step], MULT)
                 nc.scalar.activation(result[:, cs], scaled[:, cs], SILU, bias=b_cols[:, n : n + 1])
                 nc.sync.dma_start(out[ns, out_cols], result[:, cs])
 
@@ -297,7 +300,7 @@ def tile_list_tabts_silu_kernel(tc, tab_words, tab_scales, w4_words, w4_scales, 
                 nc.gpsimd.tensor_scalar(rounded[:, c0 : c0 + P, :], up_raw[2][:, :, cols].rearrange("p i n -> p n i"), 1.0, 0.0, MULT, ADD)
             return rounded
 
-        for i in range(TILES):
+        for i in range(len(pieces)):
             last = LEAD if i < 2 else max(5, i + min(LEAD, (TILES - i) // 6))
             while len(y_banks) <= last:
                 started = len(y_banks)

@@ -178,8 +178,9 @@ def tile_list_tabts_silu_kernel(tc, tab_words, tab_scales, w4_words, w4_scales, 
 
         order = [(jh, n0 + n) for n0 in (0, 2) for jh in range(S // BANK) for n in range(2)]
         order = order + [(jh, n) for n in range(UP_HALF // P, M // P) for jh in range(S // BANK)]
-        pieces = [(n, BANK * jh, BANK) for jh, n in order[:-1]]
-        pieces = pieces + [(M // P - 1, j0, BANK // 2) for j0 in (BANK, BANK + BANK // 2)]
+        pieces = [(n, BANK * jh, BANK) for jh, n in order[:-2]]
+        pieces = pieces + [(M // P - 1, j0, BANK // 2) for j0 in range(0, S - BANK // 2, BANK // 2)]
+        pieces = pieces + [(M // P - 1, S - 2 * P, P), (M // P - 1, S - P, P)]
         y_banks = {}
 
         def w4_pass(i, a):
@@ -249,7 +250,7 @@ def tile_list_tabts_silu_kernel(tc, tab_words, tab_scales, w4_words, w4_scales, 
             )
             scaled = keep.tile([P, BANK], F32, name=f"scaled{i}", tag=f"scaled{i}", align_bytes=256)
             result = keep.tile([P, BANK], F32, name=f"result{i}")
-            step = BANK // 2 if i >= TILES - 2 else BANK
+            step = min(width, BANK // 2) if i >= TILES - 3 else BANK
             for c0 in range(0, width, step):
                 cs = slice(c0, c0 + step)
                 out_cols = slice(j0 + c0, j0 + c0 + step)
@@ -301,7 +302,7 @@ def tile_list_tabts_silu_kernel(tc, tab_words, tab_scales, w4_words, w4_scales, 
             return rounded
 
         for i in range(len(pieces)):
-            last = LEAD if i < 2 else max(5, i + min(LEAD, (TILES - i) // 6))
+            last = LEAD if i < 2 else max(5, i + min(LEAD, max(0, TILES - 4 - i) // 4))
             while len(y_banks) <= last:
                 started = len(y_banks)
                 w4_pass(started, 0)
@@ -315,5 +316,5 @@ def tile_list_tabts_silu_kernel(tc, tab_words, tab_scales, w4_words, w4_scales, 
             if i == 5:
                 quantize_up(UP_HALF, late[:], keep.tile([P, UP_FIRST], U32, name="up_codes2", tag="scaled3", align_bytes=256))
                 late = cast_up_late(3)
-            if i == 9:
+            if i == 10:
                 quantize_up(UP_HALF + UP_FIRST, late[:], keep.tile([P, UP_FIRST], U32, name="up_codes3", tag="scaled7", align_bytes=256))

@@ -43,15 +43,22 @@ def tile_list_tabts_silu_kernel(tc, tab_words, tab_scales, w4_words, w4_scales, 
             return psum.tile(shape, F32, name=f"bank{k}", tag=f"bank{k}")
 
         offsets = keep.tile([P, S // 16], U16, name="offsets")
-        nc.sync.dma_start(offsets[:], offs)
+        down_raw = [after_down[a].tile([P, PACK, R], F32, name=f"down_raw{a}", offset=0, align_bytes=256) for a in range(2)]
+
+        def load_down(queue, a, i0, i1):
+            rows = down[K_PASS * a : K_PASS * (a + 1), :].rearrange("(p i) r -> p i r", i=PACK)
+            queue.dma_start(down_raw[a][:, i0:i1, :], rows[:, i0:i1, :])
+
         ts_cols = after_ts.tile([P, T // P], F32, name="ts_cols", offset=2048 - 32)
         nc.sync.dma_start(ts_cols[:], ts[0].rearrange("(c m) -> c m", c=P))
+        load_down(nc.sync, 0, 0, 1)
+        nc.sync.dma_start(offsets[:], offs)
 
-        tab_planes = keep.tile([P, T // 4], I32, name="tab_planes", align_bytes=256)
+        tab_planes = keep.tile([P, T // 4], I32, name="tab_planes", tag="tab_planes", align_bytes=256)
         w4_planes = keep.tile([P, 2, M // 4], I32, name="w4_planes", align_bytes=256)
         b_rows = keep.tile([P, P], F32, name="b_rows")
         nc.gpsimd.memset(tab_planes[:], 0)
-        nc.vector.memset(b_rows[0:64, :], 0.0)
+        nc.gpsimd.memset(b_rows[0:64, :], 0.0)
         nc.vector.memset(w4_planes[:], 0)
 
         for r in range(4):
@@ -59,14 +66,12 @@ def tile_list_tabts_silu_kernel(tc, tab_words, tab_scales, w4_words, w4_scales, 
 
         identity = keep.tile([P, P], F32, name="identity")
         make_identity(nc, identity[:])
-        nc.scalar.dma_start(b_rows[0 : M // P, :], b.rearrange("(c p) -> c p", p=P))
         nc.scalar.activation(b_rows[64:P, :], identity[64:P, :], SILU, scale=0.0)
 
         words = [
             keep.tile([P, T], I32, name="words0", align_bytes=256),
             after_words1.tile([P, T], I32, name="words1", offset=0, align_bytes=256),
         ]
-        down_raw = [after_down[a].tile([P, PACK, R], F32, name=f"down_raw{a}", offset=0, align_bytes=256) for a in range(2)]
         up_cuts = [0, UP_FIRST, UP_HALF, M]
         up_raw = [
             keep.tile([P, PACK, up_cuts[u + 1] - up_cuts[u]], F32, name=f"up_raw{u}", tag=f"up_raw{u}", align_bytes=256) for u in range(3)
@@ -75,9 +80,6 @@ def tile_list_tabts_silu_kernel(tc, tab_words, tab_scales, w4_words, w4_scales, 
 
         def load_words(a):
             nc.sync.dma_start(words[a][:], tab_words[a].rearrange("p t i -> p (t i)").bitcast(I32))
-
-        def load_down(a):
-            nc.sync.dma_start(down_raw[a][:], down[K_PASS * a : K_PASS * (a + 1), :].rearrange("(p i) r -> p i r", i=PACK))
 
         def load_up(u):
             nc.sync.dma_start(up_raw[u][:], up[:, up_cuts[u] : up_cuts[u + 1]].rearrange("(p i) n -> p i n", i=PACK))
@@ -91,9 +93,10 @@ def tile_list_tabts_silu_kernel(tc, tab_words, tab_scales, w4_words, w4_scales, 
         got_plane1 = keep.tile([P, S // 4], I32, name="got_plane1", align_bytes=256)
         nc.gpsimd.memset(got_plane1[96:P, :], 0)
 
-        load_down(0)
+        load_down(nc.sync, 0, 1, PACK)
+        nc.sync.dma_start(b_rows[0 : M // P, :], b.rearrange("(c p) -> c p", p=P))
         load_words(0)
-        load_down(1)
+        load_down(nc.sync, 1, 0, PACK)
         load_words(1)
         nc.sync.dma_start(got_plane1[0 : P - PLANE_SHIFT, :], got_planes[PLANE_SHIFT:P, :].bitcast(I32))
         for r in range(4):
@@ -113,8 +116,6 @@ def tile_list_tabts_silu_kernel(tc, tab_words, tab_scales, w4_words, w4_scales, 
             nc.scalar.copy(ts_view[:, :, m0 : m0 + 4], spread[:].rearrange("p m c -> p c m"))
         b_turned = bank(4, [P, PACK, P])
         nc.tensor.transpose(b_turned[:, 0, :], b_rows[:], identity[:])
-        b_cols = keep.tile([P, M // P], F32, name="b_cols")
-        nc.scalar.copy(b_cols[:], b_turned[:, 0, 0 : M // P])
 
         got_ts = []
 
@@ -146,8 +147,8 @@ def tile_list_tabts_silu_kernel(tc, tab_words, tab_scales, w4_words, w4_scales, 
         def cast_down(a, half, m0, m1, copy):
             if (a, half) not in down_bf:
                 shape = [P, PACK // 2, P, PACK]
-                pool, offset = (after_ts, 0) if a == 0 else (after_down[0], 4096)
-                down_bf[a, half] = pool.tile(shape, BF16, name=f"down_bf{a}{half}", offset=offset + 2048 * half, align_bytes=256)
+                pool, offset = (after_ts, 2048 * half) if a == 0 else (after_down[0], 6144 - 2048 * half)
+                down_bf[a, half] = pool.tile(shape, BF16, name=f"down_bf{a}{half}", offset=offset, align_bytes=256)
             raw = down_raw[a][:].rearrange("p i (m t) -> p m i t", t=PACK)
             copy(down_bf[a, half][:, :, m0:m1, :].rearrange("p t m i -> p m i t"), raw[:, m0:m1, :, 2 * half : 2 * half + 2])
 
@@ -178,9 +179,8 @@ def tile_list_tabts_silu_kernel(tc, tab_words, tab_scales, w4_words, w4_scales, 
 
         order = [(jh, n0 + n) for n0 in (0, 2) for jh in range(S // BANK) for n in range(2)]
         order = order + [(jh, n) for n in range(UP_HALF // P, M // P) for jh in range(S // BANK)]
-        pieces = [(n, BANK * jh, BANK) for jh, n in order[:-2]]
-        pieces = pieces + [(M // P - 1, j0, BANK // 2) for j0 in range(0, S - BANK // 2, BANK // 2)]
-        pieces = pieces + [(M // P - 1, S - 2 * P, P), (M // P - 1, S - P, P)]
+        pieces = [(n, BANK * jh, BANK) for jh, n in order[:-1]]
+        pieces = pieces + [(M // P - 1, j0, BANK // 2) for j0 in (BANK, BANK + BANK // 2)]
         y_banks = {}
 
         def w4_pass(i, a):
@@ -199,17 +199,14 @@ def tile_list_tabts_silu_kernel(tc, tab_words, tab_scales, w4_words, w4_scales, 
                 stop=False,
             )
 
-        h_bf = [
-            after_h0.tile([P, BANK, PACK], BF16, name="h_bf0", offset=0, align_bytes=256),
-            keep.tile([P, BANK, PACK], BF16, name="h_bf1", tag="h_bf1", align_bytes=256),
-        ]
+        h_bf = [after_h0.tile([P, 2 * P, PACK], BF16, name=f"h_bf{q}", offset=2048 * q, align_bytes=256) for q in range(4)]
         h_codes = []
         h_plane = keep.tile([P, S], U8, name="h_plane", align_bytes=256)
 
         def empty_h(jb):
-            jh, c0 = divmod(P * jb, BANK)
+            q, c0 = divmod(P * jb, 2 * P)
             nc.scalar.copy(
-                h_bf[jh][:, c0 : c0 + P, :].rearrange("p (c e) t -> p c t e", e=2), h_banks[jb][:].rearrange("p t (c e) -> p c t e", e=2)
+                h_bf[q][:, c0 : c0 + P, :].rearrange("p (c e) t -> p c t e", e=2), h_banks[jb][:].rearrange("p t (c e) -> p c t e", e=2)
             )
 
         def quantize_h(j0, j1):
@@ -217,7 +214,7 @@ def tile_list_tabts_silu_kernel(tc, tab_words, tab_scales, w4_words, w4_scales, 
             nc.vector.quantize_mx(
                 out=h_codes[jh][:, c0 : c0 + j1 - j0].bitcast(FP8X4),
                 scales=h_plane[:, j0:j1],
-                in_=h_bf[jh][:, c0 : c0 + j1 - j0, :].rearrange("p j t -> p (j t)"),
+                in_=h_bf[j0 // (2 * P)][:].rearrange("p j t -> p (j t)"),
             )
 
         up_codes = {}
@@ -250,7 +247,7 @@ def tile_list_tabts_silu_kernel(tc, tab_words, tab_scales, w4_words, w4_scales, 
             )
             scaled = keep.tile([P, BANK], F32, name=f"scaled{i}", tag=f"scaled{i}", align_bytes=256)
             result = keep.tile([P, BANK], F32, name=f"result{i}")
-            step = min(width, BANK // 2) if i >= TILES - 3 else BANK
+            step = BANK // 2 if i >= TILES - 2 else BANK
             for c0 in range(0, width, step):
                 cs = slice(c0, c0 + step)
                 out_cols = slice(j0 + c0, j0 + c0 + step)
@@ -258,21 +255,22 @@ def tile_list_tabts_silu_kernel(tc, tab_words, tab_scales, w4_words, w4_scales, 
                 nc.scalar.activation(result[:, cs], scaled[:, cs], SILU, bias=b_cols[:, n : n + 1])
                 nc.sync.dma_start(out[ns, out_cols], result[:, cs])
 
-        gather_ts(0, "got_ts0")
+        gather_ts(0, "tab_planes")
         cast_down(0, 0, 0, P, nc.scalar.copy)
         cast_down(0, 1, 0, P // 2, nc.scalar.copy)
         cast_down(0, 1, P // 2, P, nc.vector.tensor_copy)
+        b_cols = keep.tile([P, M // P], F32, name="b_cols")
+        nc.scalar.copy(b_cols[:], b_turned[:, 0, 0 : M // P])
         quantize_down(0, 0)
         quantize_down(0, 1)
-        gather_words(0, [0, P, 2 * P, BANK], after_ts, 0)
-        gather_words(0, [BANK, S], after_down[0], 0)
+        gather_words(0, [0, P, 3 * P, S], after_down[0], 0)
         for jb in range(S // P):
             h_passes(jb, 0, 0, PACK)
         cast_down(1, 0, 0, P, nc.scalar.copy)
         cast_down(1, 1, 0, P, nc.vector.tensor_copy)
         quantize_down(1, 0)
         quantize_down(1, 1)
-        gather_words(1, [0, P, 3 * P, 5 * P, 7 * P, S], after_down[0], 2048)
+        gather_words(1, [0, P, 3 * P, 5 * P, S], after_down[0], 6144)
         for jb in range(S // P):
             h_passes(jb, 1, 0, PACK)
             empty_h(jb)
@@ -281,9 +279,9 @@ def tile_list_tabts_silu_kernel(tc, tab_words, tab_scales, w4_words, w4_scales, 
                 w4_pass(started, 0)
                 w4_pass(started, 1)
 
-        up_bf0 = after_down[0].tile([P, UP_FIRST, PACK], BF16, name="up_bf0", offset=7168, align_bytes=256)
+        up_bf0 = after_down[0].tile([P, UP_FIRST, PACK], BF16, name="up_bf0", offset=4096, align_bytes=256)
         nc.vector.tensor_copy(up_bf0[:].rearrange("p (c e) i -> p c i e", e=4), up_raw[0][:].rearrange("p i (c e) -> p c i e", e=4))
-        h_codes.append(keep.tile([P, BANK], U32, name="h_codes0", align_bytes=256))
+        h_codes.append(keep.tile([P, BANK], U32, name="h_codes0", tag="up_raw0", align_bytes=256))
         quantize_h(0, BANK // 2)
         quantize_up(0, up_bf0[:], keep.tile([P, UP_FIRST], U32, name="up_codes0", align_bytes=256))
         quantize_h(BANK // 2, BANK)
@@ -291,18 +289,18 @@ def tile_list_tabts_silu_kernel(tc, tab_words, tab_scales, w4_words, w4_scales, 
         nc.vector.tensor_copy(got_ts[1][:], ts_all[:].indirect(offsets[:, BANK // 16 : S // 16]))
         h_codes.append(keep.tile([P, BANK], U32, name="h_codes1", align_bytes=256))
         quantize_h(BANK, BANK + BANK // 2)
-        up_bf1 = after_h0.tile([P, UP_FIRST, PACK], BF16, name="up_bf1", offset=0, align_bytes=256)
+        up_bf1 = after_h0.tile([P, UP_FIRST, PACK], BF16, name="up_bf1", offset=4096, align_bytes=256)
         nc.scalar.copy(up_bf1[:].rearrange("p (c e) i -> p c i e", e=4), up_raw[1][:].rearrange("p i (c e) -> p c i e", e=4))
 
         def cast_up_late(q):
-            rounded = after_h0.tile([P, UP_FIRST, PACK], BF16, name=f"up_bf{q}", offset=0, align_bytes=256)
+            rounded = after_h0.tile([P, UP_FIRST, PACK], BF16, name=f"up_bf{q}", offset=4096, align_bytes=256)
             for c0 in range(0, UP_FIRST, P):
                 cols = slice(UP_FIRST * (q - 2) + c0, UP_FIRST * (q - 2) + c0 + P)
                 nc.gpsimd.tensor_scalar(rounded[:, c0 : c0 + P, :], up_raw[2][:, :, cols].rearrange("p i n -> p n i"), 1.0, 0.0, MULT, ADD)
             return rounded
 
         for i in range(len(pieces)):
-            last = LEAD if i < 2 else max(5, i + min(LEAD, max(0, TILES - 4 - i) // 4))
+            last = LEAD if i < 2 else max(5, i + min(LEAD, (TILES - i) // 6))
             while len(y_banks) <= last:
                 started = len(y_banks)
                 w4_pass(started, 0)
@@ -313,8 +311,8 @@ def tile_list_tabts_silu_kernel(tc, tab_words, tab_scales, w4_words, w4_scales, 
             if i == 1:
                 quantize_up(UP_FIRST, up_bf1[:], keep.tile([P, UP_FIRST], U32, name="up_codes1", align_bytes=256))
                 late = cast_up_late(2)
-            if i == 5:
-                quantize_up(UP_HALF, late[:], keep.tile([P, UP_FIRST], U32, name="up_codes2", tag="scaled3", align_bytes=256))
+            if i == 4:
+                quantize_up(UP_HALF, late[:], keep.tile([P, UP_FIRST], U32, name="up_codes2", tag="scaled2", align_bytes=256))
                 late = cast_up_late(3)
-            if i == 10:
+            if i == 9:
                 quantize_up(UP_HALF + UP_FIRST, late[:], keep.tile([P, UP_FIRST], U32, name="up_codes3", tag="scaled7", align_bytes=256))

from contextlib import ExitStack

import concourse.mybir as mybir
from concourse.masks import make_identity

K, M, T, S, R = 1024, 1024, 2048, 1024, 512
FLOPS = 2 * K * R * S + 2 * K * M * S + 2 * R * M * S

F32 = mybir.dt.float32
BF16 = mybir.dt.bfloat16
I32 = mybir.dt.int32
U32 = mybir.dt.uint32
U16 = mybir.dt.uint16
U8 = mybir.dt.uint8
FP8X4 = mybir.dt.float8_e4m3fn_x4
FP4X4 = mybir.dt.float4_e2m1fn_x4
MULT = mybir.AluOpType.mult
ADD = mybir.AluOpType.add
SILU = mybir.ActivationFunctionType.Silu

P = 128
PACK = 4
K_PASS = P * PACK
BANK = 512
UP_HALF = M // 2
PLANE_SHIFT = 16
TILES = (M // P) * (S // BANK)
UP_FIRST = M // 4
LEAD = 2


def tile_list_tabts_silu_kernel(tc, tab_words, tab_scales, w4_words, w4_scales, down, up, ts, b, offs, out):
    nc = tc.nc
    with ExitStack() as ctx:
        keep = ctx.enter_context(tc.tile_pool(name="keep", bufs=1))
        after_ts = ctx.enter_context(tc.tile_pool(name="after_ts", bufs=1))
        after_down = [ctx.enter_context(tc.tile_pool(name=f"after_down{a}", bufs=1)) for a in range(2)]
        after_words1 = ctx.enter_context(tc.tile_pool(name="after_words1", bufs=1))
        after_h0 = ctx.enter_context(tc.tile_pool(name="after_h0", bufs=1))
        psum = ctx.enter_context(tc.psum_pool(name="psum", bufs=1))

        def bank(k, shape):
            return psum.tile(shape, F32, name=f"bank{k}", tag=f"bank{k}")

        offsets = keep.tile([P, S // 16], U16, name="offsets")
        down_raw = [after_down[a].tile([P, PACK, R], F32, name=f"down_raw{a}", offset=0, align_bytes=256) for a in range(2)]

        def load_down(queue, a, i0, i1):
            rows = down[K_PASS * a : K_PASS * (a + 1), :].rearrange("(p i) r -> p i r", i=PACK)
            queue.dma_start(down_raw[a][:, i0:i1, :], rows[:, i0:i1, :])

        ts_cols = after_ts.tile([P, T // P], F32, name="ts_cols", offset=2048 - 32)
        nc.sync.dma_start(ts_cols[:], ts[0].rearrange("(c m) -> c m", c=P))
        load_down(nc.sync, 0, 0, 1)
        nc.sync.dma_start(offsets[:], offs)

        tab_planes = keep.tile([P, T // 4], I32, name="tab_planes", tag="tab_planes", align_bytes=256)
        w4_planes = keep.tile([P, 2, M // 4], I32, name="w4_planes", align_bytes=256)
        b_rows = keep.tile([P, P], F32, name="b_rows")
        nc.gpsimd.memset(tab_planes[:], 0)
        nc.gpsimd.memset(b_rows[0:64, :], 0.0)
        nc.vector.memset(w4_planes[:], 0)

        for r in range(4):
            nc.sync.dma_start(tab_planes[r:P:PLANE_SHIFT, :], tab_scales[:, r:16:4, :].rearrange("a q t -> q a t").bitcast(I32))

        identity = keep.tile([P, P], F32, name="identity")
        make_identity(nc, identity[:])
        nc.scalar.activation(b_rows[64:P, :], identity[64:P, :], SILU, scale=0.0)

        words = [
            keep.tile([P, T], I32, name="words0", align_bytes=256),
            after_words1.tile([P, T], I32, name="words1", offset=0, align_bytes=256),
        ]
        up_cuts = [0, UP_FIRST, UP_HALF, M]
        up_raw = [
            keep.tile([P, PACK, up_cuts[u + 1] - up_cuts[u]], F32, name=f"up_raw{u}", tag=f"up_raw{u}", align_bytes=256) for u in range(3)
        ]
        w4_codes = [keep.tile([P, 2, 2 * UP_HALF], U8, name=f"w4_codes{u}", align_bytes=256) for u in range(2)]

        def load_words(a):
            nc.sync.dma_start(words[a][:], tab_words[a].rearrange("p t i -> p (t i)").bitcast(I32))

        def load_up(u):
            nc.sync.dma_start(up_raw[u][:], up[:, up_cuts[u] : up_cuts[u + 1]].rearrange("(p i) n -> p i n", i=PACK))

        def load_w4(u):
            w4_half = w4_words[:, :, 2 * UP_HALF * u : 2 * UP_HALF * (u + 1)]
            nc.sync.dma_start(w4_codes[u][:].bitcast(I32), w4_half.rearrange("a p n -> p a n").bitcast(I32))

        got_planes = keep.tile([P, S], U8, name="got_planes", align_bytes=256)
        nc.vector.tensor_copy(got_planes[:], tab_planes[:].bitcast(U8).indirect(offsets[:]))
        got_plane1 = keep.tile([P, S // 4], I32, name="got_plane1", align_bytes=256)
        nc.gpsimd.memset(got_plane1[96:P, :], 0)

        load_down(nc.sync, 0, 1, PACK)
        nc.sync.dma_start(b_rows[0 : M // P, :], b.rearrange("(c p) -> c p", p=P))
        load_words(0)
        load_down(nc.sync, 1, 0, PACK)
        load_words(1)
        nc.sync.dma_start(got_plane1[0 : P - PLANE_SHIFT, :], got_planes[PLANE_SHIFT:P, :].bitcast(I32))
        for r in range(4):
            nc.sync.dma_start(w4_planes[r:P:32, :, :], w4_scales[:, r:16:4, :].rearrange("a q n -> q a n").bitcast(I32))
        load_w4(0)
        load_up(0)
        load_up(1)
        load_up(2)
        load_w4(1)

        ts_all = keep.tile([P, T], F32, name="ts_all", align_bytes=256)
        ts_view = ts_all[:].rearrange("p (c m) -> p c m", m=T // P)
        for m0 in range(0, T // P, 4):
            spread = bank(m0 // 4, [P, 4, P])
            for m in range(4):
                nc.tensor.transpose(spread[:, m, :], ts_cols[:, m0 + m : m0 + m + 1].to_broadcast([P, P]), identity[:])
            nc.scalar.copy(ts_view[:, :, m0 : m0 + 4], spread[:].rearrange("p m c -> p c m"))
        b_turned = bank(4, [P, PACK, P])
        nc.tensor.transpose(b_turned[:, 0, :], b_rows[:], identity[:])

        got_ts = []

        def gather_ts(jh, tag):
            got_ts.append(keep.tile([P, BANK], F32, name=f"got_ts{jh}", tag=tag, align_bytes=256))
            nc.vector.tensor_copy(got_ts[jh][:], ts_all[:].indirect(offsets[:, BANK // 16 * jh : BANK // 16 * (jh + 1)]))

        got_words = {}

        def gather_words(a, cuts, pool, offset):
            j0 = cuts[0]
            got = pool.tile([P, cuts[-1] - j0], U32, name=f"got_words{a}_{j0}", offset=offset, align_bytes=256)
            for jh in range(j0 // BANK, cuts[-1] // BANK):
                got_words[a, jh] = got[:, BANK * jh - j0 : BANK * (jh + 1) - j0]
            for c0, c1 in zip(cuts[:-1], cuts[1:]):
                nc.vector.tensor_copy(got[:, c0 - j0 : c1 - j0], words[a][:].bitcast(U32).indirect(offsets[:, c0 // 16 : c1 // 16]))

        def tab_operand(a, j0, j1):
            jh, c0 = divmod(j0, BANK)
            codes = got_words[a, jh][:, c0 : c0 + j1 - j0].bitcast(FP8X4)
            if a == 0:
                return codes, got_planes[:, j0:j1]
            return codes, got_plane1[:, j0 // 4 : j1 // 4].bitcast(U8)

        down_bf = {}
        down_codes = keep.tile([P, 2, R], U32, name="down_codes", align_bytes=256)
        down_planes = keep.tile([P, 2, R], U8, name="down_planes", align_bytes=256)

        def cast_down(a, half, m0, m1, copy):
            if (a, half) not in down_bf:
                shape = [P, PACK // 2, P, PACK]
                pool, offset = (after_ts, 2048 * half) if a == 0 else (after_down[0], 6144 - 2048 * half)
                down_bf[a, half] = pool.tile(shape, BF16, name=f"down_bf{a}{half}", offset=offset, align_bytes=256)
            raw = down_raw[a][:].rearrange("p i (m t) -> p m i t", t=PACK)
            copy(down_bf[a, half][:, :, m0:m1, :].rearrange("p t m i -> p m i t"), raw[:, m0:m1, :, 2 * half : 2 * half + 2])

        def quantize_down(a, half):
            cols = slice(R // 2 * half, R // 2 * (half + 1))
            nc.vector.quantize_mx(
                out=down_codes[:, a, cols].bitcast(FP8X4),
                scales=down_planes[:, a, cols],
                in_=down_bf[a, half][:].rearrange("p t m i -> p (t m i)"),
            )

        h_banks = {}

        def h_passes(jb, a, t0, t1):
            if jb not in h_banks:
                h_banks[jb] = bank(jb, [P, PACK, P])
            codes, plane = tab_operand(a, P * jb, P * jb + P)
            for t in range(t0, t1):
                nc.tensor.matmul_mx(
                    out=h_banks[jb][:, t, :],
                    lhsT=down_codes[:, a, P * t : P * t + P].bitcast(FP8X4),
                    lhsT_scale=down_planes[:, a, P * t : P * t + P],
                    rhs=codes,
                    rhs_scale=plane,
                    start=(a == 0 and t == 0),
                    stop=(a == 1 and t == PACK - 1),
                )

        order = [(jh, n0 + n) for n0 in (0, 2) for jh in range(S // BANK) for n in range(2)]
        order = order + [(jh, n) for n in range(UP_HALF // P, M // P) for jh in range(S // BANK)]
        pieces = [(n, BANK * jh, BANK) for jh, n in order[:-1]]
        pieces = pieces + [(M // P - 1, j0, BANK // 2) for j0 in (BANK, BANK + BANK // 2)]
        y_banks = {}

        def w4_pass(i, a):
            n, j0, width = pieces[i]
            if a == 0:
                y_banks[i] = bank(i % 8, [P, width])
            u, c = divmod(P * n, UP_HALF)
            codes, plane = tab_operand(a, j0, j0 + width)
            nc.tensor.matmul_mx(
                out=y_banks[i][:],
                lhsT=w4_codes[u][:, a, 2 * c : 2 * (c + P)].bitcast(FP4X4),
                lhsT_scale=w4_planes[:, a, P // 4 * n : P // 4 * (n + 1)].bitcast(U8),
                rhs=codes,
                rhs_scale=plane,
                start=(a == 0),
                stop=False,
            )

        h_bf = [after_h0.tile([P, 2 * P, PACK], BF16, name=f"h_bf{q}", offset=2048 * q, align_bytes=256) for q in range(4)]
        h_codes = []
        h_plane = keep.tile([P, S], U8, name="h_plane", align_bytes=256)

        def empty_h(jb):
            q, c0 = divmod(P * jb, 2 * P)
            nc.scalar.copy(
                h_bf[q][:, c0 : c0 + P, :].rearrange("p (c e) t -> p c t e", e=2), h_banks[jb][:].rearrange("p t (c e) -> p c t e", e=2)
            )

        def quantize_h(j0, j1):
            jh, c0 = divmod(j0, BANK)
            nc.vector.quantize_mx(
                out=h_codes[jh][:, c0 : c0 + j1 - j0].bitcast(FP8X4),
                scales=h_plane[:, j0:j1],
                in_=h_bf[j0 // (2 * P)][:].rearrange("p j t -> p (j t)"),
            )

        up_codes = {}
        up_plane = keep.tile([P, M], U8, name="up_plane", align_bytes=256)

        def quantize_up(n0, rounded, codes):
            width = rounded.shape[1]
            nc.vector.quantize_mx(
                out=codes[:].bitcast(FP8X4),
                scales=up_plane[:, n0 : n0 + width],
                in_=rounded.rearrange("p n i -> p (n i)"),
            )
            for c in range(0, width, P):
                up_codes[(n0 + c) // P] = codes[:, c : c + P]

        def finish(i):
            n, j0, width = pieces[i]
            jh, h0 = divmod(j0, BANK)
            acc = y_banks[i]
            js = slice(j0, j0 + width)
            ns = slice(P * n, P * n + P)
            nc.tensor.matmul_mx(
                out=acc[:],
                lhsT=up_codes[n].bitcast(FP8X4),
                lhsT_scale=up_plane[:, ns],
                rhs=h_codes[jh][:, h0 : h0 + width].bitcast(FP8X4),
                rhs_scale=h_plane[:, js],
                start=False,
                stop=True,
            )
            scaled = keep.tile([P, BANK], F32, name=f"scaled{i}", tag=f"scaled{i}", align_bytes=256)
            result = keep.tile([P, BANK], F32, name=f"result{i}")
            step = BANK // 2 if i >= TILES - 2 else BANK
            for c0 in range(0, width, step):
                cs = slice(c0, c0 + step)
                out_cols = slice(j0 + c0, j0 + c0 + step)
                nc.vector.tensor_tensor(scaled[:, cs], acc[:, cs], got_ts[jh][:, h0 + c0 : h0 + c0 + step], MULT)
                nc.scalar.activation(result[:, cs], scaled[:, cs], SILU, bias=b_cols[:, n : n + 1])
                nc.sync.dma_start(out[ns, out_cols], result[:, cs])

        gather_ts(0, "tab_planes")
        cast_down(0, 0, 0, P, nc.scalar.copy)
        cast_down(0, 1, 0, P // 2, nc.scalar.copy)
        cast_down(0, 1, P // 2, P, nc.vector.tensor_copy)
        b_cols = keep.tile([P, M // P], F32, name="b_cols")
        nc.scalar.copy(b_cols[:], b_turned[:, 0, 0 : M // P])
        quantize_down(0, 0)
        quantize_down(0, 1)
        gather_words(0, [0, P, 3 * P, S], after_down[0], 0)
        for jb in range(S // P):
            h_passes(jb, 0, 0, PACK)
        cast_down(1, 0, 0, P, nc.scalar.copy)
        cast_down(1, 1, 0, P, nc.vector.tensor_copy)
        quantize_down(1, 0)
        quantize_down(1, 1)
        gather_words(1, [0, P, 3 * P, 5 * P, S], after_down[0], 6144)
        for jb in range(S // P):
            h_passes(jb, 1, 0, PACK)
            empty_h(jb)
            if jb in (3, 5):
                started = len(y_banks)
                w4_pass(started, 0)
                w4_pass(started, 1)

        up_bf0 = after_down[0].tile([P, UP_FIRST, PACK], BF16, name="up_bf0", offset=4096, align_bytes=256)
        nc.vector.tensor_copy(up_bf0[:].rearrange("p (c e) i -> p c i e", e=4), up_raw[0][:].rearrange("p i (c e) -> p c i e", e=4))
        h_codes.append(keep.tile([P, BANK], U32, name="h_codes0", tag="up_raw0", align_bytes=256))
        quantize_h(0, BANK // 2)
        quantize_up(0, up_bf0[:], keep.tile([P, UP_FIRST], U32, name="up_codes0", align_bytes=256))
        quantize_h(BANK // 2, BANK)
        got_ts.append(after_h0.tile([P, BANK], F32, name="got_ts1", offset=2048, align_bytes=256))
        nc.vector.tensor_copy(got_ts[1][:], ts_all[:].indirect(offsets[:, BANK // 16 : S // 16]))
        h_codes.append(keep.tile([P, BANK], U32, name="h_codes1", align_bytes=256))
        quantize_h(BANK, BANK + BANK // 2)
        up_bf1 = after_h0.tile([P, UP_FIRST, PACK], BF16, name="up_bf1", offset=4096, align_bytes=256)
        nc.scalar.copy(up_bf1[:].rearrange("p (c e) i -> p c i e", e=4), up_raw[1][:].rearrange("p i (c e) -> p c i e", e=4))

        def cast_up_late(q):
            rounded = after_h0.tile([P, UP_FIRST, PACK], BF16, name=f"up_bf{q}", offset=4096, align_bytes=256)
            for c0 in range(0, UP_FIRST, P):
                cols = slice(UP_FIRST * (q - 2) + c0, UP_FIRST * (q - 2) + c0 + P)
                nc.gpsimd.tensor_scalar(rounded[:, c0 : c0 + P, :], up_raw[2][:, :, cols].rearrange("p i n -> p n i"), 1.0, 0.0, MULT, ADD)
            return rounded

        for i in range(len(pieces)):
            last = LEAD if i < 2 else max(5, i + min(LEAD, (TILES - i) // 6))
            while len(y_banks) <= last:
                started = len(y_banks)
                w4_pass(started, 0)
                w4_pass(started, 1)
            finish(i)
            if i == 0:
                quantize_h(BANK + BANK // 2, S)
            if i == 1:
                quantize_up(UP_FIRST, up_bf1[:], keep.tile([P, UP_FIRST], U32, name="up_codes1", align_bytes=256))
                late = cast_up_late(2)
            if i == 4:
                quantize_up(UP_HALF, late[:], keep.tile([P, UP_FIRST], U32, name="up_codes2", tag="scaled2", align_bytes=256))
                late = cast_up_late(3)
            if i == 9:
                quantize_up(UP_HALF + UP_FIRST, late[:], keep.tile([P, UP_FIRST], U32, name="up_codes3", tag="scaled7", align_bytes=256))
